import numpy as np
import ml_dtypes


def mxq(x, axis, fmt="e4m3"):
    dtype, down = {"e4m3": (ml_dtypes.float8_e4m3fn, 7), "e5m2": (ml_dtypes.float8_e5m2, 14)}[fmt]
    v = np.moveaxis(np.asarray(x, np.float32).astype(ml_dtypes.bfloat16).astype(np.float64), axis, -1)
    blocks = v.reshape(v.shape[:-1] + (-1, 32))
    amax = np.abs(blocks).max(-1, keepdims=True)
    byte = np.maximum(np.where(amax > 0, np.frexp(amax)[1] - 1 + 127, 0) - down, 1)
    scale = np.exp2(byte - 127.0)
    codes = (blocks / scale).astype(np.float32).astype(dtype).astype(np.float64)
    return np.moveaxis((codes * scale).reshape(v.shape), -1, axis)


WIDE = False


def mx_kscale(k):
    if not WIDE:
        return np.ones(k)
    levels = np.array([18, -18])
    if k % 512:
        return np.exp2(np.random.permutation(np.resize(levels, k // 32))).repeat(32)
    a = np.empty((k // 512, 16))
    for p in range(k // 512):
        a[p, :8] = np.random.permutation(np.resize(levels, 8))
        for g in range(8):
            far = levels[np.abs(levels - a[p, g]) >= 10]
            a[p, g + 8] = far[np.random.randint(len(far))]
    return np.exp2(a.ravel()).repeat(32)


def f64(x):
    return np.asarray(x).astype(np.float64)


def striped(idx):
    return np.tile(np.asarray(idx).reshape(-1, 16).T, (8, 1)).astype(np.uint16)


def unstriped(offs):
    return offs[:16].T.reshape(-1).astype(np.int64)


B, N, T, D, R, TU = 1, 512, 2048, 512, 512, 2048


def setup_inputs():
    n = np.random.standard_normal
    idx = np.random.permutation(T)[:B * N]
    uidx = np.random.permutation(TU)[:B * R]
    s = mx_kscale(D)[:, None]
    z = np.ones(TU)
    z[uidx] = mx_kscale(B * R)
    u = np.ones(T)
    u[idx] = mx_kscale(B * N)
    r = np.random.uniform(0.5, 2.0, T) * u
    ur = np.random.uniform(0.5, 2.0, TU) * z
    return {
        "uT": (n((D, TU)) * s / ur).astype(np.float32),
        "vT": (n((D, T)) * (1.00 / np.sqrt(D)) / s / r).astype(np.float32),
        "us": ur[uidx].reshape(B, R, 1).astype(np.float32),
        "ts": np.tile(r, (128, 1)).astype(np.float32),
        "offs": striped(idx),
        "uoffs": striped(uidx),
    }


def reference(uT, vT, us, ts, offs, uoffs):
    idx = unstriped(offs)
    pick = lambda x: x[:, idx].reshape(x.shape[0], B, N).transpose(1, 0, 2)
    uidx = unstriped(uoffs)
    w = pick(f64(vT))
    x = f64(uT)[:, uidx].reshape(D, B, R).transpose(1, 0, 2)
    a = mxq(x, 1, "e4m3").transpose(0, 2, 1) @ mxq(w, 1, "e4m3")
    sc = f64(us) * pick(f64(ts))[:, :1, :]
    a = a * sc
    t = a[:, :, :N // 2] - a[:, :, N // 2:]
    q = 1.0 / (1.0 + np.exp(t))
    g = np.concatenate([-q, q], -1)
    h = sc * g
    dv = mxq(x, 2, "e4m3") @ mxq(h, 1, "e5m2")
    gv = np.zeros((D, T))
    gv[:, idx] = dv.transpose(1, 0, 2).reshape(D, B * N)
    du = mxq(w, 2, "e4m3") @ mxq(h, 2, "e5m2").transpose(0, 2, 1)
    gu = np.zeros((D, TU))
    gu[:, uidx] = du.transpose(1, 0, 2).reshape(D, B * R)
    return gv, gu

@@ -1,0 +1,217 @@
+from contextlib import ExitStack
+
+import concourse.mybir as mybir
+from concourse.masks import make_identity
+
+D, T, N = 512, 2048, 512
+FLOPS = 3 * 2 * D * N * N
+
+F32 = mybir.dt.float32
+BF16 = mybir.dt.bfloat16
+I32 = mybir.dt.int32
+U32 = mybir.dt.uint32
+U16 = mybir.dt.uint16
+U8 = mybir.dt.uint8
+E4M3 = mybir.dt.float8_e4m3fn_x4
+E5M2 = mybir.dt.float8_e5m2_x4
+MULT = mybir.AluOpType.mult
+ADD = mybir.AluOpType.add
+COPY = mybir.ActivationFunctionType.Copy
+SIGMOID = mybir.ActivationFunctionType.Sigmoid
+
+P = 128
+PACK = 4
+HALF = N // 2
+COLS = N // 16
+
+
+def tile_attend_gmf_bpr_vu_kernel(tc, uT, vT, us, ts, offs, uoffs, out_0, out_1):
+    nc = tc.nc
+    with ExitStack() as ctx:
+        keep = ctx.enter_context(tc.tile_pool(name="keep", bufs=1))
+        psum = ctx.enter_context(tc.psum_pool(name="psum", bufs=8))
+
+        def sbuf(name, shape, dtype):
+            return keep.tile(shape, dtype, name=name, align_bytes=64)
+
+        def bank(dtype):
+            return psum.tile([P, PACK, P], dtype, name="bank")
+
+        def planes(dram):
+            return dram.rearrange("(p t) n -> p t n", t=PACK)
+
+        def quantise(codes, scales, values, fmt):
+            nc.vector.quantize_mx(out=codes.bitcast(fmt), scales=scales, in_=values.rearrange("p c t -> p (c t)"))
+
+        user_list = keep.tile([P, COLS], U16, name="user_list")
+        item_list = keep.tile([P, COLS], U16, name="item_list")
+        u_plane = [sbuf("u_plane%d" % t, [P, T], F32) for t in range(PACK)]
+        v_plane = [sbuf("v_plane%d" % t, [P, T], F32) for t in range(PACK)]
+        nc.sync.dma_start(u_plane[0][:], planes(uT)[:, 0, :])
+        nc.sync.dma_start(user_list[:], uoffs)
+        nc.sync.dma_start(item_list[:], offs)
+        ts_row = sbuf("ts_row", [P, T], F32)
+        row_scale = sbuf("row_scale", [P, PACK], F32)
+        nc.sync.dma_start(ts_row[P - 1 : P, :], ts[0:1, :])
+        nc.sync.dma_start(row_scale[:], us.rearrange("b (p t) o -> p (b t o)", t=PACK))
+        nc.gpsimd.memset(ts_row[0 : P - 1, :].bitcast(I32), 0)
+        for t in range(1, PACK):
+            nc.sync.dma_start(u_plane[t][:], planes(uT)[:, t, :])
+        for t in range(PACK):
+            nc.sync.dma_start(v_plane[t][:], planes(vT)[:, t, :])
+
+        warm = sbuf("warm", [P, 8], F32)
+        nc.gpsimd.memset(warm[:], 0.0)
+        nc.scalar.activation(warm[:], warm[:], SIGMOID)
+
+        ident_f32 = sbuf("ident_f32", [P, P], F32)
+        make_identity(nc, ident_f32[:])
+        ident_bf16 = sbuf("ident_bf16", [P, P], BF16)
+        make_identity(nc, ident_bf16[:])
+
+        def turn_block(dst, c, source, dtype=BF16):
+            turned = bank(dtype)
+            for k in range(PACK):
+                nc.tensor.transpose(turned[:, k, :], source(k), (ident_bf16 if dtype == BF16 else ident_f32)[:])
+            nc.scalar.copy(dst[:, c * P : (c + 1) * P, :], turned[:].rearrange("p k m -> p m k"))
+
+        ts_listed = sbuf("ts_listed", [P, N], F32)
+        nc.vector.tensor_copy(ts_listed[:], ts_row[:].indirect(item_list[:]))
+        ts_turned = bank(F32)
+        for c in range(PACK):
+            nc.tensor.transpose(ts_turned[:, c, :], ts_listed[:, c * P : (c + 1) * P], ident_f32[:])
+        ts_column = sbuf("ts_column", [P, PACK], F32)
+        nc.scalar.copy(ts_column[:], ts_turned[:, :, P - 1])
+        ts_spread = bank(F32)
+        for c in range(PACK):
+            nc.tensor.transpose(ts_spread[:, c, :], ts_column[:, c : c + 1].to_broadcast([P, P]), ident_f32[:])
+        neg_row_scale = sbuf("neg_row_scale", [P, PACK], F32)
+        nc.scalar.activation(neg_row_scale[:], row_scale[:], COPY, scale=-1.0)
+        signed_by_row = sbuf("signed_by_row", [P, PACK, N], F32)
+        ts_flat = ts_spread[:].rearrange("p c m -> p (c m)")
+        for s in range(PACK):
+            nc.scalar.activation(signed_by_row[:, s, :HALF], ts_flat[:, :HALF], COPY, scale=neg_row_scale[:, s : s + 1])
+            nc.scalar.activation(signed_by_row[:, s, HALF:], ts_flat[:, HALF:], COPY, scale=row_scale[:, s : s + 1])
+        signed = sbuf("signed", [P, N, PACK], F32)
+        nc.scalar.copy(signed[:], signed_by_row[:].rearrange("p s i -> p i s"))
+
+        x_f32 = sbuf("x_f32", [P, PACK, N], F32)
+        x_r = sbuf("x_r", [P, D, PACK], BF16)
+        x_by_place = x_f32[:].rearrange("p t (m s) -> p t s m", s=PACK)
+        for t in range(PACK):
+            nc.vector.tensor_copy(x_f32[:, t, :], u_plane[t][:].indirect(user_list[:]))
+            turn_block(x_r, t, lambda s: x_by_place[:, t, s, :], F32)
+        x_d = sbuf("x_d", [P, N, PACK], BF16)
+        nc.scalar.copy(
+            x_d[:].rearrange("p (s m) t -> p m s t", s=PACK),
+            x_f32[:].rearrange("p t (m s) -> p m s t", s=PACK),
+        )
+        x_d_codes = sbuf("x_d_codes", [P, N], U32)
+        x_d_scales = sbuf("x_d_scales", [P, N], U8)
+        quantise(x_d_codes[:], x_d_scales[:], x_d[:], E4M3)
+        x_r_codes = sbuf("x_r_codes", [P, D], U32)
+        x_r_scales = sbuf("x_r_scales", [P, D], U8)
+        quantise(x_r_codes[:], x_r_scales[:], x_r[:], E4M3)
+
+        w_d = sbuf("w_d", [P, N, PACK], BF16)
+        w_i = sbuf("w_i", [P, D, PACK], BF16)
+        w_d_codes = sbuf("w_d_codes", [P, N], U32)
+        w_d_scales = sbuf("w_d_scales", [P, N], U8)
+
+        def turn_items(t):
+            turn_block(w_i, t, lambda s: w_d[:].rearrange("p (m s) t -> p s t m", s=PACK)[:, s, t, :])
+
+        for t in range(PACK - 1):
+            nc.vector.tensor_copy(w_d[:, :, t], v_plane[t][:].indirect(item_list[:]))
+            turn_items(t)
+        for half in range(2):
+            slots = slice(half * HALF, (half + 1) * HALF)
+            entries = item_list[:, half * COLS // 2 : (half + 1) * COLS // 2]
+            nc.vector.tensor_copy(w_d[:, slots, PACK - 1], v_plane[PACK - 1][:].indirect(entries))
+            quantise(w_d_codes[:, slots], w_d_scales[:, slots], w_d[:, slots, :], E4M3)
+
+        scaled = sbuf("scaled", [P, N, PACK], F32)
+        margin = sbuf("margin", [P, HALF, PACK], F32)
+        q = sbuf("q", [P, HALF, PACK], F32)
+        h_r = sbuf("h_r", [P, N, PACK], BF16)
+        for c in range(PACK):
+            slots = slice(c * P, (c + 1) * P)
+            scores = bank(F32)
+            for s in range(PACK):
+                rows = slice(s * P, (s + 1) * P)
+                nc.tensor.matmul_mx(
+                    out=scores[:, s, :],
+                    lhsT=x_d_codes[:, rows].bitcast(E4M3),
+                    lhsT_scale=x_d_scales[:, rows],
+                    rhs=w_d_codes[:, slots].bitcast(E4M3),
+                    rhs_scale=w_d_scales[:, slots],
+                    start=True,
+                    stop=True,
+                )
+            nc.vector.tensor_tensor(scaled[:, slots, :], scores[:].rearrange("p s i -> p i s"), signed[:, slots, :], MULT)
+            if c >= 2:
+                pairs = slice((c - 2) * P, (c - 1) * P)
+                nc.vector.tensor_tensor(margin[:, pairs, :], scaled[:, pairs, :], scaled[:, slots, :], ADD)
+                nc.scalar.activation(q[:, pairs, :], margin[:, pairs, :], SIGMOID)
+        for j in range(2):
+            pairs = slice(j * P, (j + 1) * P)
+            for half in range(2):
+                slots = slice(half * HALF + j * P, half * HALF + (j + 1) * P)
+                nc.vector.tensor_tensor(h_r[:, slots, :], q[:, pairs, :], signed[:, slots, :], MULT)
+        h_r_codes = sbuf("h_r_codes", [P, N], U32)
+        h_r_scales = sbuf("h_r_scales", [P, N], U8)
+        quantise(h_r_codes[:], h_r_scales[:], h_r[:], E5M2)
+
+        dv_window = [sbuf("dv_window%d" % k, [P, T], F32) for k in range(2)]
+        du_window = [sbuf("du_window%d" % k, [P, T], F32) for k in range(2)]
+        dv = [sbuf("dv%d" % t, [P, N], F32) for t in range(PACK)]
+        du = [sbuf("du%d" % t, [P, N], F32) for t in range(PACK)]
+
+        def product(t, codes, scales, h_codes, h_scales):
+            features = slice(t * P, (t + 1) * P)
+            sums = bank(F32)
+            nc.tensor.matmul_mx(
+                out=sums[:].rearrange("p s m -> p (s m)"),
+                lhsT=codes[:, features].bitcast(E4M3),
+                lhsT_scale=scales[:, features],
+                rhs=h_codes[:].bitcast(E5M2),
+                rhs_scale=h_scales[:],
+                start=True,
+                stop=True,
+            )
+            return sums
+
+        def place(t, values, windows, entries, out):
+            window = windows[t % len(windows)]
+            nc.vector.tensor_copy(window[:].indirect(entries[:]), values[:])
+            nc.sync.dma_start(planes(out)[:, t, :], window[:])
+
+        for window in dv_window + du_window:
+            nc.vector.memset(window[:].bitcast(I32), 0)
+
+        for t in range(PACK):
+            sums = product(t, x_r_codes, x_r_scales, h_r_codes, h_r_scales)
+            nc.scalar.copy(dv[t][:], sums[:].rearrange("p s m -> p (s m)"))
+        place(0, dv[0], dv_window, item_list, out_0)
+
+        turn_items(PACK - 1)
+        w_i_codes = sbuf("w_i_codes", [P, D], U32)
+        w_i_scales = sbuf("w_i_scales", [P, D], U8)
+        quantise(w_i_codes[:], w_i_scales[:], w_i[:], E4M3)
+        h_i = sbuf("h_i", [P, N, PACK], BF16)
+        for s in range(PACK):
+            turn_block(h_i, s, lambda k: h_r[:].rearrange("p (m k) s -> p k s m", k=PACK)[:, k, s, :])
+        place(1, dv[1], dv_window, item_list, out_0)
+        h_i_codes = sbuf("h_i_codes", [P, N], U32)
+        h_i_scales = sbuf("h_i_scales", [P, N], U8)
+        quantise(h_i_codes[:], h_i_scales[:], h_i[:], E5M2)
+        for t in range(PACK):
+            sums = product(t, w_i_codes, w_i_scales, h_i_codes, h_i_scales)
+            nc.scalar.copy(du[t][:].rearrange("p (m s) -> p m s", s=PACK), sums[:].rearrange("p s m -> p m s"))
+
+        place(0, du[0], du_window, user_list, out_1)
+        place(1, du[1], du_window, user_list, out_1)
+        place(2, dv[2], dv_window, item_list, out_0)
+        place(3, dv[3], dv_window, item_list, out_0)
+        place(2, du[2], du_window, user_list, out_1)
+        place(3, du[3], du_window, user_list, out_1)

@@ -29,13 +29,13 @@ def tile_attend_gmf_bpr_vu_kernel(tc, uT, vT, us, ts, offs, uoffs, out_0, out_1)
     nc = tc.nc
     with ExitStack() as ctx:
         keep = ctx.enter_context(tc.tile_pool(name="keep", bufs=1))
-        psum = ctx.enter_context(tc.psum_pool(name="psum", bufs=8))
+        psum = ctx.enter_context(tc.psum_pool(name="psum", bufs=1))
 
         def sbuf(name, shape, dtype):
             return keep.tile(shape, dtype, name=name, align_bytes=64)
 
-        def bank(dtype):
-            return psum.tile([P, PACK, P], dtype, name="bank")
+        def bank(number):
+            return psum.tile([P, PACK, P], F32, name="bank%d" % number)
 
         def planes(dram):
             return dram.rearrange("(p t) n -> p t n", t=PACK)
@@ -66,41 +66,39 @@ def tile_attend_gmf_bpr_vu_kernel(tc, uT, vT, us, ts, offs, uoffs, out_0, out_1)
 
         ident_f32 = sbuf("ident_f32", [P, P], F32)
         make_identity(nc, ident_f32[:])
-        ident_bf16 = sbuf("ident_bf16", [P, P], BF16)
-        make_identity(nc, ident_bf16[:])
 
-        def turn_block(dst, c, source, dtype=BF16):
-            turned = bank(dtype)
+        def flat(ap):
+            return ap.rearrange("p a b -> p (a b)")
+
+        def turn_pairs(dst, src, u, number):
+            words = flat(src[:]).bitcast(F32).rearrange("p (k m u) -> p u k m", k=PACK, u=2)
+            turned = bank(number)
             for k in range(PACK):
-                nc.tensor.transpose(turned[:, k, :], source(k), (ident_bf16 if dtype == BF16 else ident_f32)[:])
-            nc.scalar.copy(dst[:, c * P : (c + 1) * P, :], turned[:].rearrange("p k m -> p m k"))
+                nc.tensor.transpose(turned[:, k, :], words[:, u, k, :], ident_f32[:])
+            nc.scalar.copy(
+                dst[:, u * HALF : (u + 1) * HALF, :].rearrange("p (e c) k -> p e c k", e=2),
+                flat(turned[:]).bitcast(BF16).rearrange("p (k c e) -> p e c k", k=PACK, e=2),
+            )
 
-        ts_listed = sbuf("ts_listed", [P, N], F32)
-        nc.vector.tensor_copy(ts_listed[:], ts_row[:].indirect(item_list[:]))
-        ts_turned = bank(F32)
-        for c in range(PACK):
-            nc.tensor.transpose(ts_turned[:, c, :], ts_listed[:, c * P : (c + 1) * P], ident_f32[:])
-        ts_column = sbuf("ts_column", [P, PACK], F32)
-        nc.scalar.copy(ts_column[:], ts_turned[:, :, P - 1])
-        ts_spread = bank(F32)
-        for c in range(PACK):
-            nc.tensor.transpose(ts_spread[:, c, :], ts_column[:, c : c + 1].to_broadcast([P, P]), ident_f32[:])
-        neg_row_scale = sbuf("neg_row_scale", [P, PACK], F32)
-        nc.scalar.activation(neg_row_scale[:], row_scale[:], COPY, scale=-1.0)
-        signed_by_row = sbuf("signed_by_row", [P, PACK, N], F32)
-        ts_flat = ts_spread[:].rearrange("p c m -> p (c m)")
-        for s in range(PACK):
-            nc.scalar.activation(signed_by_row[:, s, :HALF], ts_flat[:, :HALF], COPY, scale=neg_row_scale[:, s : s + 1])
-            nc.scalar.activation(signed_by_row[:, s, HALF:], ts_flat[:, HALF:], COPY, scale=row_scale[:, s : s + 1])
-        signed = sbuf("signed", [P, N, PACK], F32)
-        nc.scalar.copy(signed[:], signed_by_row[:].rearrange("p s i -> p i s"))
+        dv_window = [sbuf("dv_window%d" % k, [P, T], F32) for k in range(3)]
+        du_window = [sbuf("du_window%d" % k, [P, T], F32) for k in range(2)]
+        for window in dv_window[:2]:
+            nc.vector.memset(window[:].bitcast(I32), 0)
+        sign = sbuf("sign", [P, 1], F32)
+        nc.gpsimd.memset(sign[: P // 2, :], -1.0)
+        nc.gpsimd.memset(sign[P // 2 :, :], 1.0)
+        for window in dv_window[2:] + du_window:
+            nc.gpsimd.memset(window[:].bitcast(I32), 0)
 
         x_f32 = sbuf("x_f32", [P, PACK, N], F32)
         x_r = sbuf("x_r", [P, D, PACK], BF16)
         x_by_place = x_f32[:].rearrange("p t (m s) -> p t s m", s=PACK)
         for t in range(PACK):
             nc.vector.tensor_copy(x_f32[:, t, :], u_plane[t][:].indirect(user_list[:]))
-            turn_block(x_r, t, lambda s: x_by_place[:, t, s, :], F32)
+            turned = bank(PACK + t)
+            for s in range(PACK):
+                nc.tensor.transpose(turned[:, s, :], x_by_place[:, t, s, :], ident_f32[:])
+            nc.scalar.copy(x_r[:, t * P : (t + 1) * P, :], turned[:].rearrange("p s c -> p c s"))
         x_d = sbuf("x_d", [P, N, PACK], BF16)
         nc.scalar.copy(
             x_d[:].rearrange("p (s m) t -> p m s t", s=PACK),
@@ -113,105 +111,123 @@ def tile_attend_gmf_bpr_vu_kernel(tc, uT, vT, us, ts, offs, uoffs, out_0, out_1)
         x_r_scales = sbuf("x_r_scales", [P, D], U8)
         quantise(x_r_codes[:], x_r_scales[:], x_r[:], E4M3)
 
+        ts_listed = sbuf("ts_listed", [P, N], F32)
+        nc.vector.tensor_copy(ts_listed[:], ts_row[:].indirect(item_list[:]))
+        ts_turned = bank(0)
+        for k in range(PACK):
+            nc.tensor.transpose(ts_turned[:, k, :], ts_listed[:].rearrange("p (m k) -> p k m", k=PACK)[:, k, :], ident_f32[:])
+        ts_column = sbuf("ts_column", [P, PACK], F32)
+        nc.scalar.activation(ts_column[:], ts_turned[:, :, P - 1], COPY, scale=sign[:])
+        ts_spread = bank(1)
+        for k in range(PACK):
+            nc.tensor.transpose(ts_spread[:, k, :], ts_column[:, k : k + 1].to_broadcast([P, P]), ident_f32[:])
+        signed_by_row = sbuf("signed_by_row", [P, PACK, N], F32)
+        for s in range(PACK):
+            nc.scalar.activation(signed_by_row[:, s, :], flat(ts_spread[:]), COPY, scale=row_scale[:, s : s + 1])
+        signed = sbuf("signed", [P, N, PACK], F32)
+        nc.scalar.copy(signed[:], signed_by_row[:].rearrange("p s i -> p i s"))
+
         w_d = sbuf("w_d", [P, N, PACK], BF16)
         w_i = sbuf("w_i", [P, D, PACK], BF16)
         w_d_codes = sbuf("w_d_codes", [P, N], U32)
         w_d_scales = sbuf("w_d_scales", [P, N], U8)
-
-        def turn_items(t):
-            turn_block(w_i, t, lambda s: w_d[:].rearrange("p (m s) t -> p s t m", s=PACK)[:, s, t, :])
-
-        for t in range(PACK - 1):
-            nc.vector.tensor_copy(w_d[:, :, t], v_plane[t][:].indirect(item_list[:]))
-            turn_items(t)
-        for half in range(2):
-            slots = slice(half * HALF, (half + 1) * HALF)
-            entries = item_list[:, half * COLS // 2 : (half + 1) * COLS // 2]
-            nc.vector.tensor_copy(w_d[:, slots, PACK - 1], v_plane[PACK - 1][:].indirect(entries))
-            quantise(w_d_codes[:, slots], w_d_scales[:, slots], w_d[:, slots, :], E4M3)
+        w_by_slot = w_d[:].rearrange("p (k m) t -> p t m k", k=PACK)
+        for t in range(PACK):
+            nc.vector.tensor_copy(w_by_slot[:, t, :, :], v_plane[t][:].indirect(item_list[:]))
+            if t == 1:
+                turn_pairs(w_i, w_d, 0, 2)
 
         scaled = sbuf("scaled", [P, N, PACK], F32)
-        margin = sbuf("margin", [P, HALF, PACK], F32)
-        q = sbuf("q", [P, HALF, PACK], F32)
+        margin = sbuf("margin", [P, PACK, HALF], F32)
+        q = sbuf("q", [P, PACK, HALF], F32)
         h_r = sbuf("h_r", [P, N, PACK], BF16)
-        for c in range(PACK):
-            slots = slice(c * P, (c + 1) * P)
-            scores = bank(F32)
+        h_r_codes = sbuf("h_r_codes", [P, N], U32)
+        h_r_scales = sbuf("h_r_scales", [P, N], U8)
+        scores = [bank(PACK + k) for k in range(PACK)]
+
+        def block(k):
+            return slice(k * P, (k + 1) * P)
+
+        def by_half(tile, k):
+            return tile[:, block(k), :].rearrange("p (a m) s -> p a (m s)", a=2)
+
+        def score(k):
+            quantise(w_d_codes[:, block(k)], w_d_scales[:, block(k)], w_d[:, block(k), :], E4M3)
             for s in range(PACK):
-                rows = slice(s * P, (s + 1) * P)
                 nc.tensor.matmul_mx(
-                    out=scores[:, s, :],
-                    lhsT=x_d_codes[:, rows].bitcast(E4M3),
-                    lhsT_scale=x_d_scales[:, rows],
-                    rhs=w_d_codes[:, slots].bitcast(E4M3),
-                    rhs_scale=w_d_scales[:, slots],
+                    out=scores[k][:, s, :],
+                    lhsT=x_d_codes[:, block(s)].bitcast(E4M3),
+                    lhsT_scale=x_d_scales[:, block(s)],
+                    rhs=w_d_codes[:, block(k)].bitcast(E4M3),
+                    rhs_scale=w_d_scales[:, block(k)],
                     start=True,
                     stop=True,
                 )
-            nc.vector.tensor_tensor(scaled[:, slots, :], scores[:].rearrange("p s i -> p i s"), signed[:, slots, :], MULT)
-            if c >= 2:
-                pairs = slice((c - 2) * P, (c - 1) * P)
-                nc.vector.tensor_tensor(margin[:, pairs, :], scaled[:, pairs, :], scaled[:, slots, :], ADD)
-                nc.scalar.activation(q[:, pairs, :], margin[:, pairs, :], SIGMOID)
-        for j in range(2):
-            pairs = slice(j * P, (j + 1) * P)
-            for half in range(2):
-                slots = slice(half * HALF + j * P, half * HALF + (j + 1) * P)
-                nc.vector.tensor_tensor(h_r[:, slots, :], q[:, pairs, :], signed[:, slots, :], MULT)
-        h_r_codes = sbuf("h_r_codes", [P, N], U32)
-        h_r_scales = sbuf("h_r_scales", [P, N], U8)
-        quantise(h_r_codes[:], h_r_scales[:], h_r[:], E5M2)
 
-        dv_window = [sbuf("dv_window%d" % k, [P, T], F32) for k in range(2)]
-        du_window = [sbuf("du_window%d" % k, [P, T], F32) for k in range(2)]
+        def scale(k):
+            nc.vector.tensor_tensor(scaled[:, block(k), :], scores[k][:].rearrange("p s m -> p m s"), signed[:, block(k), :], MULT)
+
+        def weigh(k):
+            nc.vector.tensor_tensor(margin[:, k, :], by_half(scaled, k)[:, 0, :], by_half(scaled, k)[:, 1, :], ADD)
+            nc.scalar.activation(q[:, k, :], margin[:, k, :], SIGMOID)
+
+        def gradient(k):
+            nc.vector.tensor_tensor(by_half(h_r, k), q[:, k : k + 1, :].to_broadcast([P, 2, HALF]), by_half(signed, k), MULT)
+
+        def quantise_h(k):
+            quantise(h_r_codes[:, block(k)], h_r_scales[:, block(k)], h_r[:, block(k), :], E5M2)
+
+        for k in range(PACK):
+            score(k)
+        stages = [scale, weigh, gradient, quantise_h]
+        for step in range(PACK + len(stages) - 1):
+            for lag, stage in enumerate(stages):
+                if 0 <= step - lag < PACK:
+                    stage(step - lag)
+
         dv = [sbuf("dv%d" % t, [P, N], F32) for t in range(PACK)]
         du = [sbuf("du%d" % t, [P, N], F32) for t in range(PACK)]
 
-        def product(t, codes, scales, h_codes, h_scales):
-            features = slice(t * P, (t + 1) * P)
-            sums = bank(F32)
+        def product(t, dst, number, codes, scales, h_codes, h_scales):
+            sums = bank(number)
             nc.tensor.matmul_mx(
-                out=sums[:].rearrange("p s m -> p (s m)"),
-                lhsT=codes[:, features].bitcast(E4M3),
-                lhsT_scale=scales[:, features],
+                out=flat(sums[:]),
+                lhsT=codes[:, block(t)].bitcast(E4M3),
+                lhsT_scale=scales[:, block(t)],
                 rhs=h_codes[:].bitcast(E5M2),
                 rhs_scale=h_scales[:],
                 start=True,
                 stop=True,
             )
-            return sums
+            nc.scalar.copy(dst[:].rearrange("p (m s) -> p m s", s=PACK), sums[:].rearrange("p s m -> p m s"))
 
         def place(t, values, windows, entries, out):
             window = windows[t % len(windows)]
             nc.vector.tensor_copy(window[:].indirect(entries[:]), values[:])
             nc.sync.dma_start(planes(out)[:, t, :], window[:])
 
-        for window in dv_window + du_window:
-            nc.vector.memset(window[:].bitcast(I32), 0)
-
-        for t in range(PACK):
-            sums = product(t, x_r_codes, x_r_scales, h_r_codes, h_r_scales)
-            nc.scalar.copy(dv[t][:], sums[:].rearrange("p s m -> p (s m)"))
-        place(0, dv[0], dv_window, item_list, out_0)
-
-        turn_items(PACK - 1)
         w_i_codes = sbuf("w_i_codes", [P, D], U32)
         w_i_scales = sbuf("w_i_scales", [P, D], U8)
-        quantise(w_i_codes[:], w_i_scales[:], w_i[:], E4M3)
         h_i = sbuf("h_i", [P, N, PACK], BF16)
-        for s in range(PACK):
-            turn_block(h_i, s, lambda k: h_r[:].rearrange("p (m k) s -> p k s m", k=PACK)[:, k, s, :])
-        place(1, dv[1], dv_window, item_list, out_0)
         h_i_codes = sbuf("h_i_codes", [P, N], U32)
         h_i_scales = sbuf("h_i_scales", [P, N], U8)
-        quantise(h_i_codes[:], h_i_scales[:], h_i[:], E5M2)
-        for t in range(PACK):
-            sums = product(t, w_i_codes, w_i_scales, h_i_codes, h_i_scales)
-            nc.scalar.copy(du[t][:].rearrange("p (m s) -> p m s", s=PACK), sums[:].rearrange("p s m -> p m s"))
 
+        product(0, dv[0], 0, x_r_codes, x_r_scales, h_r_codes, h_r_scales)
+        place(0, dv[0], dv_window, item_list, out_0)
+        product(1, dv[1], 1, x_r_codes, x_r_scales, h_r_codes, h_r_scales)
+        for u in range(2):
+            turn_pairs(h_i, h_r, u, 2 + u)
+        turn_pairs(w_i, w_d, 1, 0)
+        quantise(h_i_codes[:], h_i_scales[:], h_i[:], E5M2)
+        quantise(w_i_codes[:], w_i_scales[:], w_i[:], E4M3)
+        place(1, dv[1], dv_window, item_list, out_0)
+        for t in range(2, PACK):
+            product(t, dv[t], PACK + t, x_r_codes, x_r_scales, h_r_codes, h_r_scales)
+        for t in range(PACK):
+            product(t, du[t], t, w_i_codes, w_i_scales, h_i_codes, h_i_scales)
+        place(2, dv[2], dv_window, item_list, out_0)
         place(0, du[0], du_window, user_list, out_1)
         place(1, du[1], du_window, user_list, out_1)
-        place(2, dv[2], dv_window, item_list, out_0)
         place(3, dv[3], dv_window, item_list, out_0)
         place(2, du[2], du_window, user_list, out_1)
         place(3, du[3], du_window, user_list, out_1)

@@ -31,8 +31,8 @@ def tile_attend_gmf_bpr_vu_kernel(tc, uT, vT, us, ts, offs, uoffs, out_0, out_1)
         keep = ctx.enter_context(tc.tile_pool(name="keep", bufs=1))
         psum = ctx.enter_context(tc.psum_pool(name="psum", bufs=1))
 
-        def sbuf(name, shape, dtype):
-            return keep.tile(shape, dtype, name=name, align_bytes=64)
+        def sbuf(name, shape, dtype, tag=""):
+            return keep.tile(shape, dtype, name=name, tag=tag or name, align_bytes=64)
 
         def bank(number):
             return psum.tile([P, PACK, P], F32, name="bank%d" % number)
@@ -76,19 +76,35 @@ def tile_attend_gmf_bpr_vu_kernel(tc, uT, vT, us, ts, offs, uoffs, out_0, out_1)
             for k in range(PACK):
                 nc.tensor.transpose(turned[:, k, :], words[:, u, k, :], ident_f32[:])
             nc.scalar.copy(
-                dst[:, u * HALF : (u + 1) * HALF, :].rearrange("p (e c) k -> p e c k", e=2),
+                dst.rearrange("p (e c) k -> p e c k", e=2),
                 flat(turned[:]).bitcast(BF16).rearrange("p (k c e) -> p e c k", k=PACK, e=2),
             )
 
-        dv_window = [sbuf("dv_window%d" % k, [P, T], F32) for k in range(3)]
+        dv_window = [sbuf("dv_window%d" % k, [P, T], F32) for k in range(2)]
         du_window = [sbuf("du_window%d" % k, [P, T], F32) for k in range(2)]
-        for window in dv_window[:2]:
+        for window in dv_window:
             nc.vector.memset(window[:].bitcast(I32), 0)
         sign = sbuf("sign", [P, 1], F32)
         nc.gpsimd.memset(sign[: P // 2, :], -1.0)
         nc.gpsimd.memset(sign[P // 2 :, :], 1.0)
-        for window in dv_window[2:] + du_window:
+        for window in du_window:
             nc.gpsimd.memset(window[:].bitcast(I32), 0)
+
+        ts_listed = sbuf("ts_listed", [P, N], F32)
+        nc.vector.tensor_copy(ts_listed[:], ts_row[:].indirect(item_list[:]))
+        ts_turned = bank(0)
+        for k in range(PACK):
+            nc.tensor.transpose(ts_turned[:, k, :], ts_listed[:].rearrange("p (m k) -> p k m", k=PACK)[:, k, :], ident_f32[:])
+        ts_column = sbuf("ts_column", [P, PACK], F32)
+        nc.scalar.activation(ts_column[:], ts_turned[:, :, P - 1], COPY, scale=sign[:])
+        ts_spread = bank(1)
+        for k in range(PACK):
+            nc.tensor.transpose(ts_spread[:, k, :], ts_column[:, k : k + 1].to_broadcast([P, P]), ident_f32[:])
+        signed_by_row = sbuf("signed_by_row", [P, PACK, N], F32)
+        for s in range(PACK):
+            nc.scalar.activation(signed_by_row[:, s, :], flat(ts_spread[:]), COPY, scale=row_scale[:, s : s + 1])
+        signed = sbuf("signed", [P, N, PACK], F32)
+        nc.scalar.copy(signed[:], signed_by_row[:].rearrange("p s i -> p i s"))
 
         x_f32 = sbuf("x_f32", [P, PACK, N], F32)
         x_r = sbuf("x_r", [P, D, PACK], BF16)
@@ -111,35 +127,22 @@ def tile_attend_gmf_bpr_vu_kernel(tc, uT, vT, us, ts, offs, uoffs, out_0, out_1)
         x_r_scales = sbuf("x_r_scales", [P, D], U8)
         quantise(x_r_codes[:], x_r_scales[:], x_r[:], E4M3)
 
-        ts_listed = sbuf("ts_listed", [P, N], F32)
-        nc.vector.tensor_copy(ts_listed[:], ts_row[:].indirect(item_list[:]))
-        ts_turned = bank(0)
-        for k in range(PACK):
-            nc.tensor.transpose(ts_turned[:, k, :], ts_listed[:].rearrange("p (m k) -> p k m", k=PACK)[:, k, :], ident_f32[:])
-        ts_column = sbuf("ts_column", [P, PACK], F32)
-        nc.scalar.activation(ts_column[:], ts_turned[:, :, P - 1], COPY, scale=sign[:])
-        ts_spread = bank(1)
-        for k in range(PACK):
-            nc.tensor.transpose(ts_spread[:, k, :], ts_column[:, k : k + 1].to_broadcast([P, P]), ident_f32[:])
-        signed_by_row = sbuf("signed_by_row", [P, PACK, N], F32)
-        for s in range(PACK):
-            nc.scalar.activation(signed_by_row[:, s, :], flat(ts_spread[:]), COPY, scale=row_scale[:, s : s + 1])
-        signed = sbuf("signed", [P, N, PACK], F32)
-        nc.scalar.copy(signed[:], signed_by_row[:].rearrange("p s i -> p i s"))
-
         w_d = sbuf("w_d", [P, N, PACK], BF16)
-        w_i = sbuf("w_i", [P, D, PACK], BF16)
+        w_i = [sbuf("w_i%d" % u, [P, HALF, PACK], BF16) for u in range(2)]
+        w_i_scales = [sbuf("w_i_scales%d" % u, [P, HALF], U8) for u in range(2)]
+        w_i_codes = [sbuf("w_i_codes0", [P, HALF], U32)]
         w_d_codes = sbuf("w_d_codes", [P, N], U32)
         w_d_scales = sbuf("w_d_scales", [P, N], U8)
         w_by_slot = w_d[:].rearrange("p (k m) t -> p t m k", k=PACK)
         for t in range(PACK):
             nc.vector.tensor_copy(w_by_slot[:, t, :, :], v_plane[t][:].indirect(item_list[:]))
             if t == 1:
-                turn_pairs(w_i, w_d, 0, 2)
+                turn_pairs(w_i[0][:], w_d, 0, 2)
+                quantise(w_i_codes[0][:], w_i_scales[0][:], w_i[0][:], E4M3)
 
         scaled = sbuf("scaled", [P, N, PACK], F32)
         margin = sbuf("margin", [P, PACK, HALF], F32)
-        q = sbuf("q", [P, PACK, HALF], F32)
+        q = [sbuf("q%d" % k, [P, 1, HALF], F32) for k in range(PACK)]
         h_r = sbuf("h_r", [P, N, PACK], BF16)
         h_r_codes = sbuf("h_r_codes", [P, N], U32)
         h_r_scales = sbuf("h_r_scales", [P, N], U8)
@@ -169,10 +172,10 @@ def tile_attend_gmf_bpr_vu_kernel(tc, uT, vT, us, ts, offs, uoffs, out_0, out_1)
 
         def weigh(k):
             nc.vector.tensor_tensor(margin[:, k, :], by_half(scaled, k)[:, 0, :], by_half(scaled, k)[:, 1, :], ADD)
-            nc.scalar.activation(q[:, k, :], margin[:, k, :], SIGMOID)
+            nc.scalar.activation(q[k][:, 0, :], margin[:, k, :], SIGMOID)
 
         def gradient(k):
-            nc.vector.tensor_tensor(by_half(h_r, k), q[:, k : k + 1, :].to_broadcast([P, 2, HALF]), by_half(signed, k), MULT)
+            nc.vector.tensor_tensor(by_half(h_r, k), q[k][:].to_broadcast([P, 2, HALF]), by_half(signed, k), MULT)
 
         def quantise_h(k):
             quantise(h_r_codes[:, block(k)], h_r_scales[:, block(k)], h_r[:, block(k), :], E5M2)
@@ -188,46 +191,55 @@ def tile_attend_gmf_bpr_vu_kernel(tc, uT, vT, us, ts, offs, uoffs, out_0, out_1)
         dv = [sbuf("dv%d" % t, [P, N], F32) for t in range(PACK)]
         du = [sbuf("du%d" % t, [P, N], F32) for t in range(PACK)]
 
-        def product(t, dst, number, codes, scales, h_codes, h_scales):
+        def product(dst, number, codes, scales, h_codes, h_scales, copy):
             sums = bank(number)
             nc.tensor.matmul_mx(
                 out=flat(sums[:]),
-                lhsT=codes[:, block(t)].bitcast(E4M3),
-                lhsT_scale=scales[:, block(t)],
+                lhsT=codes.bitcast(E4M3),
+                lhsT_scale=scales,
                 rhs=h_codes[:].bitcast(E5M2),
                 rhs_scale=h_scales[:],
                 start=True,
                 stop=True,
             )
-            nc.scalar.copy(dst[:].rearrange("p (m s) -> p m s", s=PACK), sums[:].rearrange("p s m -> p m s"))
+            copy(dst[:].rearrange("p (m s) -> p m s", s=PACK), sums[:].rearrange("p s m -> p m s"))
 
         def place(t, values, windows, entries, out):
             window = windows[t % len(windows)]
             nc.vector.tensor_copy(window[:].indirect(entries[:]), values[:])
             nc.sync.dma_start(planes(out)[:, t, :], window[:])
 
-        w_i_codes = sbuf("w_i_codes", [P, D], U32)
-        w_i_scales = sbuf("w_i_scales", [P, D], U8)
         h_i = sbuf("h_i", [P, N, PACK], BF16)
         h_i_codes = sbuf("h_i_codes", [P, N], U32)
         h_i_scales = sbuf("h_i_scales", [P, N], U8)
 
-        product(0, dv[0], 0, x_r_codes, x_r_scales, h_r_codes, h_r_scales)
+        def item_product(t, number, copy=nc.scalar.copy):
+            product(dv[t], number, x_r_codes[:, block(t)], x_r_scales[:, block(t)], h_r_codes, h_r_scales, copy)
+
+        def user_product(t, number):
+            u, e = divmod(t, 2)
+            product(du[t], number, w_i_codes[u][:, block(e)], w_i_scales[u][:, block(e)], h_i_codes, h_i_scales, nc.scalar.copy)
+
+        turn_pairs(w_i[1][:], w_d, 1, PACK)
+        w_i_codes.append(sbuf("w_i_codes1", [P, HALF], U32, tag="q%d" % (PACK - 1)))
+        quantise(w_i_codes[1][:], w_i_scales[1][:], w_i[1][:], E4M3)
+
+        item_product(0, 0, nc.vector.tensor_copy)
         place(0, dv[0], dv_window, item_list, out_0)
-        product(1, dv[1], 1, x_r_codes, x_r_scales, h_r_codes, h_r_scales)
         for u in range(2):
-            turn_pairs(h_i, h_r, u, 2 + u)
-        turn_pairs(w_i, w_d, 1, 0)
+            turn_pairs(h_i[:, u * HALF : (u + 1) * HALF, :], h_r, u, 1 + u)
         quantise(h_i_codes[:], h_i_scales[:], h_i[:], E5M2)
-        quantise(w_i_codes[:], w_i_scales[:], w_i[:], E4M3)
+        item_product(1, 2)
         place(1, dv[1], dv_window, item_list, out_0)
-        for t in range(2, PACK):
-            product(t, dv[t], PACK + t, x_r_codes, x_r_scales, h_r_codes, h_r_scales)
-        for t in range(PACK):
-            product(t, du[t], t, w_i_codes, w_i_scales, h_i_codes, h_i_scales)
-        place(2, dv[2], dv_window, item_list, out_0)
+        user_product(0, 7)
         place(0, du[0], du_window, user_list, out_1)
+        user_product(1, 3)
         place(1, du[1], du_window, user_list, out_1)
+        item_product(2, 5)
+        place(2, dv[2], dv_window, item_list, out_0)
+        item_product(3, 6)
         place(3, dv[3], dv_window, item_list, out_0)
+        user_product(2, 0)
         place(2, du[2], du_window, user_list, out_1)
+        user_product(3, 1)
         place(3, du[3], du_window, user_list, out_1)

@@ -106,20 +106,13 @@ def tile_attend_gmf_bpr_vu_kernel(tc, uT, vT, us, ts, offs, uoffs, out_0, out_1)
         signed = sbuf("signed", [P, N, PACK], F32)
         nc.scalar.copy(signed[:], signed_by_row[:].rearrange("p s i -> p i s"))
 
-        x_f32 = sbuf("x_f32", [P, PACK, N], F32)
-        x_r = sbuf("x_r", [P, D, PACK], BF16)
-        x_by_place = x_f32[:].rearrange("p t (m s) -> p t s m", s=PACK)
-        for t in range(PACK):
-            nc.vector.tensor_copy(x_f32[:, t, :], u_plane[t][:].indirect(user_list[:]))
-            turned = bank(PACK + t)
-            for s in range(PACK):
-                nc.tensor.transpose(turned[:, s, :], x_by_place[:, t, s, :], ident_f32[:])
-            nc.scalar.copy(x_r[:, t * P : (t + 1) * P, :], turned[:].rearrange("p s c -> p c s"))
         x_d = sbuf("x_d", [P, N, PACK], BF16)
-        nc.scalar.copy(
-            x_d[:].rearrange("p (s m) t -> p m s t", s=PACK),
-            x_f32[:].rearrange("p t (m s) -> p m s t", s=PACK),
-        )
+        x_r = sbuf("x_r", [P, D, PACK], BF16)
+        x_by_slot = x_d[:].rearrange("p (s m) t -> p t m s", s=PACK)
+        for t in range(PACK):
+            nc.vector.tensor_copy(x_by_slot[:, t, :, :], u_plane[t][:].indirect(user_list[:]))
+        for u in range(2):
+            turn_pairs(x_r[:, u * HALF : (u + 1) * HALF, :], x_d, u, 2 + u)
         x_d_codes = sbuf("x_d_codes", [P, N], U32)
         x_d_scales = sbuf("x_d_scales", [P, N], U8)
         quantise(x_d_codes[:], x_d_scales[:], x_d[:], E4M3)
@@ -128,17 +121,13 @@ def tile_attend_gmf_bpr_vu_kernel(tc, uT, vT, us, ts, offs, uoffs, out_0, out_1)
         quantise(x_r_codes[:], x_r_scales[:], x_r[:], E4M3)
 
         w_d = sbuf("w_d", [P, N, PACK], BF16)
-        w_i = [sbuf("w_i%d" % u, [P, HALF, PACK], BF16) for u in range(2)]
-        w_i_scales = [sbuf("w_i_scales%d" % u, [P, HALF], U8) for u in range(2)]
-        w_i_codes = [sbuf("w_i_codes0", [P, HALF], U32)]
+        w_i = sbuf("w_i", [P, D, PACK], BF16)
+        w_i_scales = sbuf("w_i_scales", [P, D], U8)
         w_d_codes = sbuf("w_d_codes", [P, N], U32)
         w_d_scales = sbuf("w_d_scales", [P, N], U8)
         w_by_slot = w_d[:].rearrange("p (k m) t -> p t m k", k=PACK)
         for t in range(PACK):
             nc.vector.tensor_copy(w_by_slot[:, t, :, :], v_plane[t][:].indirect(item_list[:]))
-            if t == 1:
-                turn_pairs(w_i[0][:], w_d, 0, 2)
-                quantise(w_i_codes[0][:], w_i_scales[0][:], w_i[0][:], E4M3)
 
         scaled = sbuf("scaled", [P, N, PACK], F32)
         margin = sbuf("margin", [P, PACK, HALF], F32)
@@ -217,12 +206,12 @@ def tile_attend_gmf_bpr_vu_kernel(tc, uT, vT, us, ts, offs, uoffs, out_0, out_1)
             product(dv[t], number, x_r_codes[:, block(t)], x_r_scales[:, block(t)], h_r_codes, h_r_scales, copy)
 
         def user_product(t, number):
-            u, e = divmod(t, 2)
-            product(du[t], number, w_i_codes[u][:, block(e)], w_i_scales[u][:, block(e)], h_i_codes, h_i_scales, nc.scalar.copy)
+            product(du[t], number, w_i_codes[:, block(t)], w_i_scales[:, block(t)], h_i_codes, h_i_scales, nc.scalar.copy)
 
-        turn_pairs(w_i[1][:], w_d, 1, PACK)
-        w_i_codes.append(sbuf("w_i_codes1", [P, HALF], U32, tag="q%d" % (PACK - 1)))
-        quantise(w_i_codes[1][:], w_i_scales[1][:], w_i[1][:], E4M3)
+        for u in range(2):
+            turn_pairs(w_i[:, u * HALF : (u + 1) * HALF, :], w_d, u, PACK + u)
+        w_i_codes = sbuf("w_i_codes", [P, D], U32, tag="q%d" % (PACK - 1))
+        quantise(w_i_codes[:], w_i_scales[:], w_i[:], E4M3)
 
         item_product(0, 0, nc.vector.tensor_copy)
         place(0, dv[0], dv_window, item_list, out_0)
@@ -235,7 +224,7 @@ def tile_attend_gmf_bpr_vu_kernel(tc, uT, vT, us, ts, offs, uoffs, out_0, out_1)
         place(0, du[0], du_window, user_list, out_1)
         user_product(1, 3)
         place(1, du[1], du_window, user_list, out_1)
-        item_product(2, 5)
+        item_product(2, 4)
         place(2, dv[2], dv_window, item_list, out_0)
         item_product(3, 6)
         place(3, dv[3], dv_window, item_list, out_0)

@@ -106,13 +106,26 @@ def tile_attend_gmf_bpr_vu_kernel(tc, uT, vT, us, ts, offs, uoffs, out_0, out_1)
         signed = sbuf("signed", [P, N, PACK], F32)
         nc.scalar.copy(signed[:], signed_by_row[:].rearrange("p s i -> p i s"))
 
+        def turn_plane(turned_tile, listed, t, number):
+            words = listed[:, t, :].bitcast(F32).rearrange("p (m u) -> p u m", u=2)
+            turned = bank(number)
+            for u in range(2):
+                nc.tensor.transpose(turned[:, u, :], words[:, u, :], ident_f32[:])
+            nc.scalar.copy(
+                flat(turned_tile[:, t * P : (t + 1) * P, :]).bitcast(F32).rearrange("p (c u) -> p c u", u=2),
+                turned[:, 0:2, :].rearrange("p u c -> p c u"),
+            )
+
+        x_listed = sbuf("x_listed", [P, PACK, N], BF16)
         x_d = sbuf("x_d", [P, N, PACK], BF16)
         x_r = sbuf("x_r", [P, D, PACK], BF16)
-        x_by_slot = x_d[:].rearrange("p (s m) t -> p t m s", s=PACK)
         for t in range(PACK):
-            nc.vector.tensor_copy(x_by_slot[:, t, :, :], u_plane[t][:].indirect(user_list[:]))
-        for u in range(2):
-            turn_pairs(x_r[:, u * HALF : (u + 1) * HALF, :], x_d, u, 2 + u)
+            nc.vector.tensor_copy(x_listed[:, t, :], u_plane[t][:].indirect(user_list[:]))
+            turn_plane(x_r, x_listed, t, PACK + t)
+        nc.scalar.copy(
+            x_d[:].rearrange("p (s m) t -> p m s t", s=PACK),
+            x_listed[:].rearrange("p t (m s) -> p m s t", s=PACK),
+        )
         x_d_codes = sbuf("x_d_codes", [P, N], U32)
         x_d_scales = sbuf("x_d_scales", [P, N], U8)
         quantise(x_d_codes[:], x_d_scales[:], x_d[:], E4M3)
@@ -125,9 +138,15 @@ def tile_attend_gmf_bpr_vu_kernel(tc, uT, vT, us, ts, offs, uoffs, out_0, out_1)
         w_i_scales = sbuf("w_i_scales", [P, D], U8)
         w_d_codes = sbuf("w_d_codes", [P, N], U32)
         w_d_scales = sbuf("w_d_scales", [P, N], U8)
-        w_by_slot = w_d[:].rearrange("p (k m) t -> p t m k", k=PACK)
+        w_listed = sbuf("w_listed", [P, PACK, N], BF16)
         for t in range(PACK):
-            nc.vector.tensor_copy(w_by_slot[:, t, :, :], v_plane[t][:].indirect(item_list[:]))
+            nc.vector.tensor_copy(w_listed[:, t, :], v_plane[t][:].indirect(item_list[:]))
+            if t < PACK - 1:
+                turn_plane(w_i, w_listed, t, 2 + t % 2)
+        w_by_block = w_listed[:].rearrange("p t (m k) -> p k m t", k=PACK)
+        for k in range(PACK):
+            copy = nc.vector.tensor_copy if k < 2 else nc.scalar.copy
+            copy(w_d[:, k * P : (k + 1) * P, :], w_by_block[:, k, :, :])
 
         scaled = sbuf("scaled", [P, N, PACK], F32)
         margin = sbuf("margin", [P, PACK, HALF], F32)
@@ -208,8 +227,7 @@ def tile_attend_gmf_bpr_vu_kernel(tc, uT, vT, us, ts, offs, uoffs, out_0, out_1)
         def user_product(t, number):
             product(du[t], number, w_i_codes[:, block(t)], w_i_scales[:, block(t)], h_i_codes, h_i_scales, nc.scalar.copy)
 
-        for u in range(2):
-            turn_pairs(w_i[:, u * HALF : (u + 1) * HALF, :], w_d, u, PACK + u)
+        turn_plane(w_i, w_listed, PACK - 1, 3)
         w_i_codes = sbuf("w_i_codes", [P, D], U32, tag="q%d" % (PACK - 1))
         quantise(w_i_codes[:], w_i_scales[:], w_i[:], E4M3)
 

@@ -71,10 +71,10 @@ def tile_attend_gmf_bpr_vu_kernel(tc, uT, vT, us, ts, offs, uoffs, out_0, out_1)
             return ap.rearrange("p a b -> p (a b)")
 
         def turn_pairs(dst, src, u, number):
-            words = flat(src[:]).bitcast(F32).rearrange("p (k m u) -> p u k m", k=PACK, u=2)
             turned = bank(number)
             for k in range(PACK):
-                nc.tensor.transpose(turned[:, k, :], words[:, u, k, :], ident_f32[:])
+                words = flat(src[k][:]).bitcast(F32).rearrange("p (m u) -> p u m", u=2)
+                nc.tensor.transpose(turned[:, k, :], words[:, u, :], ident_f32[:])
             nc.scalar.copy(
                 dst.rearrange("p (e c) k -> p e c k", e=2),
                 flat(turned[:]).bitcast(BF16).rearrange("p (k c e) -> p e c k", k=PACK, e=2),
@@ -151,7 +151,7 @@ def tile_attend_gmf_bpr_vu_kernel(tc, uT, vT, us, ts, offs, uoffs, out_0, out_1)
         scaled = sbuf("scaled", [P, N, PACK], F32)
         margin = sbuf("margin", [P, PACK, HALF], F32)
         q = [sbuf("q%d" % k, [P, 1, HALF], F32) for k in range(PACK)]
-        h_r = sbuf("h_r", [P, N, PACK], BF16)
+        h_r = [sbuf("h_r%d" % k, [P, P, PACK], BF16) for k in range(PACK)]
         h_r_codes = sbuf("h_r_codes", [P, N], U32)
         h_r_scales = sbuf("h_r_scales", [P, N], U8)
         scores = [bank(PACK + k) for k in range(PACK)]
@@ -178,23 +178,30 @@ def tile_attend_gmf_bpr_vu_kernel(tc, uT, vT, us, ts, offs, uoffs, out_0, out_1)
         def scale(k):
             nc.vector.tensor_tensor(scaled[:, block(k), :], scores[k][:].rearrange("p s m -> p m s"), signed[:, block(k), :], MULT)
 
-        def weigh(k):
-            nc.vector.tensor_tensor(margin[:, k, :], by_half(scaled, k)[:, 0, :], by_half(scaled, k)[:, 1, :], ADD)
-            nc.scalar.activation(q[k][:, 0, :], margin[:, k, :], SIGMOID)
+        def weigh(engine, blocks):
+            halves = scaled[:].rearrange("p (k a m) s -> p k a (m s)", k=PACK, a=2)
+            engine.tensor_tensor(margin[:, blocks, :], halves[:, blocks, 0, :], halves[:, blocks, 1, :], ADD)
+            for k in range(blocks.start, blocks.stop):
+                nc.scalar.activation(q[k][:, 0, :], margin[:, k, :], SIGMOID)
 
         def gradient(k):
-            nc.vector.tensor_tensor(by_half(h_r, k), q[k][:].to_broadcast([P, 2, HALF]), by_half(signed, k), MULT)
+            nc.vector.tensor_tensor(h_r[k][:].rearrange("p (a m) s -> p a (m s)", a=2), q[k][:].to_broadcast([P, 2, HALF]), by_half(signed, k), MULT)
 
         def quantise_h(k):
-            quantise(h_r_codes[:, block(k)], h_r_scales[:, block(k)], h_r[:, block(k), :], E5M2)
+            quantise(h_r_codes[:, block(k)], h_r_scales[:, block(k)], h_r[k][:], E5M2)
 
         for k in range(PACK):
             score(k)
-        stages = [scale, weigh, gradient, quantise_h]
-        for step in range(PACK + len(stages) - 1):
-            for lag, stage in enumerate(stages):
-                if 0 <= step - lag < PACK:
-                    stage(step - lag)
+        for k in range(PACK):
+            scale(k)
+        weigh(nc.gpsimd, slice(0, 1))
+        weigh(nc.gpsimd, slice(1, 2))
+        gradient(0)
+        weigh(nc.vector, slice(2, PACK))
+        for k in range(1, PACK):
+            gradient(k)
+            quantise_h(k - 1)
+        quantise_h(PACK - 1)
 
         dv = [sbuf("dv%d" % t, [P, N], F32) for t in range(PACK)]
         du = [sbuf("du%d" % t, [P, N], F32) for t in range(PACK)]
@@ -228,13 +235,13 @@ def tile_attend_gmf_bpr_vu_kernel(tc, uT, vT, us, ts, offs, uoffs, out_0, out_1)
             product(du[t], number, w_i_codes[:, block(t)], w_i_scales[:, block(t)], h_i_codes, h_i_scales, nc.scalar.copy)
 
         turn_plane(w_i, w_listed, PACK - 1, 3)
-        w_i_codes = sbuf("w_i_codes", [P, D], U32, tag="q%d" % (PACK - 1))
-        quantise(w_i_codes[:], w_i_scales[:], w_i[:], E4M3)
 
         item_product(0, 0, nc.vector.tensor_copy)
         place(0, dv[0], dv_window, item_list, out_0)
         for u in range(2):
             turn_pairs(h_i[:, u * HALF : (u + 1) * HALF, :], h_r, u, 1 + u)
+        w_i_codes = sbuf("w_i_codes", [P, D], U32, tag="h_r%d" % (PACK - 1))
+        quantise(w_i_codes[:], w_i_scales[:], w_i[:], E4M3)
         quantise(h_i_codes[:], h_i_scales[:], h_i[:], E5M2)
         item_product(1, 2)
         place(1, dv[1], dv_window, item_list, out_0)

@@ -143,6 +143,17 @@ def tile_attend_gmf_bpr_vu_kernel(tc, uT, vT, us, ts, offs, uoffs, out_0, out_1)
             nc.vector.tensor_copy(w_listed[:, t, :], v_plane[t][:].indirect(item_list[:]))
             if t < PACK - 1:
                 turn_plane(w_i, w_listed, t, 2 + t % 2)
+        warm_bank = bank(2)
+        for repeat in range(3):
+            nc.tensor.matmul_mx(
+                out=flat(warm_bank[:]),
+                lhsT=x_d_codes[:, 0:P].bitcast(E4M3),
+                lhsT_scale=x_d_scales[:, 0:P],
+                rhs=x_d_codes[:].bitcast(E4M3),
+                rhs_scale=x_d_scales[:],
+                start=True,
+                stop=True,
+            )
         w_by_block = w_listed[:].rearrange("p t (m k) -> p k m t", k=PACK)
         for k in range(PACK):
             copy = nc.vector.tensor_copy if k < 2 else nc.scalar.copy
@@ -234,7 +245,7 @@ def tile_attend_gmf_bpr_vu_kernel(tc, uT, vT, us, ts, offs, uoffs, out_0, out_1)
         def user_product(t, number):
             product(du[t], number, w_i_codes[:, block(t)], w_i_scales[:, block(t)], h_i_codes, h_i_scales, nc.scalar.copy)
 
-        turn_plane(w_i, w_listed, PACK - 1, 3)
+        turn_plane(w_i, w_listed, PACK - 1, PACK)
 
         item_product(0, 0, nc.vector.tensor_copy)
         place(0, dv[0], dv_window, item_list, out_0)
@@ -249,7 +260,7 @@ def tile_attend_gmf_bpr_vu_kernel(tc, uT, vT, us, ts, offs, uoffs, out_0, out_1)
         place(0, du[0], du_window, user_list, out_1)
         user_product(1, 3)
         place(1, du[1], du_window, user_list, out_1)
-        item_product(2, 4)
+        item_product(2, 5)
         place(2, dv[2], dv_window, item_list, out_0)
         item_product(3, 6)
         place(3, dv[3], dv_window, item_list, out_0)

@@ -47,13 +47,13 @@ def tile_attend_gmf_bpr_vu_kernel(tc, uT, vT, us, ts, offs, uoffs, out_0, out_1)
         item_list = keep.tile([P, COLS], U16, name="item_list")
         u_plane = [sbuf("u_plane%d" % t, [P, T], F32) for t in range(PACK)]
         v_plane = [sbuf("v_plane%d" % t, [P, T], F32) for t in range(PACK)]
+        nc.sync.dma_start(item_list[:], offs)
         nc.sync.dma_start(u_plane[0][:], planes(uT)[:, 0, :])
         nc.sync.dma_start(user_list[:], uoffs)
-        nc.sync.dma_start(item_list[:], offs)
         ts_row = sbuf("ts_row", [P, T], F32)
         row_scale = sbuf("row_scale", [P, PACK], F32)
-        nc.sync.dma_start(ts_row[P - 1 : P, :], ts[0:1, :])
-        nc.sync.dma_start(row_scale[:], us.rearrange("b (p t) o -> p (b t o)", t=PACK))
+        nc.scalar.dma_start(ts_row[P - 1 : P, :], ts[0:1, :])
+        nc.scalar.dma_start(row_scale[:], us.rearrange("b (p t) o -> p (b t o)", t=PACK))
         nc.gpsimd.memset(ts_row[0 : P - 1, :].bitcast(I32), 0)
         for t in range(1, PACK):
             nc.sync.dma_start(u_plane[t][:], planes(uT)[:, t, :])
@@ -122,16 +122,19 @@ def tile_attend_gmf_bpr_vu_kernel(tc, uT, vT, us, ts, offs, uoffs, out_0, out_1)
         for t in range(PACK):
             nc.vector.tensor_copy(x_listed[:, t, :], u_plane[t][:].indirect(user_list[:]))
             turn_plane(x_r, x_listed, t, PACK + t)
-        nc.scalar.copy(
+        nc.vector.tensor_copy(
             x_d[:].rearrange("p (s m) t -> p m s t", s=PACK),
             x_listed[:].rearrange("p t (m s) -> p m s t", s=PACK),
         )
         x_d_codes = sbuf("x_d_codes", [P, N], U32)
         x_d_scales = sbuf("x_d_scales", [P, N], U8)
         quantise(x_d_codes[:], x_d_scales[:], x_d[:], E4M3)
-        x_r_codes = sbuf("x_r_codes", [P, D], U32)
+        x_r_codes = [sbuf("x_r_codes0", [P, P], U32), sbuf("x_r_codes1", [P, P], U32), sbuf("x_r_codes23", [P, HALF], U32)]
         x_r_scales = sbuf("x_r_scales", [P, D], U8)
-        quantise(x_r_codes[:], x_r_scales[:], x_r[:], E4M3)
+        quantise(x_r_codes[0][:], x_r_scales[:, 0:P], x_r[:, 0:P, :], E4M3)
+        quantise(x_r_codes[1][:], x_r_scales[:, P:HALF], x_r[:, P:HALF, :], E4M3)
+        quantise(x_r_codes[2][:], x_r_scales[:, HALF:], x_r[:, HALF:, :], E4M3)
+        x_r_block = [x_r_codes[0][:], x_r_codes[1][:], x_r_codes[2][:, 0:P], x_r_codes[2][:, P:]]
 
         w_d = sbuf("w_d", [P, N, PACK], BF16)
         w_i = sbuf("w_i", [P, D, PACK], BF16)
@@ -154,10 +157,10 @@ def tile_attend_gmf_bpr_vu_kernel(tc, uT, vT, us, ts, offs, uoffs, out_0, out_1)
                 start=True,
                 stop=True,
             )
-        w_by_block = w_listed[:].rearrange("p t (m k) -> p k m t", k=PACK)
-        for k in range(PACK):
-            copy = nc.vector.tensor_copy if k < 2 else nc.scalar.copy
-            copy(w_d[:, k * P : (k + 1) * P, :], w_by_block[:, k, :, :])
+        w_by_slot = w_d[:].rearrange("p (k m) t -> p m k t", k=PACK)
+        w_by_plane = w_listed[:].rearrange("p t (m k) -> p m k t", k=PACK)
+        nc.vector.tensor_copy(w_by_slot[:, :, 0:2, :], w_by_plane[:, :, 0:2, :])
+        nc.scalar.copy(w_by_slot[:, :, 2:4, :], w_by_plane[:, :, 2:4, :])
 
         scaled = sbuf("scaled", [P, N, PACK], F32)
         margin = sbuf("margin", [P, PACK, HALF], F32)
@@ -189,11 +192,9 @@ def tile_attend_gmf_bpr_vu_kernel(tc, uT, vT, us, ts, offs, uoffs, out_0, out_1)
         def scale(k):
             nc.vector.tensor_tensor(scaled[:, block(k), :], scores[k][:].rearrange("p s m -> p m s"), signed[:, block(k), :], MULT)
 
-        def weigh(engine, blocks):
-            halves = scaled[:].rearrange("p (k a m) s -> p k a (m s)", k=PACK, a=2)
-            engine.tensor_tensor(margin[:, blocks, :], halves[:, blocks, 0, :], halves[:, blocks, 1, :], ADD)
-            for k in range(blocks.start, blocks.stop):
-                nc.scalar.activation(q[k][:, 0, :], margin[:, k, :], SIGMOID)
+        def weigh(k):
+            nc.vector.tensor_tensor(margin[:, k, :], by_half(scaled, k)[:, 0, :], by_half(scaled, k)[:, 1, :], ADD)
+            nc.scalar.activation(q[k][:, 0, :], margin[:, k, :], SIGMOID)
 
         def gradient(k):
             nc.vector.tensor_tensor(h_r[k][:].rearrange("p (a m) s -> p a (m s)", a=2), q[k][:].to_broadcast([P, 2, HALF]), by_half(signed, k), MULT)
@@ -203,16 +204,11 @@ def tile_attend_gmf_bpr_vu_kernel(tc, uT, vT, us, ts, offs, uoffs, out_0, out_1)
 
         for k in range(PACK):
             score(k)
-        for k in range(PACK):
-            scale(k)
-        weigh(nc.gpsimd, slice(0, 1))
-        weigh(nc.gpsimd, slice(1, 2))
-        gradient(0)
-        weigh(nc.vector, slice(2, PACK))
-        for k in range(1, PACK):
-            gradient(k)
-            quantise_h(k - 1)
-        quantise_h(PACK - 1)
+        stages = [scale, weigh, gradient, quantise_h]
+        for step in range(PACK + len(stages) - 1):
+            for lag, stage in enumerate(stages):
+                if 0 <= step - lag < PACK:
+                    stage(step - lag)
 
         dv = [sbuf("dv%d" % t, [P, N], F32) for t in range(PACK)]
         du = [sbuf("du%d" % t, [P, N], F32) for t in range(PACK)]
@@ -235,20 +231,20 @@ def tile_attend_gmf_bpr_vu_kernel(tc, uT, vT, us, ts, offs, uoffs, out_0, out_1)
             nc.vector.tensor_copy(window[:].indirect(entries[:]), values[:])
             nc.sync.dma_start(planes(out)[:, t, :], window[:])
 
-        h_i = sbuf("h_i", [P, N, PACK], BF16)
         h_i_codes = sbuf("h_i_codes", [P, N], U32)
         h_i_scales = sbuf("h_i_scales", [P, N], U8)
 
         def item_product(t, number, copy=nc.scalar.copy):
-            product(dv[t], number, x_r_codes[:, block(t)], x_r_scales[:, block(t)], h_r_codes, h_r_scales, copy)
+            product(dv[t], number, x_r_block[t], x_r_scales[:, block(t)], h_r_codes, h_r_scales, copy)
 
         def user_product(t, number):
             product(du[t], number, w_i_codes[:, block(t)], w_i_scales[:, block(t)], h_i_codes, h_i_scales, nc.scalar.copy)
 
         turn_plane(w_i, w_listed, PACK - 1, PACK)
 
-        item_product(0, 0, nc.vector.tensor_copy)
+        item_product(0, 0)
         place(0, dv[0], dv_window, item_list, out_0)
+        h_i = sbuf("h_i", [P, N, PACK], BF16, tag="x_r_codes0")
         for u in range(2):
             turn_pairs(h_i[:, u * HALF : (u + 1) * HALF, :], h_r, u, 1 + u)
         w_i_codes = sbuf("w_i_codes", [P, D], U32, tag="h_r%d" % (PACK - 1))

@@ -97,6 +97,18 @@ def tile_attend_gmf_bpr_vu_kernel(tc, uT, vT, us, ts, offs, uoffs, out_0, out_1)
             nc.tensor.transpose(ts_turned[:, k, :], ts_listed[:].rearrange("p (m k) -> p k m", k=PACK)[:, k, :], ident_f32[:])
         ts_column = sbuf("ts_column", [P, PACK], F32)
         nc.scalar.activation(ts_column[:], ts_turned[:, :, P - 1], COPY, scale=sign[:])
+        ts_paired = sbuf("ts_paired", [P, N], F32)
+        nc.scalar.copy(
+            ts_paired[:].rearrange("p (j m e) -> p j m e", j=2, e=2),
+            ts_listed[:].rearrange("p (m j e) -> p j m e", j=2, e=2),
+        )
+        pair_turned = bank(3)
+        for c in range(PACK):
+            nc.tensor.transpose(pair_turned[:, c, :], ts_paired[:, c * P : (c + 1) * P], ident_f32[:])
+        pair_scale = sbuf("pair_scale", [P, 2, 2], F32)
+        pair_last = pair_turned[:, :, P - 1].rearrange("p (j a) -> p j a", a=2)
+        nc.scalar.activation(pair_scale[:, :, 0], pair_last[:, :, 0], COPY, scale=-1.0)
+        nc.scalar.activation(pair_scale[:, :, 1], pair_last[:, :, 1], COPY)
         ts_spread = bank(1)
         for k in range(PACK):
             nc.tensor.transpose(ts_spread[:, k, :], ts_column[:, k : k + 1].to_broadcast([P, P]), ident_f32[:])
@@ -106,13 +118,16 @@ def tile_attend_gmf_bpr_vu_kernel(tc, uT, vT, us, ts, offs, uoffs, out_0, out_1)
         signed = sbuf("signed", [P, N, PACK], F32)
         nc.scalar.copy(signed[:], signed_by_row[:].rearrange("p s i -> p i s"))
 
-        def turn_plane(turned_tile, listed, t, number):
+        def turn_plane(listed, t, number):
             words = listed[:, t, :].bitcast(F32).rearrange("p (m u) -> p u m", u=2)
             turned = bank(number)
             for u in range(2):
                 nc.tensor.transpose(turned[:, u, :], words[:, u, :], ident_f32[:])
+            return turned
+
+        def lay_turned(dst, turned):
             nc.scalar.copy(
-                flat(turned_tile[:, t * P : (t + 1) * P, :]).bitcast(F32).rearrange("p (c u) -> p c u", u=2),
+                flat(dst).bitcast(F32).rearrange("p (c u) -> p c u", u=2),
                 turned[:, 0:2, :].rearrange("p u c -> p c u"),
             )
 
@@ -121,7 +136,7 @@ def tile_attend_gmf_bpr_vu_kernel(tc, uT, vT, us, ts, offs, uoffs, out_0, out_1)
         x_r = sbuf("x_r", [P, D, PACK], BF16)
         for t in range(PACK):
             nc.vector.tensor_copy(x_listed[:, t, :], u_plane[t][:].indirect(user_list[:]))
-            turn_plane(x_r, x_listed, t, PACK + t)
+            lay_turned(x_r[:, t * P : (t + 1) * P, :], turn_plane(x_listed, t, PACK + t))
         nc.vector.tensor_copy(
             x_d[:].rearrange("p (s m) t -> p m s t", s=PACK),
             x_listed[:].rearrange("p t (m s) -> p m s t", s=PACK),
@@ -137,78 +152,105 @@ def tile_attend_gmf_bpr_vu_kernel(tc, uT, vT, us, ts, offs, uoffs, out_0, out_1)
         x_r_block = [x_r_codes[0][:], x_r_codes[1][:], x_r_codes[2][:, 0:P], x_r_codes[2][:, P:]]
 
         w_d = sbuf("w_d", [P, N, PACK], BF16)
-        w_i = sbuf("w_i", [P, D, PACK], BF16)
+        w_i = [sbuf("w_i0", [P, HALF, PACK], BF16)]
         w_i_scales = sbuf("w_i_scales", [P, D], U8)
         w_d_codes = sbuf("w_d_codes", [P, N], U32)
         w_d_scales = sbuf("w_d_scales", [P, N], U8)
         w_listed = sbuf("w_listed", [P, PACK, N], BF16)
-        for t in range(PACK):
+        for t in range(2):
             nc.vector.tensor_copy(w_listed[:, t, :], v_plane[t][:].indirect(item_list[:]))
-            if t < PACK - 1:
-                turn_plane(w_i, w_listed, t, 2 + t % 2)
-        warm_bank = bank(2)
-        for repeat in range(3):
+            lay_turned(w_i[0][:, t * P : (t + 1) * P, :], turn_plane(w_listed, t, 2 + t))
+        nc.vector.tensor_copy(w_listed[:, 2, :], v_plane[2][:].indirect(item_list[:]))
+        third_turned = turn_plane(w_listed, 2, 2)
+        for repeat in range(6):
             nc.tensor.matmul_mx(
-                out=flat(warm_bank[:]),
+                out=flat(third_turned[:])[:, HALF:],
                 lhsT=x_d_codes[:, 0:P].bitcast(E4M3),
                 lhsT_scale=x_d_scales[:, 0:P],
-                rhs=x_d_codes[:].bitcast(E4M3),
-                rhs_scale=x_d_scales[:],
+                rhs=x_d_codes[:, 0:HALF].bitcast(E4M3),
+                rhs_scale=x_d_scales[:, 0:HALF],
                 start=True,
                 stop=True,
             )
-        w_by_slot = w_d[:].rearrange("p (k m) t -> p m k t", k=PACK)
-        w_by_plane = w_listed[:].rearrange("p t (m k) -> p m k t", k=PACK)
-        nc.vector.tensor_copy(w_by_slot[:, :, 0:2, :], w_by_plane[:, :, 0:2, :])
-        nc.scalar.copy(w_by_slot[:, :, 2:4, :], w_by_plane[:, :, 2:4, :])
+        for a in range(2):
+            nc.vector.tensor_copy(
+                w_listed[:, PACK - 1, a * HALF : (a + 1) * HALF],
+                v_plane[PACK - 1][:].indirect(item_list[:, a * COLS // 2 : (a + 1) * COLS // 2]),
+            )
+        w_by_tile = w_d[:].rearrange("p (j a m e) t -> p j a m e t", j=2, a=2, e=2)
+        w_by_plane = w_listed[:].rearrange("p t (a m j e) -> p j a m e t", a=2, j=2, e=2)
+        for j in range(2):
+            nc.scalar.copy(w_by_tile[:, j, 0], w_by_plane[:, j, 0])
+            nc.vector.tensor_copy(w_by_tile[:, j, 1], w_by_plane[:, j, 1])
 
-        scaled = sbuf("scaled", [P, N, PACK], F32)
-        margin = sbuf("margin", [P, PACK, HALF], F32)
-        q = [sbuf("q%d" % k, [P, 1, HALF], F32) for k in range(PACK)]
+        negative = sbuf("negative", [P, 2, N], F32)
+        margin = sbuf("margin", [P, 2, N], F32)
+        q = [sbuf("q%d" % j, [P, 2, PACK, P // 2], F32) for j in range(2)]
         h_r = [sbuf("h_r%d" % k, [P, P, PACK], BF16) for k in range(PACK)]
         h_r_codes = sbuf("h_r_codes", [P, N], U32)
         h_r_scales = sbuf("h_r_scales", [P, N], U8)
-        scores = [bank(PACK + k) for k in range(PACK)]
 
         def block(k):
             return slice(k * P, (k + 1) * P)
 
-        def by_half(tile, k):
-            return tile[:, block(k), :].rearrange("p (a m) s -> p a (m s)", a=2)
+        def half(u):
+            return slice(u * HALF, (u + 1) * HALF)
 
-        def score(k):
-            quantise(w_d_codes[:, block(k)], w_d_scales[:, block(k)], w_d[:, block(k), :], E4M3)
-            for s in range(PACK):
+        def subtract(j, u):
+            scores = flat(bank(PACK + 2 * j + u)[:])
+            for a in (1, 0):
                 nc.tensor.matmul_mx(
-                    out=scores[k][:, s, :],
-                    lhsT=x_d_codes[:, block(s)].bitcast(E4M3),
-                    lhsT_scale=x_d_scales[:, block(s)],
-                    rhs=w_d_codes[:, block(k)].bitcast(E4M3),
-                    rhs_scale=w_d_scales[:, block(k)],
+                    out=scores[:, half(a)],
+                    lhsT=w_d_codes[:, block(2 * j + a)].bitcast(E4M3),
+                    lhsT_scale=w_d_scales[:, block(2 * j + a)],
+                    rhs=x_d_codes[:, half(u)].bitcast(E4M3),
+                    rhs_scale=x_d_scales[:, half(u)],
                     start=True,
                     stop=True,
                 )
+            nc.scalar.activation(negative[:, j, half(u)], scores[:, half(1)], COPY, scale=pair_scale[:, j, 1:2])
+            nc.vector.scalar_tensor_tensor(
+                margin[:, j, half(u)], scores[:, half(0)], pair_scale[:, j, 0:1], negative[:, j, half(u)], MULT, ADD
+            )
 
-        def scale(k):
-            nc.vector.tensor_tensor(scaled[:, block(k), :], scores[k][:].rearrange("p s m -> p m s"), signed[:, block(k), :], MULT)
-
-        def weigh(k):
-            nc.vector.tensor_tensor(margin[:, k, :], by_half(scaled, k)[:, 0, :], by_half(scaled, k)[:, 1, :], ADD)
-            nc.scalar.activation(q[k][:, 0, :], margin[:, k, :], SIGMOID)
+        def weigh(j, u):
+            turned = bank(PACK + 2 * j + u)
+            for e in range(2):
+                nc.tensor.transpose(turned[:, e, :], margin[:, j, block(2 * u + e)], ident_f32[:])
+            for e in range(2):
+                s = 2 * u + e
+                nc.scalar.activation(
+                    q[j][:, :, s, :], turned[:, e, :].rearrange("p (m e) -> p e m", e=2), SIGMOID, scale=row_scale[:, s : s + 1]
+                )
 
         def gradient(k):
-            nc.vector.tensor_tensor(h_r[k][:].rearrange("p (a m) s -> p a (m s)", a=2), q[k][:].to_broadcast([P, 2, HALF]), by_half(signed, k), MULT)
+            j, e = divmod(k, 2)
+            nc.vector.tensor_tensor(
+                h_r[k][:].rearrange("p (a m) s -> p a m s", a=2),
+                q[j][:, e : e + 1, :, :].rearrange("p a s m -> p a m s").to_broadcast([P, 2, P // 2, PACK]),
+                signed[:, block(k), :].rearrange("p (a m) s -> p a m s", a=2),
+                MULT,
+            )
 
         def quantise_h(k):
             quantise(h_r_codes[:, block(k)], h_r_scales[:, block(k)], h_r[k][:], E5M2)
 
-        for k in range(PACK):
-            score(k)
-        stages = [scale, weigh, gradient, quantise_h]
-        for step in range(PACK + len(stages) - 1):
-            for lag, stage in enumerate(stages):
-                if 0 <= step - lag < PACK:
-                    stage(step - lag)
+        for c in (1, 0, 3, 2):
+            quantise(w_d_codes[:, block(c)], w_d_scales[:, block(c)], w_d[:, block(c), :], E4M3)
+        for j in range(2):
+            for u in range(2):
+                subtract(j, u)
+        for j in range(2):
+            for u in range(2):
+                weigh(j, u)
+        w_i.append(sbuf("w_i1", [P, HALF, PACK], BF16, tag="margin"))
+        lay_turned(w_i[1][:, 0:P, :], third_turned)
+        lay_turned(w_i[1][:, P:, :], turn_plane(w_listed, PACK - 1, 7))
+        gradient(0)
+        for k in range(1, PACK):
+            gradient(k)
+            quantise_h(k - 1)
+        quantise_h(PACK - 1)
 
         dv = [sbuf("dv%d" % t, [P, N], F32) for t in range(PACK)]
         du = [sbuf("du%d" % t, [P, N], F32) for t in range(PACK)]
@@ -240,7 +282,6 @@ def tile_attend_gmf_bpr_vu_kernel(tc, uT, vT, us, ts, offs, uoffs, out_0, out_1)
         def user_product(t, number):
             product(du[t], number, w_i_codes[:, block(t)], w_i_scales[:, block(t)], h_i_codes, h_i_scales, nc.scalar.copy)
 
-        turn_plane(w_i, w_listed, PACK - 1, PACK)
 
         item_product(0, 0)
         place(0, dv[0], dv_window, item_list, out_0)
@@ -248,11 +289,12 @@ def tile_attend_gmf_bpr_vu_kernel(tc, uT, vT, us, ts, offs, uoffs, out_0, out_1)
         for u in range(2):
             turn_pairs(h_i[:, u * HALF : (u + 1) * HALF, :], h_r, u, 1 + u)
         w_i_codes = sbuf("w_i_codes", [P, D], U32, tag="h_r%d" % (PACK - 1))
-        quantise(w_i_codes[:], w_i_scales[:], w_i[:], E4M3)
+        for u in range(2):
+            quantise(w_i_codes[:, half(u)], w_i_scales[:, half(u)], w_i[u][:], E4M3)
         quantise(h_i_codes[:], h_i_scales[:], h_i[:], E5M2)
         item_product(1, 2)
         place(1, dv[1], dv_window, item_list, out_0)
-        user_product(0, 7)
+        user_product(0, 4)
         place(0, du[0], du_window, user_list, out_1)
         user_product(1, 3)
         place(1, du[1], du_window, user_list, out_1)

@@ -116,7 +116,10 @@ def tile_attend_gmf_bpr_vu_kernel(tc, uT, vT, us, ts, offs, uoffs, out_0, out_1)
         for s in range(PACK):
             nc.scalar.activation(signed_by_row[:, s, :], flat(ts_spread[:]), COPY, scale=row_scale[:, s : s + 1])
         signed = sbuf("signed", [P, N, PACK], F32)
-        nc.scalar.copy(signed[:], signed_by_row[:].rearrange("p s i -> p i s"))
+        nc.scalar.copy(
+            flat(signed[:]).rearrange("p (c s i) -> p c s i", s=PACK, i=PACK),
+            signed_by_row[:].rearrange("p s (c i) -> p c s i", i=PACK),
+        )
 
         def turn_plane(listed, t, number):
             words = listed[:, t, :].bitcast(F32).rearrange("p (m u) -> p u m", u=2)
@@ -177,15 +180,15 @@ def tile_attend_gmf_bpr_vu_kernel(tc, uT, vT, us, ts, offs, uoffs, out_0, out_1)
                 w_listed[:, PACK - 1, a * HALF : (a + 1) * HALF],
                 v_plane[PACK - 1][:].indirect(item_list[:, a * COLS // 2 : (a + 1) * COLS // 2]),
             )
-        w_by_tile = w_d[:].rearrange("p (j a m e) t -> p j a m e t", j=2, a=2, e=2)
-        w_by_plane = w_listed[:].rearrange("p t (a m j e) -> p j a m e t", a=2, j=2, e=2)
+        w_by_tile = w_d[:].rearrange("p (j a c n e) t -> p j a c t n e", j=2, a=2, n=2, e=2)
+        w_by_plane = w_listed[:].rearrange("p t (a c n j e) -> p j a c t n e", a=2, n=2, j=2, e=2)
         for j in range(2):
             nc.scalar.copy(w_by_tile[:, j, 0], w_by_plane[:, j, 0])
             nc.vector.tensor_copy(w_by_tile[:, j, 1], w_by_plane[:, j, 1])
 
         negative = sbuf("negative", [P, 2, N], F32)
         margin = sbuf("margin", [P, 2, N], F32)
-        q = [sbuf("q%d" % j, [P, 2, PACK, P // 2], F32) for j in range(2)]
+        q = [sbuf("q%d" % j, [P, 2, HALF], F32) for j in range(2)]
         h_r = [sbuf("h_r%d" % k, [P, P, PACK], BF16) for k in range(PACK)]
         h_r_codes = sbuf("h_r_codes", [P, N], U32)
         h_r_scales = sbuf("h_r_scales", [P, N], U8)
@@ -220,15 +223,18 @@ def tile_attend_gmf_bpr_vu_kernel(tc, uT, vT, us, ts, offs, uoffs, out_0, out_1)
             for e in range(2):
                 s = 2 * u + e
                 nc.scalar.activation(
-                    q[j][:, :, s, :], turned[:, e, :].rearrange("p (m e) -> p e m", e=2), SIGMOID, scale=row_scale[:, s : s + 1]
+                    q[j][:].rearrange("p e (c s i) -> p s e c i", s=PACK, i=PACK)[:, s],
+                    turned[:, e, :].rearrange("p (c i e) -> p e c i", i=PACK, e=2),
+                    SIGMOID,
+                    scale=row_scale[:, s : s + 1],
                 )
 
         def gradient(k):
             j, e = divmod(k, 2)
             nc.vector.tensor_tensor(
-                h_r[k][:].rearrange("p (a m) s -> p a m s", a=2),
-                q[j][:, e : e + 1, :, :].rearrange("p a s m -> p a m s").to_broadcast([P, 2, P // 2, PACK]),
-                signed[:, block(k), :].rearrange("p (a m) s -> p a m s", a=2),
+                h_r[k][:].rearrange("p (a c i) s -> p a c s i", a=2, i=PACK),
+                q[j][:, e : e + 1, :].rearrange("p a (c s i) -> p a c s i", s=PACK, i=PACK).to_broadcast([P, 2, 16, PACK, PACK]),
+                flat(signed[:, block(k), :]).rearrange("p (a c s i) -> p a c s i", a=2, s=PACK, i=PACK),
                 MULT,
             )
 

@@ -182,9 +182,9 @@ def tile_attend_gmf_bpr_vu_kernel(tc, uT, vT, us, ts, offs, uoffs, out_0, out_1)
             )
         w_by_tile = w_d[:].rearrange("p (j a c n e) t -> p j a c t n e", j=2, a=2, n=2, e=2)
         w_by_plane = w_listed[:].rearrange("p t (a c n j e) -> p j a c t n e", a=2, n=2, j=2, e=2)
-        for j in range(2):
-            nc.scalar.copy(w_by_tile[:, j, 0], w_by_plane[:, j, 0])
-            nc.vector.tensor_copy(w_by_tile[:, j, 1], w_by_plane[:, j, 1])
+        for a in range(2):
+            nc.vector.tensor_copy(w_by_tile[:, 0, a], w_by_plane[:, 0, a])
+            nc.scalar.copy(w_by_tile[:, 1, a], w_by_plane[:, 1, a])
 
         negative = sbuf("negative", [P, 2, N], F32)
         margin = sbuf("margin", [P, 2, N], F32)
@@ -201,7 +201,7 @@ def tile_attend_gmf_bpr_vu_kernel(tc, uT, vT, us, ts, offs, uoffs, out_0, out_1)
 
         def subtract(j, u):
             scores = flat(bank(PACK + 2 * j + u)[:])
-            for a in (1, 0):
+            for a in range(2):
                 nc.tensor.matmul_mx(
                     out=scores[:, half(a)],
                     lhsT=w_d_codes[:, block(2 * j + a)].bitcast(E4M3),
@@ -241,7 +241,7 @@ def tile_attend_gmf_bpr_vu_kernel(tc, uT, vT, us, ts, offs, uoffs, out_0, out_1)
         def quantise_h(k):
             quantise(h_r_codes[:, block(k)], h_r_scales[:, block(k)], h_r[k][:], E5M2)
 
-        for c in (1, 0, 3, 2):
+        for c in range(PACK):
             quantise(w_d_codes[:, block(c)], w_d_scales[:, block(c)], w_d[:, block(c), :], E4M3)
         for j in range(2):
             for u in range(2):
@@ -304,9 +304,9 @@ def tile_attend_gmf_bpr_vu_kernel(tc, uT, vT, us, ts, offs, uoffs, out_0, out_1)
         place(0, du[0], du_window, user_list, out_1)
         user_product(1, 3)
         place(1, du[1], du_window, user_list, out_1)
-        item_product(2, 5)
+        item_product(2, 2)
         place(2, dv[2], dv_window, item_list, out_0)
-        item_product(3, 6)
+        item_product(3, 4)
         place(3, dv[3], dv_window, item_list, out_0)
         user_product(2, 0)
         place(2, du[2], du_window, user_list, out_1)

@@ -165,16 +165,6 @@ def tile_attend_gmf_bpr_vu_kernel(tc, uT, vT, us, ts, offs, uoffs, out_0, out_1)
             lay_turned(w_i[0][:, t * P : (t + 1) * P, :], turn_plane(w_listed, t, 2 + t))
         nc.vector.tensor_copy(w_listed[:, 2, :], v_plane[2][:].indirect(item_list[:]))
         third_turned = turn_plane(w_listed, 2, 2)
-        for repeat in range(6):
-            nc.tensor.matmul_mx(
-                out=flat(third_turned[:])[:, HALF:],
-                lhsT=x_d_codes[:, 0:P].bitcast(E4M3),
-                lhsT_scale=x_d_scales[:, 0:P],
-                rhs=x_d_codes[:, 0:HALF].bitcast(E4M3),
-                rhs_scale=x_d_scales[:, 0:HALF],
-                start=True,
-                stop=True,
-            )
         for a in range(2):
             nc.vector.tensor_copy(
                 w_listed[:, PACK - 1, a * HALF : (a + 1) * HALF],

@@ -23,6 +23,7 @@ P = 128
 PACK = 4
 HALF = N // 2
 COLS = N // 16
+BLOCK_COLS = P // 16
 
 
 def tile_attend_gmf_bpr_vu_kernel(tc, uT, vT, us, ts, offs, uoffs, out_0, out_1):
@@ -43,6 +44,18 @@ def tile_attend_gmf_bpr_vu_kernel(tc, uT, vT, us, ts, offs, uoffs, out_0, out_1)
         def quantise(codes, scales, values, fmt):
             nc.vector.quantize_mx(out=codes.bitcast(fmt), scales=scales, in_=values.rearrange("p c t -> p (c t)"))
 
+        def flat(ap):
+            return ap.rearrange("p a b -> p (a b)")
+
+        def block(k):
+            return slice(k * P, (k + 1) * P)
+
+        def half(u):
+            return slice(u * HALF, (u + 1) * HALF)
+
+        def groups(k):
+            return slice(k * P // PACK, (k + 1) * P // PACK)
+
         user_list = keep.tile([P, COLS], U16, name="user_list")
         item_list = keep.tile([P, COLS], U16, name="item_list")
         u_plane = [sbuf("u_plane%d" % t, [P, T], F32) for t in range(PACK)]
@@ -60,6 +73,10 @@ def tile_attend_gmf_bpr_vu_kernel(tc, uT, vT, us, ts, offs, uoffs, out_0, out_1)
         for t in range(PACK):
             nc.sync.dma_start(v_plane[t][:], planes(vT)[:, t, :])
 
+        def item_entries(c, a):
+            first = (2 * a + c) * BLOCK_COLS
+            return item_list[:, first : first + BLOCK_COLS]
+
         warm = sbuf("warm", [P, 8], F32)
         nc.gpsimd.memset(warm[:], 0.0)
         nc.scalar.activation(warm[:], warm[:], SIGMOID)
@@ -67,62 +84,43 @@ def tile_attend_gmf_bpr_vu_kernel(tc, uT, vT, us, ts, offs, uoffs, out_0, out_1)
         ident_f32 = sbuf("ident_f32", [P, P], F32)
         make_identity(nc, ident_f32[:])
 
-        def flat(ap):
-            return ap.rearrange("p a b -> p (a b)")
-
-        def turn_pairs(dst, src, u, number):
-            turned = bank(number)
-            for k in range(PACK):
-                words = flat(src[k][:]).bitcast(F32).rearrange("p (m u) -> p u m", u=2)
-                nc.tensor.transpose(turned[:, k, :], words[:, u, :], ident_f32[:])
-            nc.scalar.copy(
-                dst.rearrange("p (e c) k -> p e c k", e=2),
-                flat(turned[:]).bitcast(BF16).rearrange("p (k c e) -> p e c k", k=PACK, e=2),
-            )
-
         dv_window = [sbuf("dv_window%d" % k, [P, T], F32) for k in range(2)]
         du_window = [sbuf("du_window%d" % k, [P, T], F32) for k in range(2)]
         for window in dv_window:
             nc.vector.memset(window[:].bitcast(I32), 0)
-        sign = sbuf("sign", [P, 1], F32)
-        nc.gpsimd.memset(sign[: P // 2, :], -1.0)
-        nc.gpsimd.memset(sign[P // 2 :, :], 1.0)
+        zeros = sbuf("zeros", [P, P], F32)
+        nc.gpsimd.memset(zeros[:], 0.0)
+        h_r_codes = sbuf("h_r_codes", [P, HALF + N], U32)
+        h_r_scales = sbuf("h_r_scales", [P, HALF + N], U8)
+        nc.gpsimd.memset(h_r_codes[:, 0:HALF], 0)
+        nc.gpsimd.memset(h_r_scales[:, 0:HALF].bitcast(I32), 0)
         for window in du_window:
             nc.gpsimd.memset(window[:].bitcast(I32), 0)
 
         ts_listed = sbuf("ts_listed", [P, N], F32)
         nc.vector.tensor_copy(ts_listed[:], ts_row[:].indirect(item_list[:]))
         ts_turned = bank(0)
-        for k in range(PACK):
-            nc.tensor.transpose(ts_turned[:, k, :], ts_listed[:].rearrange("p (m k) -> p k m", k=PACK)[:, k, :], ident_f32[:])
-        ts_column = sbuf("ts_column", [P, PACK], F32)
-        nc.scalar.activation(ts_column[:], ts_turned[:, :, P - 1], COPY, scale=sign[:])
-        ts_paired = sbuf("ts_paired", [P, N], F32)
-        nc.scalar.copy(
-            ts_paired[:].rearrange("p (j m e) -> p j m e", j=2, e=2),
-            ts_listed[:].rearrange("p (m j e) -> p j m e", j=2, e=2),
-        )
-        pair_turned = bank(3)
-        for c in range(PACK):
-            nc.tensor.transpose(pair_turned[:, c, :], ts_paired[:, c * P : (c + 1) * P], ident_f32[:])
-        pair_scale = sbuf("pair_scale", [P, 2, 2], F32)
-        pair_last = pair_turned[:, :, P - 1].rearrange("p (j a) -> p j a", a=2)
-        nc.scalar.activation(pair_scale[:, :, 0], pair_last[:, :, 0], COPY, scale=-1.0)
-        nc.scalar.activation(pair_scale[:, :, 1], pair_last[:, :, 1], COPY)
+        for c in range(2):
+            for a in range(2):
+                nc.tensor.transpose(ts_turned[:, 2 * c + a, :], ts_listed[:, block(2 * a + c)], ident_f32[:])
+        ts_column = sbuf("ts_column", [P, 2, 2], F32)
+        ts_last = ts_turned[:, :, P - 1].rearrange("p (c a) -> p c a", a=2)
+        nc.scalar.activation(ts_column[:, :, 0], ts_last[:, :, 0], COPY, scale=-1.0)
+        nc.scalar.activation(ts_column[:, :, 1], ts_last[:, :, 1], COPY)
         ts_spread = bank(1)
         for k in range(PACK):
-            nc.tensor.transpose(ts_spread[:, k, :], ts_column[:, k : k + 1].to_broadcast([P, P]), ident_f32[:])
-        signed_by_row = sbuf("signed_by_row", [P, PACK, N], F32)
+            nc.tensor.transpose(ts_spread[:, k, :], flat(ts_column[:])[:, k : k + 1].to_broadcast([P, P]), ident_f32[:])
+        signed = sbuf("signed", [P, N // PACK, PACK, PACK], F32)
         for s in range(PACK):
-            nc.scalar.activation(signed_by_row[:, s, :], flat(ts_spread[:]), COPY, scale=row_scale[:, s : s + 1])
-        signed = sbuf("signed", [P, N, PACK], F32)
-        nc.scalar.copy(
-            flat(signed[:]).rearrange("p (c s i) -> p c s i", s=PACK, i=PACK),
-            signed_by_row[:].rearrange("p s (c i) -> p c s i", i=PACK),
-        )
+            nc.scalar.activation(
+                signed[:, :, s, :],
+                flat(ts_spread[:]).rearrange("p (g i) -> p g i", i=PACK),
+                COPY,
+                scale=row_scale[:, s : s + 1],
+            )
 
         def turn_plane(listed, t, number):
-            words = listed[:, t, :].bitcast(F32).rearrange("p (m u) -> p u m", u=2)
+            words = listed[t // 2][:, t % 2, :].bitcast(F32).rearrange("p (m u) -> p u m", u=2)
             turned = bank(number)
             for u in range(2):
                 nc.tensor.transpose(turned[:, u, :], words[:, u, :], ident_f32[:])
@@ -134,171 +132,225 @@ def tile_attend_gmf_bpr_vu_kernel(tc, uT, vT, us, ts, offs, uoffs, out_0, out_1)
                 turned[:, 0:2, :].rearrange("p u c -> p c u"),
             )
 
-        x_listed = sbuf("x_listed", [P, PACK, N], BF16)
+        x_listed = [sbuf("x_listed%d" % u, [P, 2, N], BF16) for u in range(2)]
         x_d = sbuf("x_d", [P, N, PACK], BF16)
         x_r = sbuf("x_r", [P, D, PACK], BF16)
+        x_by_column = x_d[:].rearrange("p (s m) t -> p m s t", s=PACK)
+        x_by_plane = [pair[:].rearrange("p t (m s) -> p m s t", s=PACK) for pair in x_listed]
         for t in range(PACK):
-            nc.vector.tensor_copy(x_listed[:, t, :], u_plane[t][:].indirect(user_list[:]))
-            lay_turned(x_r[:, t * P : (t + 1) * P, :], turn_plane(x_listed, t, PACK + t))
-        nc.vector.tensor_copy(
-            x_d[:].rearrange("p (s m) t -> p m s t", s=PACK),
-            x_listed[:].rearrange("p t (m s) -> p m s t", s=PACK),
-        )
+            nc.vector.tensor_copy(x_listed[t // 2][:, t % 2, :], u_plane[t][:].indirect(user_list[:]))
+            lay_turned(x_r[:, block(t), :], turn_plane(x_listed, t, PACK + t))
+            if t == 1:
+                nc.scalar.copy(x_by_column[:, :, :, 0:2], x_by_plane[0])
+        nc.vector.tensor_copy(x_by_column[:, :, :, 2:PACK], x_by_plane[1])
         x_d_codes = sbuf("x_d_codes", [P, N], U32)
         x_d_scales = sbuf("x_d_scales", [P, N], U8)
         quantise(x_d_codes[:], x_d_scales[:], x_d[:], E4M3)
-        x_r_codes = [sbuf("x_r_codes0", [P, P], U32), sbuf("x_r_codes1", [P, P], U32), sbuf("x_r_codes23", [P, HALF], U32)]
+        x_r_codes = [sbuf("x_r_codes0", [P, HALF], U32, tag="u_plane2"), sbuf("x_r_codes1", [P, HALF], U32, tag="v_plane0")]
         x_r_scales = sbuf("x_r_scales", [P, D], U8)
-        quantise(x_r_codes[0][:], x_r_scales[:, 0:P], x_r[:, 0:P, :], E4M3)
-        quantise(x_r_codes[1][:], x_r_scales[:, P:HALF], x_r[:, P:HALF, :], E4M3)
-        quantise(x_r_codes[2][:], x_r_scales[:, HALF:], x_r[:, HALF:, :], E4M3)
-        x_r_block = [x_r_codes[0][:], x_r_codes[1][:], x_r_codes[2][:, 0:P], x_r_codes[2][:, P:]]
+        quantise(x_r_codes[0][:], x_r_scales[:, half(0)], x_r[:, half(0), :], E4M3)
 
-        w_d = sbuf("w_d", [P, N, PACK], BF16)
-        w_i = [sbuf("w_i0", [P, HALF, PACK], BF16)]
-        w_i_scales = sbuf("w_i_scales", [P, D], U8)
-        w_d_codes = sbuf("w_d_codes", [P, N], U32)
+        shared = sbuf("w_shared", [P, 2 * N + HALF], BF16)
+        w_low = sbuf("w_low", [P, 2, N], BF16)
+        w_listed = [w_low[:], shared[:, 0 : 2 * N].rearrange("p (t n) -> p t n", t=2)]
+        w_rest = sbuf("w_rest", [P, PACK - 1, P, PACK], BF16)
+        w_d = [w_rest[:, 0], shared[:, N + HALF :].rearrange("p (c t) -> p c t", t=PACK), w_rest[:, 1], w_rest[:, 2]]
         w_d_scales = sbuf("w_d_scales", [P, N], U8)
-        w_listed = sbuf("w_listed", [P, PACK, N], BF16)
-        for t in range(2):
-            nc.vector.tensor_copy(w_listed[:, t, :], v_plane[t][:].indirect(item_list[:]))
-            lay_turned(w_i[0][:, t * P : (t + 1) * P, :], turn_plane(w_listed, t, 2 + t))
-        nc.vector.tensor_copy(w_listed[:, 2, :], v_plane[2][:].indirect(item_list[:]))
-        third_turned = turn_plane(w_listed, 2, 2)
-        for a in range(2):
+        w_i = sbuf("w_i", [P, D, PACK], BF16)
+        w_i_scales = sbuf("w_i_scales", [P, D], U8)
+        w_i_early = sbuf("w_i_early", [P, HALF], U32, tag="v_plane2")
+        w_by_column = [columns.rearrange("p (g i) t -> p g t i", i=PACK) for columns in w_d]
+        w_by_plane = [pair.rearrange("p t (g i) -> p g t i", i=PACK) for pair in w_listed]
+        for t in range(PACK - 1):
             nc.vector.tensor_copy(
-                w_listed[:, PACK - 1, a * HALF : (a + 1) * HALF],
-                v_plane[PACK - 1][:].indirect(item_list[:, a * COLS // 2 : (a + 1) * COLS // 2]),
+                w_listed[t // 2][:, t % 2, :].rearrange("p (c a m) -> p a c m", c=2, a=2),
+                v_plane[t][:].indirect(item_list[:]),
             )
-        w_by_tile = w_d[:].rearrange("p (j a c n e) t -> p j a c t n e", j=2, a=2, n=2, e=2)
-        w_by_plane = w_listed[:].rearrange("p t (a c n j e) -> p j a c t n e", a=2, n=2, j=2, e=2)
-        for a in range(2):
-            nc.vector.tensor_copy(w_by_tile[:, 0, a], w_by_plane[:, 0, a])
-            nc.scalar.copy(w_by_tile[:, 1, a], w_by_plane[:, 1, a])
+            lay_turned(w_i[:, block(t), :], turn_plane(w_listed, t, 2 + t % 2))
+            if t == 0:
+                quantise(x_r_codes[1][:], x_r_scales[:, half(1)], x_r[:, half(1), :], E4M3)
+            if t == 1:
+                for k in (1, 0, 3, 2):
+                    nc.scalar.copy(w_by_column[k][:, :, 0:2, :], w_by_plane[0][:, groups(k)])
+        quantise(w_i_early[:], w_i_scales[:, half(0)], w_i[:, half(0), :], E4M3)
 
-        negative = sbuf("negative", [P, 2, N], F32)
-        margin = sbuf("margin", [P, 2, N], F32)
-        q = [sbuf("q%d" % j, [P, 2, HALF], F32) for j in range(2)]
-        h_r = [sbuf("h_r%d" % k, [P, P, PACK], BF16) for k in range(PACK)]
-        h_r_codes = sbuf("h_r_codes", [P, N], U32)
-        h_r_scales = sbuf("h_r_scales", [P, N], U8)
+        w_d_codes = {}
+        margin = sbuf("margin", [P, 1, N], F32)
+        q = [sbuf("q%d" % c, [P, P // PACK, PACK, PACK], F32) for c in range(2)]
+        h_r = sbuf("h_r", [P, N, PACK], BF16)
 
-        def block(k):
-            return slice(k * P, (k + 1) * P)
+        def finish_items(c):
+            for a in (1, 0):
+                nc.vector.tensor_copy(w_listed[1][:, 1, block(2 * c + a)], v_plane[PACK - 1][:].indirect(item_entries(c, a)))
+            for k in (2 * c + 1, 2 * c):
+                nc.vector.tensor_copy(w_by_column[k][:, :, 2:PACK, :], w_by_plane[1][:, groups(k)])
 
-        def half(u):
-            return slice(u * HALF, (u + 1) * HALF)
+        def quantise_items(k, tag=""):
+            w_d_codes[k] = sbuf("w_d_codes%d" % k, [P, P], U32, tag=tag)
+            quantise(w_d_codes[k][:], w_d_scales[:, block(k)], w_d[k], E4M3)
 
-        def subtract(j, u):
-            scores = flat(bank(PACK + 2 * j + u)[:])
-            for a in range(2):
-                nc.tensor.matmul_mx(
-                    out=scores[:, half(a)],
-                    lhsT=w_d_codes[:, block(2 * j + a)].bitcast(E4M3),
-                    lhsT_scale=w_d_scales[:, block(2 * j + a)],
-                    rhs=x_d_codes[:, half(u)].bitcast(E4M3),
-                    rhs_scale=x_d_scales[:, half(u)],
-                    start=True,
-                    stop=True,
-                )
-            nc.scalar.activation(negative[:, j, half(u)], scores[:, half(1)], COPY, scale=pair_scale[:, j, 1:2])
+        def score_bank(c, u, a):
+            return PACK * (1 - c) + 2 * u + 1 - a
+
+        def score(c, u, a):
+            scores = flat(bank(score_bank(c, u, a))[:])[:, 0:HALF]
+            nc.tensor.matmul_mx(
+                out=scores,
+                lhsT=w_d_codes[2 * c + a][:].bitcast(E4M3),
+                lhsT_scale=w_d_scales[:, block(2 * c + a)],
+                rhs=x_d_codes[:, half(u)].bitcast(E4M3),
+                rhs_scale=x_d_scales[:, half(u)],
+                start=True,
+                stop=True,
+            )
+            return scores
+
+        def subtract(c, u):
+            negative = sbuf("negative%d" % (2 * c + u), [P, HALF], F32)
+            nc.scalar.activation(negative[:], score(c, u, 1), COPY, scale=ts_column[:, c, 1:2])
             nc.vector.scalar_tensor_tensor(
-                margin[:, j, half(u)], scores[:, half(0)], pair_scale[:, j, 0:1], negative[:, j, half(u)], MULT, ADD
+                margin[:, c, half(u)], score(c, u, 0), ts_column[:, c, 0:1], negative[:], MULT, ADD
             )
 
-        def weigh(j, u):
-            turned = bank(PACK + 2 * j + u)
+        def weigh(c, u):
+            turned = bank(score_bank(c, u, 1))
             for e in range(2):
-                nc.tensor.transpose(turned[:, e, :], margin[:, j, block(2 * u + e)], ident_f32[:])
+                nc.tensor.transpose(turned[:, e, :], margin[:, c, block(2 * u + e)], ident_f32[:])
             for e in range(2):
                 s = 2 * u + e
                 nc.scalar.activation(
-                    q[j][:].rearrange("p e (c s i) -> p s e c i", s=PACK, i=PACK)[:, s],
-                    turned[:, e, :].rearrange("p (c i e) -> p e c i", i=PACK, e=2),
+                    q[c][:, :, s, :],
+                    turned[:, e, :].rearrange("p (g i) -> p g i", i=PACK),
                     SIGMOID,
                     scale=row_scale[:, s : s + 1],
                 )
 
-        def gradient(k):
-            j, e = divmod(k, 2)
-            nc.vector.tensor_tensor(
-                h_r[k][:].rearrange("p (a c i) s -> p a c s i", a=2, i=PACK),
-                q[j][:, e : e + 1, :].rearrange("p a (c s i) -> p a c s i", s=PACK, i=PACK).to_broadcast([P, 2, 16, PACK, PACK]),
-                flat(signed[:, block(k), :]).rearrange("p (a c s i) -> p a c s i", a=2, s=PACK, i=PACK),
-                MULT,
-            )
+        def weigh_summed(c, u):
+            scaled = []
+            for a in (1, 0):
+                part = sbuf("scaled%d" % (2 * u + a), [P, HALF], F32)
+                nc.scalar.activation(part[:], score(c, u, a), COPY, scale=ts_column[:, c, a : a + 1])
+                scaled.append(part)
+            turned = bank(score_bank(c, u, 1))
+            for e in range(2):
+                for k in range(2):
+                    nc.tensor.matmul(
+                        turned[:, e, :], scaled[k][:, block(e)], ident_f32[:], start=k == 0, stop=k == 1, is_transpose=True
+                    )
+            return turned
 
-        def quantise_h(k):
-            quantise(h_r_codes[:, block(k)], h_r_scales[:, block(k)], h_r[k][:], E5M2)
+        def sigmoids(c, u, turned):
+            for e in range(2):
+                s = 2 * u + e
+                nc.scalar.activation(
+                    q[c][:, :, s, :],
+                    turned[:, e, :].rearrange("p (g i) -> p g i", i=PACK),
+                    SIGMOID,
+                    scale=row_scale[:, s : s + 1],
+                )
 
-        for c in range(PACK):
-            quantise(w_d_codes[:, block(c)], w_d_scales[:, block(c)], w_d[:, block(c), :], E4M3)
-        for j in range(2):
-            for u in range(2):
-                subtract(j, u)
-        for j in range(2):
-            for u in range(2):
-                weigh(j, u)
-        w_i.append(sbuf("w_i1", [P, HALF, PACK], BF16, tag="margin"))
-        lay_turned(w_i[1][:, 0:P, :], third_turned)
-        lay_turned(w_i[1][:, P:, :], turn_plane(w_listed, PACK - 1, 7))
-        gradient(0)
-        for k in range(1, PACK):
-            gradient(k)
-            quantise_h(k - 1)
-        quantise_h(PACK - 1)
+        def gradient(c):
+            for k in (2 * c, 2 * c + 1):
+                nc.vector.tensor_tensor(
+                    h_r[:, block(k), :].rearrange("p (g i) s -> p g s i", i=PACK), q[c][:], signed[:, groups(k)], MULT
+                )
+            for k in (2 * c, 2 * c + 1):
+                columns = slice(HALF + k * P, HALF + (k + 1) * P)
+                quantise(h_r_codes[:, columns], h_r_scales[:, columns], h_r[:, block(k), :], E5M2)
 
-        dv = [sbuf("dv%d" % t, [P, N], F32) for t in range(PACK)]
-        du = [sbuf("du%d" % t, [P, N], F32) for t in range(PACK)]
-
-        def product(dst, number, codes, scales, h_codes, h_scales, copy):
+        def product(number, codes, scales, h_codes, h_scales):
             sums = bank(number)
             nc.tensor.matmul_mx(
                 out=flat(sums[:]),
                 lhsT=codes.bitcast(E4M3),
                 lhsT_scale=scales,
-                rhs=h_codes[:].bitcast(E5M2),
-                rhs_scale=h_scales[:],
+                rhs=h_codes.bitcast(E5M2),
+                rhs_scale=h_scales,
                 start=True,
                 stop=True,
             )
-            copy(dst[:].rearrange("p (m s) -> p m s", s=PACK), sums[:].rearrange("p s m -> p m s"))
+            return sums
+
+        def item_product(t, number, first=HALF):
+            columns = slice(first, first + N)
+            return product(number, x_r_codes[t // 2][:, block(t % 2)], x_r_scales[:, block(t)], h_r_codes[:, columns], h_r_scales[:, columns])
+
+        def place_block(t, c, a, values):
+            nc.vector.tensor_tensor(dv_window[t][:].indirect(item_entries(c, a)), values, zeros[:], ADD)
 
         def place(t, values, windows, entries, out):
             window = windows[t % len(windows)]
             nc.vector.tensor_copy(window[:].indirect(entries[:]), values[:])
             nc.sync.dma_start(planes(out)[:, t, :], window[:])
 
+        def item_plane(t, number):
+            values = sbuf("dv%d" % t, [P, N], F32)
+            nc.scalar.copy(
+                values[:].rearrange("p (a c m) -> p c a m", a=2, c=2),
+                item_product(t, number)[:].rearrange("p (c a) m -> p c a m", a=2),
+            )
+            place(t, values, dv_window, item_list, out_0)
+
+        h_i = sbuf("h_i", [P, N, PACK], BF16)
         h_i_codes = sbuf("h_i_codes", [P, N], U32)
         h_i_scales = sbuf("h_i_scales", [P, N], U8)
+        w_i_late = sbuf("w_i_late", [P, HALF], U32)
+        w_i_codes = [w_i_early[:, 0:P], w_i_early[:, P:], w_i_late[:, 0:P], w_i_late[:, P:]]
 
-        def item_product(t, number, copy=nc.scalar.copy):
-            product(dv[t], number, x_r_block[t], x_r_scales[:, block(t)], h_r_codes, h_r_scales, copy)
+        def user_plane(t, number):
+            values = sbuf("du%d" % t, [P, N], F32)
+            sums = product(number, w_i_codes[t], w_i_scales[:, block(t)], h_i_codes[:], h_i_scales[:])
+            nc.scalar.copy(values[:].rearrange("p (m s) -> p m s", s=PACK), sums[:].rearrange("p s m -> p m s"))
+            place(t, values, du_window, user_list, out_1)
 
-        def user_product(t, number):
-            product(du[t], number, w_i_codes[:, block(t)], w_i_scales[:, block(t)], h_i_codes, h_i_scales, nc.scalar.copy)
+        def turn_pairs(u, number):
+            turned = bank(number)
+            words = flat(h_r[:]).bitcast(F32).rearrange("p (m k u) -> p k u m", k=PACK, u=2)
+            for k in range(PACK):
+                nc.tensor.transpose(turned[:, k, :], words[:, k, u, :], ident_f32[:])
+            nc.scalar.copy(
+                h_i[:, half(u), :].rearrange("p (e c) k -> p e c k", e=2),
+                flat(turned[:]).bitcast(BF16).rearrange("p (k c e) -> p e c k", k=PACK, e=2),
+            )
 
+        def late_blocks(t, number):
+            values = sbuf("late%d" % t, [P, 2, P], F32)
+            nc.scalar.copy(values[:], item_product(t, number)[:, 2:PACK, :])
+            for a in range(2):
+                place_block(t, 1, a, values[:, a, :])
+            nc.sync.dma_start(planes(out_0)[:, t, :], dv_window[t][:])
 
-        item_product(0, 0)
-        place(0, dv[0], dv_window, item_list, out_0)
-        h_i = sbuf("h_i", [P, N, PACK], BF16, tag="x_r_codes0")
+        finish_items(0)
+        quantise_items(1)
+        quantise_items(0)
         for u in range(2):
-            turn_pairs(h_i[:, u * HALF : (u + 1) * HALF, :], h_r, u, 1 + u)
-        w_i_codes = sbuf("w_i_codes", [P, D], U32, tag="h_r%d" % (PACK - 1))
+            subtract(0, u)
         for u in range(2):
-            quantise(w_i_codes[:, half(u)], w_i_scales[:, half(u)], w_i[u][:], E4M3)
+            weigh(0, u)
+        finish_items(1)
+        quantise_items(3, tag="negative0")
+        quantise_items(2, tag="negative1")
+        gradient(0)
+        summed = [weigh_summed(1, u) for u in range(2)]
+        for u in range(2):
+            sigmoids(1, u, summed[u])
+        early = [item_product(t, 5 + 2 * t, first=0) for t in range(2)]
+        gradient(1)
+        for t in range(2):
+            values = sbuf("early%d" % t, [P, 2, P], F32, tag="q1" if t == 0 else "")
+            nc.scalar.copy(values[:], early[t][:, 2:PACK, :])
+            for a in range(2):
+                place_block(t, 0, a, values[:, a, :])
+        late_blocks(0, 1)
+        turn_pairs(0, 4)
+        turn_pairs(1, 6)
         quantise(h_i_codes[:], h_i_scales[:], h_i[:], E5M2)
-        item_product(1, 2)
-        place(1, dv[1], dv_window, item_list, out_0)
-        user_product(0, 4)
-        place(0, du[0], du_window, user_list, out_1)
-        user_product(1, 3)
-        place(1, du[1], du_window, user_list, out_1)
-        item_product(2, 2)
-        place(2, dv[2], dv_window, item_list, out_0)
-        item_product(3, 4)
-        place(3, dv[3], dv_window, item_list, out_0)
-        user_product(2, 0)
-        place(2, du[2], du_window, user_list, out_1)
-        user_product(3, 1)
-        place(3, du[3], du_window, user_list, out_1)
+        late_blocks(1, 6)
+        user_plane(0, 5)
+        user_plane(1, 7)
+        lay_turned(w_i[:, block(PACK - 1), :], turn_plane(w_listed, PACK - 1, 7))
+        quantise(w_i_late[:], w_i_scales[:, half(1)], w_i[:, half(1), :], E4M3)
+        item_plane(2, 5)
+        item_plane(3, 5)
+        user_plane(2, 3)
+        user_plane(3, 1)

@@ -24,6 +24,7 @@ PACK = 4
 HALF = N // 2
 COLS = N // 16
 BLOCK_COLS = P // 16
+PAD = N - P
 
 
 def tile_attend_gmf_bpr_vu_kernel(tc, uT, vT, us, ts, offs, uoffs, out_0, out_1):
@@ -86,15 +87,13 @@ def tile_attend_gmf_bpr_vu_kernel(tc, uT, vT, us, ts, offs, uoffs, out_0, out_1)
 
         dv_window = [sbuf("dv_window%d" % k, [P, T], F32) for k in range(2)]
         du_window = [sbuf("du_window%d" % k, [P, T], F32) for k in range(2)]
-        for window in dv_window:
-            nc.vector.memset(window[:].bitcast(I32), 0)
         zeros = sbuf("zeros", [P, P], F32)
         nc.gpsimd.memset(zeros[:], 0.0)
-        h_r_codes = sbuf("h_r_codes", [P, HALF + N], U32)
-        h_r_scales = sbuf("h_r_scales", [P, HALF + N], U8)
-        nc.gpsimd.memset(h_r_codes[:, 0:HALF], 0)
-        nc.gpsimd.memset(h_r_scales[:, 0:HALF].bitcast(I32), 0)
-        for window in du_window:
+        h_r_codes = sbuf("h_r_codes", [P, PAD + N], U32)
+        h_r_scales = sbuf("h_r_scales", [P, PAD + N], U8)
+        nc.gpsimd.memset(h_r_codes[:, 0:PAD], 0)
+        nc.gpsimd.memset(h_r_scales[:, 0:PAD].bitcast(I32), 0)
+        for window in dv_window + du_window:
             nc.gpsimd.memset(window[:].bitcast(I32), 0)
 
         ts_listed = sbuf("ts_listed", [P, N], F32)
@@ -146,7 +145,7 @@ def tile_attend_gmf_bpr_vu_kernel(tc, uT, vT, us, ts, offs, uoffs, out_0, out_1)
         x_d_codes = sbuf("x_d_codes", [P, N], U32)
         x_d_scales = sbuf("x_d_scales", [P, N], U8)
         quantise(x_d_codes[:], x_d_scales[:], x_d[:], E4M3)
-        x_r_codes = [sbuf("x_r_codes0", [P, HALF], U32, tag="u_plane2"), sbuf("x_r_codes1", [P, HALF], U32, tag="v_plane0")]
+        x_r_codes = [sbuf("x_r_codes0", [P, HALF], U32, tag="u_plane3"), sbuf("x_r_codes1", [P, HALF], U32, tag="v_plane0")]
         x_r_scales = sbuf("x_r_scales", [P, D], U8)
         quantise(x_r_codes[0][:], x_r_scales[:, half(0)], x_r[:, half(0), :], E4M3)
 
@@ -255,7 +254,8 @@ def tile_attend_gmf_bpr_vu_kernel(tc, uT, vT, us, ts, offs, uoffs, out_0, out_1)
                     h_r[:, block(k), :].rearrange("p (g i) s -> p g s i", i=PACK), q[c][:], signed[:, groups(k)], MULT
                 )
             for k in (2 * c, 2 * c + 1):
-                columns = slice(HALF + k * P, HALF + (k + 1) * P)
+                first = PAD + (2 * (k % 2) + c) * P
+                columns = slice(first, first + P)
                 quantise(h_r_codes[:, columns], h_r_scales[:, columns], h_r[:, block(k), :], E5M2)
 
         def product(number, codes, scales, h_codes, h_scales):
@@ -271,12 +271,14 @@ def tile_attend_gmf_bpr_vu_kernel(tc, uT, vT, us, ts, offs, uoffs, out_0, out_1)
             )
             return sums
 
-        def item_product(t, number, first=HALF):
+        def item_product(t, number, first=PAD):
             columns = slice(first, first + N)
             return product(number, x_r_codes[t // 2][:, block(t % 2)], x_r_scales[:, block(t)], h_r_codes[:, columns], h_r_scales[:, columns])
 
-        def place_block(t, c, a, values):
-            nc.vector.tensor_tensor(dv_window[t][:].indirect(item_entries(c, a)), values, zeros[:], ADD)
+        def early_block(t, number, tag=""):
+            values = sbuf("early%d" % t, [P, P], F32, tag=tag)
+            nc.scalar.copy(values[:], item_product(t, number, first=0)[:, PACK - 1, :])
+            nc.vector.tensor_tensor(dv_window[t][:].indirect(item_entries(0, 0)), values[:], zeros[:], ADD)
 
         def place(t, values, windows, entries, out):
             window = windows[t % len(windows)]
@@ -285,10 +287,7 @@ def tile_attend_gmf_bpr_vu_kernel(tc, uT, vT, us, ts, offs, uoffs, out_0, out_1)
 
         def item_plane(t, number):
             values = sbuf("dv%d" % t, [P, N], F32)
-            nc.scalar.copy(
-                values[:].rearrange("p (a c m) -> p c a m", a=2, c=2),
-                item_product(t, number)[:].rearrange("p (c a) m -> p c a m", a=2),
-            )
+            nc.scalar.copy(values[:], flat(item_product(t, number)[:]))
             place(t, values, dv_window, item_list, out_0)
 
         h_i = sbuf("h_i", [P, N, PACK], BF16)
@@ -314,10 +313,9 @@ def tile_attend_gmf_bpr_vu_kernel(tc, uT, vT, us, ts, offs, uoffs, out_0, out_1)
             )
 
         def late_blocks(t, number):
-            values = sbuf("late%d" % t, [P, 2, P], F32)
-            nc.scalar.copy(values[:], item_product(t, number)[:, 2:PACK, :])
-            for a in range(2):
-                place_block(t, 1, a, values[:, a, :])
+            values = sbuf("late%d" % t, [P, PACK - 1, P], F32)
+            nc.scalar.copy(values[:], item_product(t, number)[:, 1:PACK, :])
+            nc.vector.tensor_copy(dv_window[t][:].indirect(item_list[:, BLOCK_COLS:]), flat(values[:]))
             nc.sync.dma_start(planes(out_0)[:, t, :], dv_window[t][:])
 
         finish_items(0)
@@ -334,13 +332,11 @@ def tile_attend_gmf_bpr_vu_kernel(tc, uT, vT, us, ts, offs, uoffs, out_0, out_1)
         summed = [weigh_summed(1, u) for u in range(2)]
         for u in range(2):
             sigmoids(1, u, summed[u])
-        early = [item_product(t, 5 + 2 * t, first=0) for t in range(2)]
+        early_block(0, 5)
         gradient(1)
-        for t in range(2):
-            values = sbuf("early%d" % t, [P, 2, P], F32, tag="q1" if t == 0 else "")
-            nc.scalar.copy(values[:], early[t][:, 2:PACK, :])
-            for a in range(2):
-                place_block(t, 0, a, values[:, a, :])
+        lay_turned(w_i[:, block(PACK - 1), :], turn_plane(w_listed, PACK - 1, score_bank(1, 1, 1)))
+        quantise(w_i_late[:], w_i_scales[:, half(1)], w_i[:, half(1), :], E4M3)
+        early_block(1, 7, tag="q1")
         late_blocks(0, 1)
         turn_pairs(0, 4)
         turn_pairs(1, 6)
@@ -348,8 +344,6 @@ def tile_attend_gmf_bpr_vu_kernel(tc, uT, vT, us, ts, offs, uoffs, out_0, out_1)
         late_blocks(1, 6)
         user_plane(0, 5)
         user_plane(1, 7)
-        lay_turned(w_i[:, block(PACK - 1), :], turn_plane(w_listed, PACK - 1, 7))
-        quantise(w_i_late[:], w_i_scales[:, half(1)], w_i[:, half(1), :], E4M3)
         item_plane(2, 5)
         item_plane(3, 5)
         user_plane(2, 3)

@@ -131,20 +131,19 @@ def tile_attend_gmf_bpr_vu_kernel(tc, uT, vT, us, ts, offs, uoffs, out_0, out_1)
                 turned[:, 0:2, :].rearrange("p u c -> p c u"),
             )
 
-        x_listed = [sbuf("x_listed%d" % u, [P, 2, N], BF16) for u in range(2)]
+        x_planes = sbuf("x_planes", [P, PACK, N], BF16)
+        x_listed = [x_planes[:, 0:2, :], x_planes[:, 2:PACK, :]]
         x_d = sbuf("x_d", [P, N, PACK], BF16)
         x_r = sbuf("x_r", [P, D, PACK], BF16)
         x_by_column = x_d[:].rearrange("p (s m) t -> p m s t", s=PACK)
-        x_by_plane = [pair[:].rearrange("p t (m s) -> p m s t", s=PACK) for pair in x_listed]
         for t in range(PACK):
             nc.vector.tensor_copy(x_listed[t // 2][:, t % 2, :], u_plane[t][:].indirect(user_list[:]))
             lay_turned(x_r[:, block(t), :], turn_plane(x_listed, t, PACK + t))
-            if t == 1:
-                nc.scalar.copy(x_by_column[:, :, :, 0:2], x_by_plane[0])
-        nc.vector.tensor_copy(x_by_column[:, :, :, 2:PACK], x_by_plane[1])
-        x_d_codes = sbuf("x_d_codes", [P, N], U32)
+        x_by_plane = x_planes[:].rearrange("p t (m s) -> p m s t", s=PACK)
+        for k in range(PACK):
+            nc.scalar.copy(x_by_column[:, groups(k)], x_by_plane[:, groups(k)])
+        x_d_codes = sbuf("x_d_codes", [P, N], U32, tag="v_plane1")
         x_d_scales = sbuf("x_d_scales", [P, N], U8)
-        quantise(x_d_codes[:], x_d_scales[:], x_d[:], E4M3)
         x_r_codes = [sbuf("x_r_codes0", [P, HALF], U32, tag="u_plane3"), sbuf("x_r_codes1", [P, HALF], U32, tag="v_plane0")]
         x_r_scales = sbuf("x_r_scales", [P, D], U8)
         quantise(x_r_codes[0][:], x_r_scales[:, half(0)], x_r[:, half(0), :], E4M3)
@@ -169,12 +168,13 @@ def tile_attend_gmf_bpr_vu_kernel(tc, uT, vT, us, ts, offs, uoffs, out_0, out_1)
             if t == 0:
                 quantise(x_r_codes[1][:], x_r_scales[:, half(1)], x_r[:, half(1), :], E4M3)
             if t == 1:
+                quantise(x_d_codes[:], x_d_scales[:], x_d[:], E4M3)
                 for k in (1, 0, 3, 2):
                     nc.scalar.copy(w_by_column[k][:, :, 0:2, :], w_by_plane[0][:, groups(k)])
         quantise(w_i_early[:], w_i_scales[:, half(0)], w_i[:, half(0), :], E4M3)
 
         w_d_codes = {}
-        margin = sbuf("margin", [P, 1, N], F32)
+        margin = sbuf("margin", [P, 2, N], F32)
         q = [sbuf("q%d" % c, [P, P // PACK, PACK, PACK], F32) for c in range(2)]
         h_r = sbuf("h_r", [P, N, PACK], BF16)
 
@@ -215,30 +215,6 @@ def tile_attend_gmf_bpr_vu_kernel(tc, uT, vT, us, ts, offs, uoffs, out_0, out_1)
             turned = bank(score_bank(c, u, 1))
             for e in range(2):
                 nc.tensor.transpose(turned[:, e, :], margin[:, c, block(2 * u + e)], ident_f32[:])
-            for e in range(2):
-                s = 2 * u + e
-                nc.scalar.activation(
-                    q[c][:, :, s, :],
-                    turned[:, e, :].rearrange("p (g i) -> p g i", i=PACK),
-                    SIGMOID,
-                    scale=row_scale[:, s : s + 1],
-                )
-
-        def weigh_summed(c, u):
-            scaled = []
-            for a in (1, 0):
-                part = sbuf("scaled%d" % (2 * u + a), [P, HALF], F32)
-                nc.scalar.activation(part[:], score(c, u, a), COPY, scale=ts_column[:, c, a : a + 1])
-                scaled.append(part)
-            turned = bank(score_bank(c, u, 1))
-            for e in range(2):
-                for k in range(2):
-                    nc.tensor.matmul(
-                        turned[:, e, :], scaled[k][:, block(e)], ident_f32[:], start=k == 0, stop=k == 1, is_transpose=True
-                    )
-            return turned
-
-        def sigmoids(c, u, turned):
             for e in range(2):
                 s = 2 * u + e
                 nc.scalar.activation(
@@ -326,12 +302,13 @@ def tile_attend_gmf_bpr_vu_kernel(tc, uT, vT, us, ts, offs, uoffs, out_0, out_1)
         for u in range(2):
             weigh(0, u)
         finish_items(1)
-        quantise_items(3, tag="negative0")
-        quantise_items(2, tag="negative1")
-        gradient(0)
-        summed = [weigh_summed(1, u) for u in range(2)]
+        quantise_items(3)
+        quantise_items(2)
         for u in range(2):
-            sigmoids(1, u, summed[u])
+            subtract(1, u)
+        gradient(0)
+        for u in range(2):
+            weigh(1, u)
         early_block(0, 5)
         gradient(1)
         lay_turned(w_i[:, block(PACK - 1), :], turn_plane(w_listed, PACK - 1, score_bank(1, 1, 1)))

@@ -85,7 +85,7 @@ def tile_attend_gmf_bpr_vu_kernel(tc, uT, vT, us, ts, offs, uoffs, out_0, out_1)
         ident_f32 = sbuf("ident_f32", [P, P], F32)
         make_identity(nc, ident_f32[:])
 
-        dv_window = [sbuf("dv_window%d" % k, [P, T], F32) for k in range(2)]
+        dv_window = [sbuf("dv_window%d" % k, [P, T], F32) for k in range(PACK - 1)]
         du_window = [sbuf("du_window%d" % k, [P, T], F32) for k in range(2)]
         zeros = sbuf("zeros", [P, P], F32)
         nc.gpsimd.memset(zeros[:], 0.0)
@@ -144,9 +144,8 @@ def tile_attend_gmf_bpr_vu_kernel(tc, uT, vT, us, ts, offs, uoffs, out_0, out_1)
             nc.scalar.copy(x_by_column[:, groups(k)], x_by_plane[:, groups(k)])
         x_d_codes = sbuf("x_d_codes", [P, N], U32, tag="v_plane1")
         x_d_scales = sbuf("x_d_scales", [P, N], U8)
-        x_r_codes = [sbuf("x_r_codes0", [P, HALF], U32, tag="u_plane3"), sbuf("x_r_codes1", [P, HALF], U32, tag="v_plane0")]
+        x_r_codes = sbuf("x_r_codes", [P, D], U32, tag="v_plane0")
         x_r_scales = sbuf("x_r_scales", [P, D], U8)
-        quantise(x_r_codes[0][:], x_r_scales[:, half(0)], x_r[:, half(0), :], E4M3)
 
         shared = sbuf("w_shared", [P, 2 * N + HALF], BF16)
         w_low = sbuf("w_low", [P, 2, N], BF16)
@@ -166,7 +165,7 @@ def tile_attend_gmf_bpr_vu_kernel(tc, uT, vT, us, ts, offs, uoffs, out_0, out_1)
             )
             lay_turned(w_i[:, block(t), :], turn_plane(w_listed, t, 2 + t % 2))
             if t == 0:
-                quantise(x_r_codes[1][:], x_r_scales[:, half(1)], x_r[:, half(1), :], E4M3)
+                quantise(x_r_codes[:], x_r_scales[:], x_r[:], E4M3)
             if t == 1:
                 quantise(x_d_codes[:], x_d_scales[:], x_d[:], E4M3)
                 for k in (1, 0, 3, 2):
@@ -249,7 +248,7 @@ def tile_attend_gmf_bpr_vu_kernel(tc, uT, vT, us, ts, offs, uoffs, out_0, out_1)
 
         def item_product(t, number, first=PAD):
             columns = slice(first, first + N)
-            return product(number, x_r_codes[t // 2][:, block(t % 2)], x_r_scales[:, block(t)], h_r_codes[:, columns], h_r_scales[:, columns])
+            return product(number, x_r_codes[:, block(t)], x_r_scales[:, block(t)], h_r_codes[:, columns], h_r_scales[:, columns])
 
         def early_block(t, number, tag=""):
             values = sbuf("early%d" % t, [P, P], F32, tag=tag)
@@ -314,14 +313,15 @@ def tile_attend_gmf_bpr_vu_kernel(tc, uT, vT, us, ts, offs, uoffs, out_0, out_1)
         lay_turned(w_i[:, block(PACK - 1), :], turn_plane(w_listed, PACK - 1, score_bank(1, 1, 1)))
         quantise(w_i_late[:], w_i_scales[:, half(1)], w_i[:, half(1), :], E4M3)
         early_block(1, 7, tag="q1")
+        early_block(2, 7)
         late_blocks(0, 1)
+        late_blocks(1, 3)
         turn_pairs(0, 4)
         turn_pairs(1, 6)
         quantise(h_i_codes[:], h_i_scales[:], h_i[:], E5M2)
-        late_blocks(1, 6)
+        late_blocks(2, 6)
         user_plane(0, 5)
         user_plane(1, 7)
-        item_plane(2, 5)
         item_plane(3, 5)
         user_plane(2, 3)
         user_plane(3, 1)

@@ -34,7 +34,7 @@ def tile_attend_gmf_bpr_vu_kernel(tc, uT, vT, us, ts, offs, uoffs, out_0, out_1)
         psum = ctx.enter_context(tc.psum_pool(name="psum", bufs=1))
 
         def sbuf(name, shape, dtype, tag=""):
-            return keep.tile(shape, dtype, name=name, tag=tag or name, align_bytes=64)
+            return keep.tile(shape, dtype, name=name, tag=tag or name, align_bytes=256)
 
         def bank(number):
             return psum.tile([P, PACK, P], F32, name="bank%d" % number)
@@ -68,7 +68,7 @@ def tile_attend_gmf_bpr_vu_kernel(tc, uT, vT, us, ts, offs, uoffs, out_0, out_1)
         row_scale = sbuf("row_scale", [P, PACK], F32)
         nc.scalar.dma_start(ts_row[P - 1 : P, :], ts[0:1, :])
         nc.scalar.dma_start(row_scale[:], us.rearrange("b (p t) o -> p (b t o)", t=PACK))
-        nc.gpsimd.memset(ts_row[0 : P - 1, :].bitcast(I32), 0)
+        nc.vector.memset(ts_row[0 : P - 1, :].bitcast(I32), 0)
         for t in range(1, PACK):
             nc.sync.dma_start(u_plane[t][:], planes(uT)[:, t, :])
         for t in range(PACK):
@@ -85,15 +85,16 @@ def tile_attend_gmf_bpr_vu_kernel(tc, uT, vT, us, ts, offs, uoffs, out_0, out_1)
         ident_f32 = sbuf("ident_f32", [P, P], F32)
         make_identity(nc, ident_f32[:])
 
-        dv_window = [sbuf("dv_window%d" % k, [P, T], F32) for k in range(PACK - 1)]
-        du_window = [sbuf("du_window%d" % k, [P, T], F32) for k in range(2)]
+        dv_window = [sbuf("dv_window%d" % k, [P, T], F32) for k in range(PACK)]
+        du_window = [sbuf("du_window%d" % k, [P, T], F32) for k in range(PACK - 1)]
         zeros = sbuf("zeros", [P, P], F32)
         nc.gpsimd.memset(zeros[:], 0.0)
         h_r_codes = sbuf("h_r_codes", [P, PAD + N], U32)
         h_r_scales = sbuf("h_r_scales", [P, PAD + N], U8)
         nc.gpsimd.memset(h_r_codes[:, 0:PAD], 0)
         nc.gpsimd.memset(h_r_scales[:, 0:PAD].bitcast(I32), 0)
-        for window in dv_window + du_window:
+        nc.vector.memset(dv_window[0][:].bitcast(I32), 0)
+        for window in dv_window[1:] + du_window:
             nc.gpsimd.memset(window[:].bitcast(I32), 0)
 
         ts_listed = sbuf("ts_listed", [P, N], F32)
@@ -268,8 +269,12 @@ def tile_attend_gmf_bpr_vu_kernel(tc, uT, vT, us, ts, offs, uoffs, out_0, out_1)
         h_i = sbuf("h_i", [P, N, PACK], BF16)
         h_i_codes = sbuf("h_i_codes", [P, N], U32)
         h_i_scales = sbuf("h_i_scales", [P, N], U8)
-        w_i_late = sbuf("w_i_late", [P, HALF], U32)
-        w_i_codes = [w_i_early[:, 0:P], w_i_early[:, P:], w_i_late[:, 0:P], w_i_late[:, P:]]
+        w_i_codes = [w_i_early[:, 0:P], w_i_early[:, P:]]
+
+        def quantise_turned_items(t, tag=""):
+            codes = sbuf("w_i_codes%d" % t, [P, P], U32, tag=tag)
+            quantise(codes[:], w_i_scales[:, block(t)], w_i[:, block(t), :], E4M3)
+            w_i_codes.append(codes[:])
 
         def user_plane(t, number):
             values = sbuf("du%d" % t, [P, N], F32)
@@ -298,6 +303,7 @@ def tile_attend_gmf_bpr_vu_kernel(tc, uT, vT, us, ts, offs, uoffs, out_0, out_1)
         quantise_items(0)
         for u in range(2):
             subtract(0, u)
+        quantise_turned_items(2, tag="negative0")
         for u in range(2):
             weigh(0, u)
         finish_items(1)
@@ -311,17 +317,17 @@ def tile_attend_gmf_bpr_vu_kernel(tc, uT, vT, us, ts, offs, uoffs, out_0, out_1)
         early_block(0, 5)
         gradient(1)
         lay_turned(w_i[:, block(PACK - 1), :], turn_plane(w_listed, PACK - 1, score_bank(1, 1, 1)))
-        quantise(w_i_late[:], w_i_scales[:, half(1)], w_i[:, half(1), :], E4M3)
+        quantise_turned_items(3)
         early_block(1, 7, tag="q1")
         early_block(2, 7)
         late_blocks(0, 1)
         late_blocks(1, 3)
+        late_blocks(2, 0)
         turn_pairs(0, 4)
         turn_pairs(1, 6)
         quantise(h_i_codes[:], h_i_scales[:], h_i[:], E5M2)
-        late_blocks(2, 6)
+        item_plane(3, 6)
         user_plane(0, 5)
         user_plane(1, 7)
-        item_plane(3, 5)
         user_plane(2, 3)
         user_plane(3, 1)

@@ -34,7 +34,7 @@ def tile_attend_gmf_bpr_vu_kernel(tc, uT, vT, us, ts, offs, uoffs, out_0, out_1)
         psum = ctx.enter_context(tc.psum_pool(name="psum", bufs=1))
 
         def sbuf(name, shape, dtype, tag=""):
-            return keep.tile(shape, dtype, name=name, tag=tag or name, align_bytes=256)
+            return keep.tile(shape, dtype, name=name, tag=tag or name, align_bytes=64)
 
         def bank(number):
             return psum.tile([P, PACK, P], F32, name="bank%d" % number)
@@ -68,7 +68,7 @@ def tile_attend_gmf_bpr_vu_kernel(tc, uT, vT, us, ts, offs, uoffs, out_0, out_1)
         row_scale = sbuf("row_scale", [P, PACK], F32)
         nc.scalar.dma_start(ts_row[P - 1 : P, :], ts[0:1, :])
         nc.scalar.dma_start(row_scale[:], us.rearrange("b (p t) o -> p (b t o)", t=PACK))
-        nc.vector.memset(ts_row[0 : P - 1, :].bitcast(I32), 0)
+        nc.gpsimd.memset(ts_row[0 : P - 1, :].bitcast(I32), 0)
         for t in range(1, PACK):
             nc.sync.dma_start(u_plane[t][:], planes(uT)[:, t, :])
         for t in range(PACK):
@@ -86,15 +86,13 @@ def tile_attend_gmf_bpr_vu_kernel(tc, uT, vT, us, ts, offs, uoffs, out_0, out_1)
         make_identity(nc, ident_f32[:])
 
         dv_window = [sbuf("dv_window%d" % k, [P, T], F32) for k in range(PACK)]
-        du_window = [sbuf("du_window%d" % k, [P, T], F32) for k in range(PACK - 1)]
         zeros = sbuf("zeros", [P, P], F32)
         nc.gpsimd.memset(zeros[:], 0.0)
         h_r_codes = sbuf("h_r_codes", [P, PAD + N], U32)
         h_r_scales = sbuf("h_r_scales", [P, PAD + N], U8)
         nc.gpsimd.memset(h_r_codes[:, 0:PAD], 0)
         nc.gpsimd.memset(h_r_scales[:, 0:PAD].bitcast(I32), 0)
-        nc.vector.memset(dv_window[0][:].bitcast(I32), 0)
-        for window in dv_window[1:] + du_window:
+        for window in dv_window:
             nc.gpsimd.memset(window[:].bitcast(I32), 0)
 
         ts_listed = sbuf("ts_listed", [P, N], F32)
@@ -282,6 +280,13 @@ def tile_attend_gmf_bpr_vu_kernel(tc, uT, vT, us, ts, offs, uoffs, out_0, out_1)
             nc.scalar.copy(values[:].rearrange("p (m s) -> p m s", s=PACK), sums[:].rearrange("p s m -> p m s"))
             place(t, values, du_window, user_list, out_1)
 
+        du_window = []
+
+        def zero_user_window(tag):
+            window = sbuf("du_window%d" % len(du_window), [P, T], F32, tag=tag)
+            nc.gpsimd.memset(window[:].bitcast(I32), 0)
+            du_window.append(window)
+
         def turn_pairs(u, number):
             turned = bank(number)
             words = flat(h_r[:]).bitcast(F32).rearrange("p (m k u) -> p k u m", k=PACK, u=2)
@@ -323,6 +328,8 @@ def tile_attend_gmf_bpr_vu_kernel(tc, uT, vT, us, ts, offs, uoffs, out_0, out_1)
         late_blocks(0, 1)
         late_blocks(1, 3)
         late_blocks(2, 0)
+        for tag in ("w_i", "early2", "late0"):
+            zero_user_window(tag)
         turn_pairs(0, 4)
         turn_pairs(1, 6)
         quantise(h_i_codes[:], h_i_scales[:], h_i[:], E5M2)

@@ -24,7 +24,8 @@ PACK = 4
 HALF = N // 2
 COLS = N // 16
 BLOCK_COLS = P // 16
-PAD = N - P
+USER_WINDOWS = 3
+WARM_PASSES = 2
 
 
 def tile_attend_gmf_bpr_vu_kernel(tc, uT, vT, us, ts, offs, uoffs, out_0, out_1):
@@ -88,10 +89,8 @@ def tile_attend_gmf_bpr_vu_kernel(tc, uT, vT, us, ts, offs, uoffs, out_0, out_1)
         dv_window = [sbuf("dv_window%d" % k, [P, T], F32) for k in range(PACK)]
         zeros = sbuf("zeros", [P, P], F32)
         nc.gpsimd.memset(zeros[:], 0.0)
-        h_r_codes = sbuf("h_r_codes", [P, PAD + N], U32)
-        h_r_scales = sbuf("h_r_scales", [P, PAD + N], U8)
-        nc.gpsimd.memset(h_r_codes[:, 0:PAD], 0)
-        nc.gpsimd.memset(h_r_scales[:, 0:PAD].bitcast(I32), 0)
+        h_r_codes = sbuf("h_r_codes", [P, N], U32)
+        h_r_scales = sbuf("h_r_scales", [P, N], U8)
         for window in dv_window:
             nc.gpsimd.memset(window[:].bitcast(I32), 0)
 
@@ -171,6 +170,18 @@ def tile_attend_gmf_bpr_vu_kernel(tc, uT, vT, us, ts, offs, uoffs, out_0, out_1)
                     nc.scalar.copy(w_by_column[k][:, :, 0:2, :], w_by_plane[0][:, groups(k)])
         quantise(w_i_early[:], w_i_scales[:, half(0)], w_i[:, half(0), :], E4M3)
 
+        warm_bank = bank(1)
+        for k in range(WARM_PASSES):
+            nc.tensor.matmul_mx(
+                out=flat(warm_bank[:]),
+                lhsT=w_i_early[:, block(k)].bitcast(E4M3),
+                lhsT_scale=w_i_scales[:, block(k)],
+                rhs=x_d_codes[:].bitcast(E4M3),
+                rhs_scale=x_d_scales[:],
+                start=True,
+                stop=True,
+            )
+
         w_d_codes = {}
         margin = sbuf("margin", [P, 2, N], F32)
         q = [sbuf("q%d" % c, [P, P // PACK, PACK, PACK], F32) for c in range(2)]
@@ -182,8 +193,8 @@ def tile_attend_gmf_bpr_vu_kernel(tc, uT, vT, us, ts, offs, uoffs, out_0, out_1)
             for k in (2 * c + 1, 2 * c):
                 nc.vector.tensor_copy(w_by_column[k][:, :, 2:PACK, :], w_by_plane[1][:, groups(k)])
 
-        def quantise_items(k, tag=""):
-            w_d_codes[k] = sbuf("w_d_codes%d" % k, [P, P], U32, tag=tag)
+        def quantise_items(k):
+            w_d_codes[k] = sbuf("w_d_codes%d" % k, [P, P], U32)
             quantise(w_d_codes[k][:], w_d_scales[:, block(k)], w_d[k], E4M3)
 
         def score_bank(c, u, a):
@@ -222,15 +233,14 @@ def tile_attend_gmf_bpr_vu_kernel(tc, uT, vT, us, ts, offs, uoffs, out_0, out_1)
                     scale=row_scale[:, s : s + 1],
                 )
 
-        def gradient(c):
-            for k in (2 * c, 2 * c + 1):
-                nc.vector.tensor_tensor(
-                    h_r[:, block(k), :].rearrange("p (g i) s -> p g s i", i=PACK), q[c][:], signed[:, groups(k)], MULT
-                )
-            for k in (2 * c, 2 * c + 1):
-                first = PAD + (2 * (k % 2) + c) * P
-                columns = slice(first, first + P)
-                quantise(h_r_codes[:, columns], h_r_scales[:, columns], h_r[:, block(k), :], E5M2)
+        def gradient(k, parts=1):
+            c, a = divmod(k, 2)
+            columns = h_r[:, block(k), :].rearrange("p (g i) s -> p g s i", i=PACK)
+            for part in range(parts):
+                some = slice(part * P // PACK // parts, (part + 1) * P // PACK // parts)
+                nc.vector.tensor_tensor(columns[:, some], q[c][:, some], signed[:, groups(k)][:, some], MULT)
+            in_list = block(2 * a + c)
+            quantise(h_r_codes[:, in_list], h_r_scales[:, in_list], h_r[:, block(k), :], E5M2)
 
         def product(number, codes, scales, h_codes, h_scales):
             sums = bank(number)
@@ -245,40 +255,40 @@ def tile_attend_gmf_bpr_vu_kernel(tc, uT, vT, us, ts, offs, uoffs, out_0, out_1)
             )
             return sums
 
-        def item_product(t, number, first=PAD):
-            columns = slice(first, first + N)
-            return product(number, x_r_codes[:, block(t)], x_r_scales[:, block(t)], h_r_codes[:, columns], h_r_scales[:, columns])
+        def item_product(t, number):
+            return product(number, x_r_codes[:, block(t)], x_r_scales[:, block(t)], h_r_codes[:], h_r_scales[:])
 
-        def early_block(t, number, tag=""):
-            values = sbuf("early%d" % t, [P, P], F32, tag=tag)
-            nc.scalar.copy(values[:], item_product(t, number, first=0)[:, PACK - 1, :])
-            nc.vector.tensor_tensor(dv_window[t][:].indirect(item_entries(0, 0)), values[:], zeros[:], ADD)
-
-        def place(t, values, windows, entries, out):
-            window = windows[t % len(windows)]
-            nc.vector.tensor_copy(window[:].indirect(entries[:]), values[:])
-            nc.sync.dma_start(planes(out)[:, t, :], window[:])
-
-        def item_plane(t, number):
-            values = sbuf("dv%d" % t, [P, N], F32)
-            nc.scalar.copy(values[:], flat(item_product(t, number)[:]))
-            place(t, values, dv_window, item_list, out_0)
+        def early_blocks(number, turn_banks):
+            sums = bank(number)
+            nc.tensor.matmul_mx(
+                out=flat(sums[:]),
+                lhsT=h_r_codes[:, block(0)].bitcast(E5M2),
+                lhsT_scale=h_r_scales[:, block(0)],
+                rhs=x_r_codes[:].bitcast(E4M3),
+                rhs_scale=x_r_scales[:],
+                start=True,
+                stop=True,
+            )
+            by_item = sbuf("by_item", [P, PACK, P], F32)
+            for t in range(PACK):
+                nc.scalar.copy(by_item[:, t, :], sums[:, t, :])
+            turned = [bank(other) for other in turn_banks]
+            for t in range(PACK):
+                nc.tensor.transpose(turned[t][:, 0, :], by_item[:, t, :], ident_f32[:])
+            return turned
 
         h_i = sbuf("h_i", [P, N, PACK], BF16)
         h_i_codes = sbuf("h_i_codes", [P, N], U32)
         h_i_scales = sbuf("h_i_scales", [P, N], U8)
         w_i_codes = [w_i_early[:, 0:P], w_i_early[:, P:]]
 
-        def quantise_turned_items(t, tag=""):
-            codes = sbuf("w_i_codes%d" % t, [P, P], U32, tag=tag)
-            quantise(codes[:], w_i_scales[:, block(t)], w_i[:, block(t), :], E4M3)
-            w_i_codes.append(codes[:])
-
         def user_plane(t, number):
             values = sbuf("du%d" % t, [P, N], F32)
             sums = product(number, w_i_codes[t], w_i_scales[:, block(t)], h_i_codes[:], h_i_scales[:])
             nc.scalar.copy(values[:].rearrange("p (m s) -> p m s", s=PACK), sums[:].rearrange("p s m -> p m s"))
-            place(t, values, du_window, user_list, out_1)
+            window = du_window[t % USER_WINDOWS]
+            nc.vector.tensor_copy(window[:].indirect(user_list[:]), values[:])
+            nc.sync.dma_start(planes(out_1)[:, t, :], window[:])
 
         du_window = []
 
@@ -308,7 +318,6 @@ def tile_attend_gmf_bpr_vu_kernel(tc, uT, vT, us, ts, offs, uoffs, out_0, out_1)
         quantise_items(0)
         for u in range(2):
             subtract(0, u)
-        quantise_turned_items(2, tag="negative0")
         for u in range(2):
             weigh(0, u)
         finish_items(1)
@@ -317,24 +326,27 @@ def tile_attend_gmf_bpr_vu_kernel(tc, uT, vT, us, ts, offs, uoffs, out_0, out_1)
         for u in range(2):
             subtract(1, u)
         gradient(0)
+        gradient(1, parts=2)
         for u in range(2):
             weigh(1, u)
-        early_block(0, 5)
-        gradient(1)
-        lay_turned(w_i[:, block(PACK - 1), :], turn_plane(w_listed, PACK - 1, score_bank(1, 1, 1)))
-        quantise_turned_items(3)
-        early_block(1, 7, tag="q1")
-        early_block(2, 7)
-        late_blocks(0, 1)
-        late_blocks(1, 3)
-        late_blocks(2, 0)
-        for tag in ("w_i", "early2", "late0"):
+        lay_turned(w_i[:, block(PACK - 1), :], turn_plane(w_listed, PACK - 1, score_bank(1, 1, 0)))
+        early = early_blocks(score_bank(0, 0, 0), (score_bank(0, 1, 0), score_bank(0, 0, 1), score_bank(0, 1, 1), score_bank(1, 0, 1)))
+        gradient(2)
+        gradient(3)
+        w_i_late = sbuf("w_i_late", [P, HALF], U32, tag="signed")
+        quantise(w_i_late[:], w_i_scales[:, half(1)], w_i[:, half(1), :], E4M3)
+        w_i_codes.extend([w_i_late[:, 0:P], w_i_late[:, P:]])
+        early_values = sbuf("early_values", [P, PACK, P], F32, tag="q1")
+        for t in range(PACK):
+            nc.scalar.copy(early_values[:, t, :], early[t][:, 0, :])
+            nc.vector.tensor_tensor(dv_window[t][:].indirect(item_entries(0, 0)), early_values[:, t, :], zeros[:], ADD)
+        for t in range(PACK - 1):
+            late_blocks(t, t + 1)
+        for tag in ("w_i", "q1", "late0"):
             zero_user_window(tag)
-        turn_pairs(0, 4)
-        turn_pairs(1, 6)
+        turn_pairs(0, 7)
+        turn_pairs(1, 1)
         quantise(h_i_codes[:], h_i_scales[:], h_i[:], E5M2)
-        item_plane(3, 6)
-        user_plane(0, 5)
-        user_plane(1, 7)
-        user_plane(2, 3)
-        user_plane(3, 1)
+        late_blocks(PACK - 1, 1)
+        for t in range(PACK):
+            user_plane(t, (PACK + 2 * t) % (2 * PACK))

@@ -24,8 +24,7 @@ PACK = 4
 HALF = N // 2
 COLS = N // 16
 BLOCK_COLS = P // 16
-USER_WINDOWS = 3
-WARM_PASSES = 2
+HALF_COLS = COLS // 2
 
 
 def tile_attend_gmf_bpr_vu_kernel(tc, uT, vT, us, ts, offs, uoffs, out_0, out_1):
@@ -58,6 +57,13 @@ def tile_attend_gmf_bpr_vu_kernel(tc, uT, vT, us, ts, offs, uoffs, out_0, out_1)
         def groups(k):
             return slice(k * P // PACK, (k + 1) * P // PACK)
 
+        warm = sbuf("warm", [P, 8], F32)
+        nc.gpsimd.memset(warm[:], 0.0)
+        nc.scalar.activation(warm[:], warm[:], SIGMOID)
+
+        ident_f32 = sbuf("ident_f32", [P, P], F32)
+        make_identity(nc, ident_f32[:])
+
         user_list = keep.tile([P, COLS], U16, name="user_list")
         item_list = keep.tile([P, COLS], U16, name="item_list")
         u_plane = [sbuf("u_plane%d" % t, [P, T], F32) for t in range(PACK)]
@@ -79,18 +85,8 @@ def tile_attend_gmf_bpr_vu_kernel(tc, uT, vT, us, ts, offs, uoffs, out_0, out_1)
             first = (2 * a + c) * BLOCK_COLS
             return item_list[:, first : first + BLOCK_COLS]
 
-        warm = sbuf("warm", [P, 8], F32)
-        nc.gpsimd.memset(warm[:], 0.0)
-        nc.scalar.activation(warm[:], warm[:], SIGMOID)
-
-        ident_f32 = sbuf("ident_f32", [P, P], F32)
-        make_identity(nc, ident_f32[:])
-
         dv_window = [sbuf("dv_window%d" % k, [P, T], F32) for k in range(PACK)]
-        zeros = sbuf("zeros", [P, P], F32)
-        nc.gpsimd.memset(zeros[:], 0.0)
-        h_r_codes = sbuf("h_r_codes", [P, N], U32)
-        h_r_scales = sbuf("h_r_scales", [P, N], U8)
+        du_window = []
         for window in dv_window:
             nc.gpsimd.memset(window[:].bitcast(I32), 0)
 
@@ -142,8 +138,8 @@ def tile_attend_gmf_bpr_vu_kernel(tc, uT, vT, us, ts, offs, uoffs, out_0, out_1)
             nc.scalar.copy(x_by_column[:, groups(k)], x_by_plane[:, groups(k)])
         x_d_codes = sbuf("x_d_codes", [P, N], U32, tag="v_plane1")
         x_d_scales = sbuf("x_d_scales", [P, N], U8)
-        x_r_codes = sbuf("x_r_codes", [P, D], U32, tag="v_plane0")
-        x_r_scales = sbuf("x_r_scales", [P, D], U8)
+        x_r_codes = [sbuf("x_r_codes0", [P, HALF], U32), sbuf("x_r_codes1", [P, HALF], U32, tag="v_plane0")]
+        x_r_scales = [sbuf("x_r_scales%d" % u, [P, HALF], U8) for u in range(2)]
 
         shared = sbuf("w_shared", [P, 2 * N + HALF], BF16)
         w_low = sbuf("w_low", [P, 2, N], BF16)
@@ -163,24 +159,13 @@ def tile_attend_gmf_bpr_vu_kernel(tc, uT, vT, us, ts, offs, uoffs, out_0, out_1)
             )
             lay_turned(w_i[:, block(t), :], turn_plane(w_listed, t, 2 + t % 2))
             if t == 0:
-                quantise(x_r_codes[:], x_r_scales[:], x_r[:], E4M3)
+                for u in range(2):
+                    quantise(x_r_codes[u][:], x_r_scales[u][:], x_r[:, half(u), :], E4M3)
             if t == 1:
                 quantise(x_d_codes[:], x_d_scales[:], x_d[:], E4M3)
                 for k in (1, 0, 3, 2):
                     nc.scalar.copy(w_by_column[k][:, :, 0:2, :], w_by_plane[0][:, groups(k)])
         quantise(w_i_early[:], w_i_scales[:, half(0)], w_i[:, half(0), :], E4M3)
-
-        warm_bank = bank(1)
-        for k in range(WARM_PASSES):
-            nc.tensor.matmul_mx(
-                out=flat(warm_bank[:]),
-                lhsT=w_i_early[:, block(k)].bitcast(E4M3),
-                lhsT_scale=w_i_scales[:, block(k)],
-                rhs=x_d_codes[:].bitcast(E4M3),
-                rhs_scale=x_d_scales[:],
-                start=True,
-                stop=True,
-            )
 
         w_d_codes = {}
         margin = sbuf("margin", [P, 2, N], F32)
@@ -233,19 +218,19 @@ def tile_attend_gmf_bpr_vu_kernel(tc, uT, vT, us, ts, offs, uoffs, out_0, out_1)
                     scale=row_scale[:, s : s + 1],
                 )
 
-        def gradient(k, parts=1):
-            c, a = divmod(k, 2)
-            columns = h_r[:, block(k), :].rearrange("p (g i) s -> p g s i", i=PACK)
-            for part in range(parts):
-                some = slice(part * P // PACK // parts, (part + 1) * P // PACK // parts)
-                nc.vector.tensor_tensor(columns[:, some], q[c][:, some], signed[:, groups(k)][:, some], MULT)
-            in_list = block(2 * a + c)
-            quantise(h_r_codes[:, in_list], h_r_scales[:, in_list], h_r[:, block(k), :], E5M2)
+        h_r_codes = sbuf("h_r_codes", [P, N], U32)
+        h_r_scales = sbuf("h_r_scales", [P, N], U8)
 
-        def product(number, codes, scales, h_codes, h_scales):
-            sums = bank(number)
+        def gradient(k):
+            columns = h_r[:, block(k), :].rearrange("p (g i) s -> p g s i", i=PACK)
+            nc.vector.tensor_tensor(columns, q[k // 2][:], signed[:, groups(k)], MULT)
+
+        def quantise_gradient(c):
+            quantise(h_r_codes[:, half(c)], h_r_scales[:, half(c)], h_r[:, half(c), :], E5M2)
+
+        def product(sums, codes, scales, h_codes, h_scales):
             nc.tensor.matmul_mx(
-                out=flat(sums[:]),
+                out=sums,
                 lhsT=codes.bitcast(E4M3),
                 lhsT_scale=scales,
                 rhs=h_codes.bitcast(E5M2),
@@ -253,49 +238,50 @@ def tile_attend_gmf_bpr_vu_kernel(tc, uT, vT, us, ts, offs, uoffs, out_0, out_1)
                 start=True,
                 stop=True,
             )
-            return sums
 
-        def item_product(t, number):
-            return product(number, x_r_codes[:, block(t)], x_r_scales[:, block(t)], h_r_codes[:], h_r_scales[:])
+        dv = [sbuf("dv%d" % t, [P, N], F32) for t in range(PACK)]
 
-        def early_blocks(number, turn_banks):
+        def item_sums(t, c, number):
             sums = bank(number)
-            nc.tensor.matmul_mx(
-                out=flat(sums[:]),
-                lhsT=h_r_codes[:, block(0)].bitcast(E5M2),
-                lhsT_scale=h_r_scales[:, block(0)],
-                rhs=x_r_codes[:].bitcast(E4M3),
-                rhs_scale=x_r_scales[:],
-                start=True,
-                stop=True,
+            columns = block(t % 2)
+            product(
+                flat(sums[:, 0:2, :]),
+                x_r_codes[t // 2][:, columns],
+                x_r_scales[t // 2][:, columns],
+                h_r_codes[:, half(c)],
+                h_r_scales[:, half(c)],
             )
-            by_item = sbuf("by_item", [P, PACK, P], F32)
-            for t in range(PACK):
-                nc.scalar.copy(by_item[:, t, :], sums[:, t, :])
-            turned = [bank(other) for other in turn_banks]
-            for t in range(PACK):
-                nc.tensor.transpose(turned[t][:, 0, :], by_item[:, t, :], ident_f32[:])
-            return turned
+            nc.scalar.copy(dv[t][:].rearrange("p (a c m) -> p c a m", a=2, c=2)[:, c], sums[:, 0:2, :])
+
+        def scatter_whole(window, entries, values):
+            nc.vector.tensor_copy(window[:].indirect(entries[:]), values[:])
+
+        def scatter_half(window, entries, values, u):
+            some = entries[:, u * HALF_COLS : (u + 1) * HALF_COLS]
+            nc.scalar.activation(window[:].indirect(some), values[:, half(u)], COPY)
 
         h_i = sbuf("h_i", [P, N, PACK], BF16)
         h_i_codes = sbuf("h_i_codes", [P, N], U32)
         h_i_scales = sbuf("h_i_scales", [P, N], U8)
         w_i_codes = [w_i_early[:, 0:P], w_i_early[:, P:]]
+        du = [sbuf("du%d" % t, [P, N], F32) for t in range(PACK)]
 
-        def user_plane(t, number):
-            values = sbuf("du%d" % t, [P, N], F32)
-            sums = product(number, w_i_codes[t], w_i_scales[:, block(t)], h_i_codes[:], h_i_scales[:])
-            nc.scalar.copy(values[:].rearrange("p (m s) -> p m s", s=PACK), sums[:].rearrange("p s m -> p m s"))
-            window = du_window[t % USER_WINDOWS]
-            nc.vector.tensor_copy(window[:].indirect(user_list[:]), values[:])
-            nc.sync.dma_start(planes(out_1)[:, t, :], window[:])
-
-        du_window = []
+        def user_sums(t, number):
+            sums = bank(number)
+            product(flat(sums[:]), w_i_codes[t], w_i_scales[:, block(t)], h_i_codes[:], h_i_scales[:])
+            listed = du[t][:].rearrange("p (m s) -> p m s", s=PACK)
+            if t % 2:
+                nc.scalar.copy(listed, sums[:].rearrange("p s m -> p m s"))
+            else:
+                nc.vector.tensor_copy(listed, sums[:].rearrange("p s m -> p m s"))
 
         def zero_user_window(tag):
             window = sbuf("du_window%d" % len(du_window), [P, T], F32, tag=tag)
             nc.gpsimd.memset(window[:].bitcast(I32), 0)
             du_window.append(window)
+
+        def store(dram, t, window):
+            nc.sync.dma_start(planes(dram)[:, t, :], window[:])
 
         def turn_pairs(u, number):
             turned = bank(number)
@@ -306,12 +292,6 @@ def tile_attend_gmf_bpr_vu_kernel(tc, uT, vT, us, ts, offs, uoffs, out_0, out_1)
                 h_i[:, half(u), :].rearrange("p (e c) k -> p e c k", e=2),
                 flat(turned[:]).bitcast(BF16).rearrange("p (k c e) -> p e c k", k=PACK, e=2),
             )
-
-        def late_blocks(t, number):
-            values = sbuf("late%d" % t, [P, PACK - 1, P], F32)
-            nc.scalar.copy(values[:], item_product(t, number)[:, 1:PACK, :])
-            nc.vector.tensor_copy(dv_window[t][:].indirect(item_list[:, BLOCK_COLS:]), flat(values[:]))
-            nc.sync.dma_start(planes(out_0)[:, t, :], dv_window[t][:])
 
         finish_items(0)
         quantise_items(1)
@@ -326,27 +306,45 @@ def tile_attend_gmf_bpr_vu_kernel(tc, uT, vT, us, ts, offs, uoffs, out_0, out_1)
         for u in range(2):
             subtract(1, u)
         gradient(0)
-        gradient(1, parts=2)
+        gradient(1)
+        quantise_gradient(0)
         for u in range(2):
             weigh(1, u)
         lay_turned(w_i[:, block(PACK - 1), :], turn_plane(w_listed, PACK - 1, score_bank(1, 1, 0)))
-        early = early_blocks(score_bank(0, 0, 0), (score_bank(0, 1, 0), score_bank(0, 0, 1), score_bank(0, 1, 1), score_bank(1, 0, 1)))
         gradient(2)
-        gradient(3)
-        w_i_late = sbuf("w_i_late", [P, HALF], U32, tag="signed")
-        quantise(w_i_late[:], w_i_scales[:, half(1)], w_i[:, half(1), :], E4M3)
-        w_i_codes.extend([w_i_late[:, 0:P], w_i_late[:, P:]])
-        early_values = sbuf("early_values", [P, PACK, P], F32, tag="q1")
         for t in range(PACK):
-            nc.scalar.copy(early_values[:, t, :], early[t][:, 0, :])
-            nc.vector.tensor_tensor(dv_window[t][:].indirect(item_entries(0, 0)), early_values[:, t, :], zeros[:], ADD)
-        for t in range(PACK - 1):
-            late_blocks(t, t + 1)
-        for tag in ("w_i", "q1", "late0"):
+            item_sums(t, 0, PACK + t)
+        gradient(3)
+        quantise_gradient(1)
+        item_sums(0, 1, 0)
+        scatter_whole(dv_window[0], item_list, dv[0])
+        store(out_0, 0, dv_window[0])
+        item_sums(1, 1, 1)
+        for tag in ("x_r_codes0", "x_r_scales0"):
             zero_user_window(tag)
-        turn_pairs(0, 7)
+        scatter_half(dv_window[1], item_list, dv[1], 0)
+        item_sums(2, 1, 2)
+        scatter_half(dv_window[1], item_list, dv[1], 1)
+        store(out_0, 1, dv_window[1])
+        scatter_whole(dv_window[2], item_list, dv[2])
+        store(out_0, 2, dv_window[2])
+        turn_pairs(0, 0)
         turn_pairs(1, 1)
         quantise(h_i_codes[:], h_i_scales[:], h_i[:], E5M2)
-        late_blocks(PACK - 1, 1)
-        for t in range(PACK):
-            user_plane(t, (PACK + 2 * t) % (2 * PACK))
+        w_i_late = sbuf("w_i_late", [P, HALF], U32, tag="h_i")
+        quantise(w_i_late[:], w_i_scales[:, half(1)], w_i[:, half(1), :], E4M3)
+        w_i_codes.extend([w_i_late[:, 0:P], w_i_late[:, P:]])
+        item_sums(3, 1, 0)
+        for u in range(2):
+            scatter_half(dv_window[3], item_list, dv[3], u)
+        store(out_0, 3, dv_window[3])
+        for tag in ("w_i", "dv3"):
+            zero_user_window(tag)
+        for t in range(0, PACK, 2):
+            user_sums(t, PACK + t)
+            user_sums(t + 1, PACK + t + 1)
+            scatter_whole(du_window[t], user_list, du[t])
+            store(out_1, t, du_window[t])
+            for u in range(2):
+                scatter_half(du_window[t + 1], user_list, du[t + 1], u)
+            store(out_1, t + 1, du_window[t + 1])

@@ -141,11 +141,10 @@ def tile_attend_gmf_bpr_vu_kernel(tc, uT, vT, us, ts, offs, uoffs, out_0, out_1)
         x_r_codes = [sbuf("x_r_codes0", [P, HALF], U32), sbuf("x_r_codes1", [P, HALF], U32, tag="v_plane0")]
         x_r_scales = [sbuf("x_r_scales%d" % u, [P, HALF], U8) for u in range(2)]
 
-        shared = sbuf("w_shared", [P, 2 * N + HALF], BF16)
-        w_low = sbuf("w_low", [P, 2, N], BF16)
-        w_listed = [w_low[:], shared[:, 0 : 2 * N].rearrange("p (t n) -> p t n", t=2)]
-        w_rest = sbuf("w_rest", [P, PACK - 1, P, PACK], BF16)
-        w_d = [w_rest[:, 0], shared[:, N + HALF :].rearrange("p (c t) -> p c t", t=PACK), w_rest[:, 1], w_rest[:, 2]]
+        w_planes = [sbuf("w_planes%d" % u, [P, 2, N], BF16) for u in range(2)]
+        w_listed = [pair[:] for pair in w_planes]
+        w_blocks = sbuf("w_blocks", [P, PACK, P, PACK], BF16)
+        w_d = [w_blocks[:, k] for k in range(PACK)]
         w_d_scales = sbuf("w_d_scales", [P, N], U8)
         w_i = sbuf("w_i", [P, D, PACK], BF16)
         w_i_scales = sbuf("w_i_scales", [P, D], U8)
@@ -172,11 +171,16 @@ def tile_attend_gmf_bpr_vu_kernel(tc, uT, vT, us, ts, offs, uoffs, out_0, out_1)
         q = [sbuf("q%d" % c, [P, P // PACK, PACK, PACK], F32) for c in range(2)]
         h_r = sbuf("h_r", [P, N, PACK], BF16)
 
-        def finish_items(c):
-            for a in (1, 0):
-                nc.vector.tensor_copy(w_listed[1][:, 1, block(2 * c + a)], v_plane[PACK - 1][:].indirect(item_entries(c, a)))
-            for k in (2 * c + 1, 2 * c):
+        def finish_items(k):
+            c, a = divmod(k, 2)
+            listed = w_listed[1][:, 1, block(k)]
+            window = v_plane[PACK - 1][:].indirect(item_entries(c, a))
+            if a:
+                nc.vector.tensor_copy(listed, window)
                 nc.vector.tensor_copy(w_by_column[k][:, :, 2:PACK, :], w_by_plane[1][:, groups(k)])
+            else:
+                nc.scalar.activation(listed, window, COPY)
+                nc.scalar.copy(w_by_column[k][:, :, 2:PACK, :], w_by_plane[1][:, groups(k)])
 
         def quantise_items(k):
             w_d_codes[k] = sbuf("w_d_codes%d" % k, [P, P], U32)
@@ -199,10 +203,13 @@ def tile_attend_gmf_bpr_vu_kernel(tc, uT, vT, us, ts, offs, uoffs, out_0, out_1)
             return scores
 
         def subtract(c, u):
-            negative = sbuf("negative%d" % (2 * c + u), [P, HALF], F32)
-            nc.scalar.activation(negative[:], score(c, u, 1), COPY, scale=ts_column[:, c, 1:2])
+            if c + u:
+                negative = sbuf("negative%d" % (2 * c + u), [P, HALF], F32)[:]
+            else:
+                negative = w_listed[1][:, 0, :].bitcast(F32)
+            nc.scalar.activation(negative, score(c, u, 1), COPY, scale=ts_column[:, c, 1:2])
             nc.vector.scalar_tensor_tensor(
-                margin[:, c, half(u)], score(c, u, 0), ts_column[:, c, 0:1], negative[:], MULT, ADD
+                margin[:, c, half(u)], score(c, u, 0), ts_column[:, c, 0:1], negative, MULT, ADD
             )
 
         def weigh(c, u):
@@ -221,12 +228,16 @@ def tile_attend_gmf_bpr_vu_kernel(tc, uT, vT, us, ts, offs, uoffs, out_0, out_1)
         h_r_codes = sbuf("h_r_codes", [P, N], U32)
         h_r_scales = sbuf("h_r_scales", [P, N], U8)
 
-        def gradient(k):
+        def gradient(k, parts=1):
             columns = h_r[:, block(k), :].rearrange("p (g i) s -> p g s i", i=PACK)
-            nc.vector.tensor_tensor(columns, q[k // 2][:], signed[:, groups(k)], MULT)
+            for part in range(parts):
+                some = slice(part * P // PACK // parts, (part + 1) * P // PACK // parts)
+                nc.vector.tensor_tensor(columns[:, some], q[k // 2][:, some], signed[:, groups(k)][:, some], MULT)
 
-        def quantise_gradient(c):
-            quantise(h_r_codes[:, half(c)], h_r_scales[:, half(c)], h_r[:, half(c), :], E5M2)
+        def quantise_gradient(k):
+            c, a = divmod(k, 2)
+            in_list = block(2 * a + c)
+            quantise(h_r_codes[:, in_list], h_r_scales[:, in_list], h_r[:, block(k), :], E5M2)
 
         def product(sums, codes, scales, h_codes, h_scales):
             nc.tensor.matmul_mx(
@@ -239,112 +250,112 @@ def tile_attend_gmf_bpr_vu_kernel(tc, uT, vT, us, ts, offs, uoffs, out_0, out_1)
                 stop=True,
             )
 
-        dv = [sbuf("dv%d" % t, [P, N], F32) for t in range(PACK)]
-
-        def item_sums(t, c, number):
-            sums = bank(number)
-            columns = block(t % 2)
+        def item_sums(t, columns, number):
+            sums = flat(bank(number)[:])[:, columns]
+            rows = block(t % 2)
             product(
-                flat(sums[:, 0:2, :]),
-                x_r_codes[t // 2][:, columns],
-                x_r_scales[t // 2][:, columns],
-                h_r_codes[:, half(c)],
-                h_r_scales[:, half(c)],
+                sums,
+                x_r_codes[t // 2][:, rows],
+                x_r_scales[t // 2][:, rows],
+                h_r_codes[:, columns],
+                h_r_scales[:, columns],
             )
-            nc.scalar.copy(dv[t][:].rearrange("p (a c m) -> p c a m", a=2, c=2)[:, c], sums[:, 0:2, :])
+            return sums
 
-        def scatter_whole(window, entries, values):
-            nc.vector.tensor_copy(window[:].indirect(entries[:]), values[:])
+        def copy_out(u, values, sums):
+            if u:
+                nc.vector.tensor_copy(values, sums)
+            else:
+                nc.scalar.copy(values, sums)
 
-        def scatter_half(window, entries, values, u):
-            some = entries[:, u * HALF_COLS : (u + 1) * HALF_COLS]
-            nc.scalar.activation(window[:].indirect(some), values[:, half(u)], COPY)
+        def put(dram, t, window, entries, halves):
+            nc.scalar.activation(window[:].indirect(entries[:, 0:HALF_COLS]), halves[0], COPY)
+            nc.vector.tensor_copy(window[:].indirect(entries[:, HALF_COLS:]), halves[1])
+            nc.sync.dma_start(planes(dram)[:, t, :], window[:])
+
+        dv = {}
+
+        def stage_item_half(t, a):
+            values = sbuf("dv%d_%d" % (t, a), [P, HALF], F32)
+            copy_out(a, values[:], item_sums(t, half(a), t if a else PACK + 2 * t))
+            dv[t, a] = values[:]
+
+        def stage_item_plane(t, tag):
+            values = sbuf("dv%d" % t, [P, N], F32, tag=tag)
+            copy_out(0, values[:], item_sums(t, slice(0, N), t))
+            for a in range(2):
+                dv[t, a] = values[:, half(a)]
+
+        def put_items(t):
+            put(out_0, t, dv_window[t], item_list, (dv[t, 0], dv[t, 1]))
 
         h_i = sbuf("h_i", [P, N, PACK], BF16)
         h_i_codes = sbuf("h_i_codes", [P, N], U32)
         h_i_scales = sbuf("h_i_scales", [P, N], U8)
         w_i_codes = [w_i_early[:, 0:P], w_i_early[:, P:]]
-        du = [sbuf("du%d" % t, [P, N], F32) for t in range(PACK)]
 
-        def user_sums(t, number):
-            sums = bank(number)
+        du = {}
+
+        def stage_users(t):
+            sums = bank(PACK + t)
             product(flat(sums[:]), w_i_codes[t], w_i_scales[:, block(t)], h_i_codes[:], h_i_scales[:])
-            listed = du[t][:].rearrange("p (m s) -> p m s", s=PACK)
-            if t % 2:
-                nc.scalar.copy(listed, sums[:].rearrange("p s m -> p m s"))
-            else:
-                nc.vector.tensor_copy(listed, sums[:].rearrange("p s m -> p m s"))
+            for u in range(2):
+                values = sbuf("du%d_%d" % (t, u), [P, HALF], F32, tag="du%d_%d" % (t % 2, u))
+                some = sums[:, :, u * P // 2 : (u + 1) * P // 2].rearrange("p s m -> p m s")
+                copy_out(u, values[:].rearrange("p (m s) -> p m s", s=PACK), some)
+                du[t, u] = values[:]
+
+        def put_users(t):
+            put(out_1, t, du_window[t], user_list, (du[t, 0], du[t, 1]))
 
         def zero_user_window(tag):
             window = sbuf("du_window%d" % len(du_window), [P, T], F32, tag=tag)
             nc.gpsimd.memset(window[:].bitcast(I32), 0)
             du_window.append(window)
 
-        def store(dram, t, window):
-            nc.sync.dma_start(planes(dram)[:, t, :], window[:])
-
         def turn_pairs(u, number):
             turned = bank(number)
             words = flat(h_r[:]).bitcast(F32).rearrange("p (m k u) -> p k u m", k=PACK, u=2)
             for k in range(PACK):
                 nc.tensor.transpose(turned[:, k, :], words[:, k, u, :], ident_f32[:])
-            nc.scalar.copy(
-                h_i[:, half(u), :].rearrange("p (e c) k -> p e c k", e=2),
-                flat(turned[:]).bitcast(BF16).rearrange("p (k c e) -> p e c k", k=PACK, e=2),
-            )
+            laid = h_i[:, half(u), :].rearrange("p (e c) k -> p e c k", e=2)
+            pairs = flat(turned[:]).bitcast(BF16).rearrange("p (k c e) -> p e c k", k=PACK, e=2)
+            copy_out(u, laid, pairs)
 
-        finish_items(0)
-        quantise_items(1)
-        quantise_items(0)
-        for u in range(2):
-            subtract(0, u)
-        for u in range(2):
-            weigh(0, u)
-        finish_items(1)
-        quantise_items(3)
-        quantise_items(2)
-        for u in range(2):
-            subtract(1, u)
-        gradient(0)
-        gradient(1)
-        quantise_gradient(0)
-        for u in range(2):
-            weigh(1, u)
+        for k in (1, 0, 3, 2):
+            finish_items(k)
+            quantise_items(k)
+        for c in range(2):
+            for u in range(2):
+                subtract(c, u)
+            for u in range(2):
+                weigh(c, u)
         lay_turned(w_i[:, block(PACK - 1), :], turn_plane(w_listed, PACK - 1, score_bank(1, 1, 0)))
-        gradient(2)
-        for t in range(PACK):
-            item_sums(t, 0, PACK + t)
-        gradient(3)
-        quantise_gradient(1)
-        item_sums(0, 1, 0)
-        scatter_whole(dv_window[0], item_list, dv[0])
-        store(out_0, 0, dv_window[0])
-        item_sums(1, 1, 1)
-        for tag in ("x_r_codes0", "x_r_scales0"):
-            zero_user_window(tag)
-        scatter_half(dv_window[1], item_list, dv[1], 0)
-        item_sums(2, 1, 2)
-        scatter_half(dv_window[1], item_list, dv[1], 1)
-        store(out_0, 1, dv_window[1])
-        scatter_whole(dv_window[2], item_list, dv[2])
-        store(out_0, 2, dv_window[2])
-        turn_pairs(0, 0)
-        turn_pairs(1, 1)
-        quantise(h_i_codes[:], h_i_scales[:], h_i[:], E5M2)
-        w_i_late = sbuf("w_i_late", [P, HALF], U32, tag="h_i")
+        for a in range(2):
+            for c in range(2):
+                gradient(2 * c + a, parts=2 if 2 * c + a == 1 else 1)
+            for c in range(2):
+                quantise_gradient(2 * c + a)
+            for t in range(2):
+                stage_item_half(t, a)
+        w_i_late = sbuf("w_i_late", [P, HALF], U32, tag="signed")
         quantise(w_i_late[:], w_i_scales[:, half(1)], w_i[:, half(1), :], E4M3)
         w_i_codes.extend([w_i_late[:, 0:P], w_i_late[:, P:]])
-        item_sums(3, 1, 0)
-        for u in range(2):
-            scatter_half(dv_window[3], item_list, dv[3], u)
-        store(out_0, 3, dv_window[3])
-        for tag in ("w_i", "dv3"):
+        for tag in ("x_r_codes0", "x_r_scales0"):
             zero_user_window(tag)
-        for t in range(0, PACK, 2):
-            user_sums(t, PACK + t)
-            user_sums(t + 1, PACK + t + 1)
-            scatter_whole(du_window[t], user_list, du[t])
-            store(out_1, t, du_window[t])
-            for u in range(2):
-                scatter_half(du_window[t + 1], user_list, du[t + 1], u)
-            store(out_1, t + 1, du_window[t + 1])
+        for t in range(2):
+            put_items(t)
+        for u in range(2):
+            turn_pairs(u, u)
+        quantise(h_i_codes[:], h_i_scales[:], h_i[:], E5M2)
+        for t, tag in ((2, "ident_f32"), (3, "h_r")):
+            stage_item_plane(t, tag)
+            put_items(t)
+        for tag in ("h_i", "h_i_scales"):
+            zero_user_window(tag)
+        for t in range(2):
+            stage_users(t)
+        for t in range(PACK):
+            put_users(t)
+            if t < 2:
+                stage_users(t + 2)

@@ -34,7 +34,7 @@ def tile_attend_gmf_bpr_vu_kernel(tc, uT, vT, us, ts, offs, uoffs, out_0, out_1)
         psum = ctx.enter_context(tc.psum_pool(name="psum", bufs=1))
 
         def sbuf(name, shape, dtype, tag=""):
-            return keep.tile(shape, dtype, name=name, tag=tag or name, align_bytes=64)
+            return keep.tile(shape, dtype, name=name, tag=tag or name, align_bytes=256)
 
         def bank(number):
             return psum.tile([P, PACK, P], F32, name="bank%d" % number)
@@ -68,9 +68,9 @@ def tile_attend_gmf_bpr_vu_kernel(tc, uT, vT, us, ts, offs, uoffs, out_0, out_1)
         item_list = keep.tile([P, COLS], U16, name="item_list")
         u_plane = [sbuf("u_plane%d" % t, [P, T], F32) for t in range(PACK)]
         v_plane = [sbuf("v_plane%d" % t, [P, T], F32) for t in range(PACK)]
-        nc.sync.dma_start(item_list[:], offs)
         nc.sync.dma_start(u_plane[0][:], planes(uT)[:, 0, :])
         nc.sync.dma_start(user_list[:], uoffs)
+        nc.sync.dma_start(item_list[:], offs)
         ts_row = sbuf("ts_row", [P, T], F32)
         row_scale = sbuf("row_scale", [P, PACK], F32)
         nc.scalar.dma_start(ts_row[P - 1 : P, :], ts[0:1, :])
@@ -202,12 +202,15 @@ def tile_attend_gmf_bpr_vu_kernel(tc, uT, vT, us, ts, offs, uoffs, out_0, out_1)
             )
             return scores
 
-        def subtract(c, u):
+        def scale_negatives(c, u):
             if c + u:
                 negative = sbuf("negative%d" % (2 * c + u), [P, HALF], F32)[:]
             else:
                 negative = w_listed[1][:, 0, :].bitcast(F32)
             nc.scalar.activation(negative, score(c, u, 1), COPY, scale=ts_column[:, c, 1:2])
+            return negative
+
+        def subtract(c, u, negative):
             nc.vector.scalar_tensor_tensor(
                 margin[:, c, half(u)], score(c, u, 0), ts_column[:, c, 0:1], negative, MULT, ADD
             )
@@ -250,8 +253,7 @@ def tile_attend_gmf_bpr_vu_kernel(tc, uT, vT, us, ts, offs, uoffs, out_0, out_1)
                 stop=True,
             )
 
-        def item_sums(t, columns, number):
-            sums = flat(bank(number)[:])[:, columns]
+        def item_sums(t, columns, sums):
             rows = block(t % 2)
             product(
                 sums,
@@ -275,16 +277,29 @@ def tile_attend_gmf_bpr_vu_kernel(tc, uT, vT, us, ts, offs, uoffs, out_0, out_1)
 
         dv = {}
 
-        def stage_item_half(t, a):
-            values = sbuf("dv%d_%d" % (t, a), [P, HALF], F32)
-            copy_out(a, values[:], item_sums(t, half(a), t if a else PACK + 2 * t))
-            dv[t, a] = values[:]
+        positives = sbuf("positives", [P, 2, HALF], F32)
+        for t in range(2):
+            dv[t, 0] = positives[:, t, :]
 
-        def stage_item_plane(t, tag):
-            values = sbuf("dv%d" % t, [P, N], F32, tag=tag)
-            copy_out(0, values[:], item_sums(t, slice(0, N), t))
+        def stage_first_positives():
+            sums = bank(PACK + 2)
+            for t in range(2):
+                item_sums(t, block(0), sums[:, t, :])
+            nc.scalar.copy(positives[:, :, block(0)], sums[:, 0:2, :])
+
+        def stage_last_positives(t, number):
+            nc.scalar.copy(positives[:, t, block(1)], item_sums(t, block(1), bank(number)[:, 0, :]))
+
+        def stage_negatives(t):
+            values = sbuf("negatives%d" % t, [P, HALF], F32)
+            nc.vector.tensor_copy(values[:], item_sums(t, half(1), flat(bank(t)[:, 0:2, :])))
+            dv[t, 1] = values[:]
+
+        def stage_item_plane(t, sums, tags):
             for a in range(2):
-                dv[t, a] = values[:, half(a)]
+                values = sbuf("dv%d_%d" % (t, a), [P, HALF], F32, tag=tags[a])
+                copy_out(a, values[:], sums[:, half(a)])
+                dv[t, a] = values[:]
 
         def put_items(t):
             put(out_0, t, dv_window[t], item_list, (dv[t, 0], dv[t, 1]))
@@ -326,18 +341,25 @@ def tile_attend_gmf_bpr_vu_kernel(tc, uT, vT, us, ts, offs, uoffs, out_0, out_1)
             finish_items(k)
             quantise_items(k)
         for c in range(2):
+            negatives = [scale_negatives(c, u) for u in range(2)]
             for u in range(2):
-                subtract(c, u)
+                subtract(c, u, negatives[u])
             for u in range(2):
                 weigh(c, u)
         lay_turned(w_i[:, block(PACK - 1), :], turn_plane(w_listed, PACK - 1, score_bank(1, 1, 0)))
-        for a in range(2):
-            for c in range(2):
-                gradient(2 * c + a, parts=2 if 2 * c + a == 1 else 1)
-            for c in range(2):
-                quantise_gradient(2 * c + a)
-            for t in range(2):
-                stage_item_half(t, a)
+        for k in (0, 2):
+            gradient(k)
+        quantise_gradient(0)
+        stage_first_positives()
+        quantise_gradient(2)
+        for t in range(2):
+            stage_last_positives(t, PACK + t)
+        gradient(1, parts=PACK)
+        gradient(3)
+        for k in (1, 3):
+            quantise_gradient(k)
+        for t in (0, 1, 3):
+            stage_negatives(t)
         w_i_late = sbuf("w_i_late", [P, HALF], U32, tag="signed")
         quantise(w_i_late[:], w_i_scales[:, half(1)], w_i[:, half(1), :], E4M3)
         w_i_codes.extend([w_i_late[:, 0:P], w_i_late[:, P:]])
@@ -347,10 +369,14 @@ def tile_attend_gmf_bpr_vu_kernel(tc, uT, vT, us, ts, offs, uoffs, out_0, out_1)
             put_items(t)
         for u in range(2):
             turn_pairs(u, u)
+        third = item_sums(2, slice(0, N), flat(bank(2)[:]))
+        stage_item_plane(2, third, ("h_r", "ident_f32"))
         quantise(h_i_codes[:], h_i_scales[:], h_i[:], E5M2)
-        for t, tag in ((2, "ident_f32"), (3, "h_r")):
-            stage_item_plane(t, tag)
-            put_items(t)
+        put_items(2)
+        last = sbuf("last_positives", [P, HALF], F32)
+        nc.scalar.copy(last[:], item_sums(3, half(0), flat(bank(0)[:, 0:2, :])))
+        dv[3, 0] = last[:]
+        put_items(3)
         for tag in ("h_i", "h_i_scales"):
             zero_user_window(tag)
         for t in range(2):

@@ -68,9 +68,9 @@ def tile_attend_gmf_bpr_vu_kernel(tc, uT, vT, us, ts, offs, uoffs, out_0, out_1)
         item_list = keep.tile([P, COLS], U16, name="item_list")
         u_plane = [sbuf("u_plane%d" % t, [P, T], F32) for t in range(PACK)]
         v_plane = [sbuf("v_plane%d" % t, [P, T], F32) for t in range(PACK)]
+        nc.sync.dma_start(item_list[:], offs)
         nc.sync.dma_start(u_plane[0][:], planes(uT)[:, 0, :])
         nc.sync.dma_start(user_list[:], uoffs)
-        nc.sync.dma_start(item_list[:], offs)
         ts_row = sbuf("ts_row", [P, T], F32)
         row_scale = sbuf("row_scale", [P, PACK], F32)
         nc.scalar.dma_start(ts_row[P - 1 : P, :], ts[0:1, :])

@@ -23,8 +23,9 @@ P = 128
 PACK = 4
 HALF = N // 2
 COLS = N // 16
-BLOCK_COLS = P // 16
+QUARTER_COLS = P // 16
 HALF_COLS = COLS // 2
+NEGATIVES_FIRST = (2, 0, 3, 1)
 
 
 def tile_attend_gmf_bpr_vu_kernel(tc, uT, vT, us, ts, offs, uoffs, out_0, out_1):
@@ -45,10 +46,34 @@ def tile_attend_gmf_bpr_vu_kernel(tc, uT, vT, us, ts, offs, uoffs, out_0, out_1)
         def quantise(codes, scales, values, fmt):
             nc.vector.quantize_mx(out=codes.bitcast(fmt), scales=scales, in_=values.rearrange("p c t -> p (c t)"))
 
+        def multiply(sums, codes, scales, moving_codes, moving_scales, moving_fmt):
+            nc.tensor.matmul_mx(
+                out=sums,
+                lhsT=codes.bitcast(E4M3),
+                lhsT_scale=scales,
+                rhs=moving_codes.bitcast(moving_fmt),
+                rhs_scale=moving_scales,
+                start=True,
+                stop=True,
+            )
+            return sums
+
+        def move(on_vector, dst, src):
+            if on_vector:
+                nc.vector.tensor_copy(dst, src)
+            else:
+                nc.scalar.copy(dst, src)
+
+        def move_listed(on_vector, dst, src):
+            if on_vector:
+                nc.vector.tensor_copy(dst, src)
+            else:
+                nc.scalar.activation(dst, src, COPY)
+
         def flat(ap):
             return ap.rearrange("p a b -> p (a b)")
 
-        def block(k):
+        def quarter(k):
             return slice(k * P, (k + 1) * P)
 
         def half(u):
@@ -81,28 +106,24 @@ def tile_attend_gmf_bpr_vu_kernel(tc, uT, vT, us, ts, offs, uoffs, out_0, out_1)
         for t in range(PACK):
             nc.sync.dma_start(v_plane[t][:], planes(vT)[:, t, :])
 
-        def item_entries(c, a):
-            first = (2 * a + c) * BLOCK_COLS
-            return item_list[:, first : first + BLOCK_COLS]
-
-        dv_window = [sbuf("dv_window%d" % k, [P, T], F32) for k in range(PACK)]
-        du_window = []
-        for window in dv_window:
+        def zeroed_window(name, tag=""):
+            window = sbuf(name, [P, T], F32, tag=tag)
             nc.gpsimd.memset(window[:].bitcast(I32), 0)
+            return window
+
+        dv_window = [zeroed_window("dv_window%d" % t) for t in range(PACK)]
 
         ts_listed = sbuf("ts_listed", [P, N], F32)
         nc.vector.tensor_copy(ts_listed[:], ts_row[:].indirect(item_list[:]))
         ts_turned = bank(0)
-        for c in range(2):
-            for a in range(2):
-                nc.tensor.transpose(ts_turned[:, 2 * c + a, :], ts_listed[:, block(2 * a + c)], ident_f32[:])
-        ts_column = sbuf("ts_column", [P, 2, 2], F32)
-        ts_last = ts_turned[:, :, P - 1].rearrange("p (c a) -> p c a", a=2)
-        nc.scalar.activation(ts_column[:, :, 0], ts_last[:, :, 0], COPY, scale=-1.0)
-        nc.scalar.activation(ts_column[:, :, 1], ts_last[:, :, 1], COPY)
+        for k in range(PACK):
+            nc.tensor.transpose(ts_turned[:, k, :], ts_listed[:, quarter(k)], ident_f32[:])
+        ts_column = sbuf("ts_column", [P, PACK], F32)
+        nc.scalar.activation(ts_column[:, 0:2], ts_turned[:, 0:2, P - 1], COPY, scale=-1.0)
+        nc.scalar.activation(ts_column[:, 2:PACK], ts_turned[:, 2:PACK, P - 1], COPY)
         ts_spread = bank(1)
         for k in range(PACK):
-            nc.tensor.transpose(ts_spread[:, k, :], flat(ts_column[:])[:, k : k + 1].to_broadcast([P, P]), ident_f32[:])
+            nc.tensor.transpose(ts_spread[:, k, :], ts_column[:, k : k + 1].to_broadcast([P, P]), ident_f32[:])
         signed = sbuf("signed", [P, N // PACK, PACK, PACK], F32)
         for s in range(PACK):
             nc.scalar.activation(
@@ -112,8 +133,8 @@ def tile_attend_gmf_bpr_vu_kernel(tc, uT, vT, us, ts, offs, uoffs, out_0, out_1)
                 scale=row_scale[:, s : s + 1],
             )
 
-        def turn_plane(listed, t, number):
-            words = listed[t // 2][:, t % 2, :].bitcast(F32).rearrange("p (m u) -> p u m", u=2)
+        def turn_plane(plane, number):
+            words = plane.bitcast(F32).rearrange("p (m u) -> p u m", u=2)
             turned = bank(number)
             for u in range(2):
                 nc.tensor.transpose(turned[:, u, :], words[:, u, :], ident_f32[:])
@@ -126,13 +147,12 @@ def tile_attend_gmf_bpr_vu_kernel(tc, uT, vT, us, ts, offs, uoffs, out_0, out_1)
             )
 
         x_planes = sbuf("x_planes", [P, PACK, N], BF16)
-        x_listed = [x_planes[:, 0:2, :], x_planes[:, 2:PACK, :]]
         x_d = sbuf("x_d", [P, N, PACK], BF16)
         x_r = sbuf("x_r", [P, D, PACK], BF16)
         x_by_column = x_d[:].rearrange("p (s m) t -> p m s t", s=PACK)
         for t in range(PACK):
-            nc.vector.tensor_copy(x_listed[t // 2][:, t % 2, :], u_plane[t][:].indirect(user_list[:]))
-            lay_turned(x_r[:, block(t), :], turn_plane(x_listed, t, PACK + t))
+            nc.vector.tensor_copy(x_planes[:, t, :], u_plane[t][:].indirect(user_list[:]))
+            lay_turned(x_r[:, quarter(t), :], turn_plane(x_planes[:, t, :], PACK + t))
         x_by_plane = x_planes[:].rearrange("p t (m s) -> p m s t", s=PACK)
         for k in range(PACK):
             nc.scalar.copy(x_by_column[:, groups(k)], x_by_plane[:, groups(k)])
@@ -142,246 +162,173 @@ def tile_attend_gmf_bpr_vu_kernel(tc, uT, vT, us, ts, offs, uoffs, out_0, out_1)
         x_r_scales = [sbuf("x_r_scales%d" % u, [P, HALF], U8) for u in range(2)]
 
         w_planes = [sbuf("w_planes%d" % u, [P, 2, N], BF16) for u in range(2)]
-        w_listed = [pair[:] for pair in w_planes]
-        w_blocks = sbuf("w_blocks", [P, PACK, P, PACK], BF16)
-        w_d = [w_blocks[:, k] for k in range(PACK)]
+        w_d = sbuf("w_d", [P, PACK, P, PACK], BF16)
         w_d_scales = sbuf("w_d_scales", [P, N], U8)
-        w_i = sbuf("w_i", [P, D, PACK], BF16)
+        w_i = [sbuf("w_i0", [P, HALF, PACK], BF16)]
         w_i_scales = sbuf("w_i_scales", [P, D], U8)
-        w_i_early = sbuf("w_i_early", [P, HALF], U32, tag="v_plane2")
-        w_by_column = [columns.rearrange("p (g i) t -> p g t i", i=PACK) for columns in w_d]
-        w_by_plane = [pair.rearrange("p t (g i) -> p g t i", i=PACK) for pair in w_listed]
-        for t in range(PACK - 1):
-            nc.vector.tensor_copy(
-                w_listed[t // 2][:, t % 2, :].rearrange("p (c a m) -> p a c m", c=2, a=2),
-                v_plane[t][:].indirect(item_list[:]),
-            )
-            lay_turned(w_i[:, block(t), :], turn_plane(w_listed, t, 2 + t % 2))
+        w_by_column = [w_d[:, k].rearrange("p (g i) t -> p g t i", i=PACK) for k in range(PACK)]
+        w_by_plane = [pair[:].rearrange("p t (g i) -> p g t i", i=PACK) for pair in w_planes]
+        for t in range(2):
+            nc.vector.tensor_copy(w_planes[0][:, t, :], v_plane[t][:].indirect(item_list[:]))
+            lay_turned(w_i[0][:, quarter(t), :], turn_plane(w_planes[0][:, t, :], 2 + t))
             if t == 0:
                 for u in range(2):
                     quantise(x_r_codes[u][:], x_r_scales[u][:], x_r[:, half(u), :], E4M3)
-            if t == 1:
-                quantise(x_d_codes[:], x_d_scales[:], x_d[:], E4M3)
-                for k in (1, 0, 3, 2):
-                    nc.scalar.copy(w_by_column[k][:, :, 0:2, :], w_by_plane[0][:, groups(k)])
-        quantise(w_i_early[:], w_i_scales[:, half(0)], w_i[:, half(0), :], E4M3)
+        quantise(x_d_codes[:], x_d_scales[:], x_d[:], E4M3)
+        for k in NEGATIVES_FIRST:
+            nc.scalar.copy(w_by_column[k][:, :, 0:2, :], w_by_plane[0][:, groups(k)])
+        nc.vector.tensor_copy(w_planes[1][:, 0, :], v_plane[2][:].indirect(item_list[:]))
+        third_turned = turn_plane(w_planes[1][:, 0, :], 6)
 
         w_d_codes = {}
+        for k in NEGATIVES_FIRST:
+            entries = item_list[:, k * QUARTER_COLS : (k + 1) * QUARTER_COLS]
+            move_listed(k // 2, w_planes[1][:, 1, quarter(k)], v_plane[PACK - 1][:].indirect(entries))
+            move(k // 2, w_by_column[k][:, :, 2:PACK, :], w_by_plane[1][:, groups(k)])
+            w_d_codes[k] = sbuf("w_d_codes%d" % k, [P, P], U32)
+            quantise(w_d_codes[k][:], w_d_scales[:, quarter(k)], w_d[:, k], E4M3)
+        w_i_codes = [sbuf("w_i_codes0", [P, HALF], U32, tag="w_d")]
+        quantise(w_i_codes[0][:], w_i_scales[:, half(0)], w_i[0][:], E4M3)
+
+        def score(k, users, number):
+            sums = flat(bank(number)[:])[:, users]
+            return multiply(
+                sums, w_d_codes[k][:], w_d_scales[:, quarter(k)], x_d_codes[:, users], x_d_scales[:, users], E4M3
+            )
+
         margin = sbuf("margin", [P, 2, N], F32)
         q = [sbuf("q%d" % c, [P, P // PACK, PACK, PACK], F32) for c in range(2)]
-        h_r = sbuf("h_r", [P, N, PACK], BF16)
 
-        def finish_items(k):
-            c, a = divmod(k, 2)
-            listed = w_listed[1][:, 1, block(k)]
-            window = v_plane[PACK - 1][:].indirect(item_entries(c, a))
-            if a:
-                nc.vector.tensor_copy(listed, window)
-                nc.vector.tensor_copy(w_by_column[k][:, :, 2:PACK, :], w_by_plane[1][:, groups(k)])
-            else:
-                nc.scalar.activation(listed, window, COPY)
-                nc.scalar.copy(w_by_column[k][:, :, 2:PACK, :], w_by_plane[1][:, groups(k)])
-
-        def quantise_items(k):
-            w_d_codes[k] = sbuf("w_d_codes%d" % k, [P, P], U32)
-            quantise(w_d_codes[k][:], w_d_scales[:, block(k)], w_d[k], E4M3)
-
-        def score_bank(c, u, a):
-            return PACK * (1 - c) + 2 * u + 1 - a
-
-        def score(c, u, a):
-            scores = flat(bank(score_bank(c, u, a))[:])[:, 0:HALF]
-            nc.tensor.matmul_mx(
-                out=scores,
-                lhsT=w_d_codes[2 * c + a][:].bitcast(E4M3),
-                lhsT_scale=w_d_scales[:, block(2 * c + a)],
-                rhs=x_d_codes[:, half(u)].bitcast(E4M3),
-                rhs_scale=x_d_scales[:, half(u)],
-                start=True,
-                stop=True,
-            )
-            return scores
-
-        def scale_negatives(c, u):
-            if c + u:
-                negative = sbuf("negative%d" % (2 * c + u), [P, HALF], F32)[:]
-            else:
-                negative = w_listed[1][:, 0, :].bitcast(F32)
-            nc.scalar.activation(negative, score(c, u, 1), COPY, scale=ts_column[:, c, 1:2])
-            return negative
-
-        def subtract(c, u, negative):
-            nc.vector.scalar_tensor_tensor(
-                margin[:, c, half(u)], score(c, u, 0), ts_column[:, c, 0:1], negative, MULT, ADD
-            )
-
-        def weigh(c, u):
-            turned = bank(score_bank(c, u, 1))
-            for e in range(2):
-                nc.tensor.transpose(turned[:, e, :], margin[:, c, block(2 * u + e)], ident_f32[:])
-            for e in range(2):
-                s = 2 * u + e
-                nc.scalar.activation(
-                    q[c][:, :, s, :],
-                    turned[:, e, :].rearrange("p (g i) -> p g i", i=PACK),
-                    SIGMOID,
-                    scale=row_scale[:, s : s + 1],
+        def weigh(c, negative_scores, positive_banks, turn_banks):
+            negative = []
+            for u in range(2):
+                if c + u:
+                    negative.append(sbuf("negative%d" % (2 * c + u), [P, HALF], F32)[:])
+                else:
+                    negative.append(w_planes[1][:, 0, :].bitcast(F32))
+                nc.scalar.activation(negative[u], negative_scores(u), COPY, scale=ts_column[:, 2 + c : 3 + c])
+            for u in range(2):
+                positive = score(c, half(u), positive_banks[u])
+                nc.vector.scalar_tensor_tensor(
+                    margin[:, c, half(u)], positive, ts_column[:, c : c + 1], negative[u], MULT, ADD
                 )
+            for u in range(2):
+                turned = bank(turn_banks[u])
+                for e in range(2):
+                    nc.tensor.transpose(turned[:, e, :], margin[:, c, quarter(2 * u + e)], ident_f32[:])
+                for e in range(2):
+                    s = 2 * u + e
+                    nc.scalar.activation(
+                        q[c][:, :, s, :],
+                        turned[:, e, :].rearrange("p (g i) -> p g i", i=PACK),
+                        SIGMOID,
+                        scale=row_scale[:, s : s + 1],
+                    )
 
+        first_negatives = score(2, slice(0, N), 4)
+        weigh(0, lambda u: first_negatives[:, half(u)], (5, 7), (4, 7))
+        weigh(1, lambda u: score(3, half(u), 2 * u), (1, 3), (0, 2))
+
+        w_i.append(sbuf("w_i1", [P, HALF, PACK], BF16, tag="margin"))
+        lay_turned(w_i[1][:, quarter(0), :], third_turned)
+        lay_turned(w_i[1][:, quarter(1), :], turn_plane(w_planes[1][:, 1, :], 3))
+
+        h_r = sbuf("h_r", [P, N, PACK], BF16)
         h_r_codes = sbuf("h_r_codes", [P, N], U32)
         h_r_scales = sbuf("h_r_scales", [P, N], U8)
 
         def gradient(k, parts=1):
-            columns = h_r[:, block(k), :].rearrange("p (g i) s -> p g s i", i=PACK)
+            columns = h_r[:, quarter(k), :].rearrange("p (g i) s -> p g s i", i=PACK)
             for part in range(parts):
                 some = slice(part * P // PACK // parts, (part + 1) * P // PACK // parts)
-                nc.vector.tensor_tensor(columns[:, some], q[k // 2][:, some], signed[:, groups(k)][:, some], MULT)
+                nc.vector.tensor_tensor(columns[:, some], q[k % 2][:, some], signed[:, groups(k)][:, some], MULT)
 
         def quantise_gradient(k):
-            c, a = divmod(k, 2)
-            in_list = block(2 * a + c)
-            quantise(h_r_codes[:, in_list], h_r_scales[:, in_list], h_r[:, block(k), :], E5M2)
+            quantise(h_r_codes[:, quarter(k)], h_r_scales[:, quarter(k)], h_r[:, quarter(k), :], E5M2)
 
-        def product(sums, codes, scales, h_codes, h_scales):
-            nc.tensor.matmul_mx(
-                out=sums,
-                lhsT=codes.bitcast(E4M3),
-                lhsT_scale=scales,
-                rhs=h_codes.bitcast(E5M2),
-                rhs_scale=h_scales,
-                start=True,
-                stop=True,
-            )
-
-        def item_sums(t, columns, sums):
-            rows = block(t % 2)
-            product(
-                sums,
-                x_r_codes[t // 2][:, rows],
-                x_r_scales[t // 2][:, rows],
-                h_r_codes[:, columns],
-                h_r_scales[:, columns],
-            )
-            return sums
-
-        def copy_out(u, values, sums):
-            if u:
-                nc.vector.tensor_copy(values, sums)
-            else:
-                nc.scalar.copy(values, sums)
+        def item_sums(t, slots, sums):
+            rows = quarter(t % 2)
+            codes, scales = x_r_codes[t // 2][:, rows], x_r_scales[t // 2][:, rows]
+            return multiply(sums, codes, scales, h_r_codes[:, slots], h_r_scales[:, slots], E5M2)
 
         def put(dram, t, window, entries, halves):
-            nc.scalar.activation(window[:].indirect(entries[:, 0:HALF_COLS]), halves[0], COPY)
-            nc.vector.tensor_copy(window[:].indirect(entries[:, HALF_COLS:]), halves[1])
+            for u in range(2):
+                move_listed(u, window[:].indirect(entries[:, u * HALF_COLS : (u + 1) * HALF_COLS]), halves[u])
             nc.sync.dma_start(planes(dram)[:, t, :], window[:])
 
         dv = {}
 
-        positives = sbuf("positives", [P, 2, HALF], F32)
-        for t in range(2):
-            dv[t, 0] = positives[:, t, :]
-
-        def stage_first_positives():
-            sums = bank(PACK + 2)
-            for t in range(2):
-                item_sums(t, block(0), sums[:, t, :])
-            nc.scalar.copy(positives[:, :, block(0)], sums[:, 0:2, :])
-
-        def stage_last_positives(t, number):
-            nc.scalar.copy(positives[:, t, block(1)], item_sums(t, block(1), bank(number)[:, 0, :]))
-
-        def stage_negatives(t):
-            values = sbuf("negatives%d" % t, [P, HALF], F32)
-            nc.vector.tensor_copy(values[:], item_sums(t, half(1), flat(bank(t)[:, 0:2, :])))
-            dv[t, 1] = values[:]
-
-        def stage_item_plane(t, sums, tags):
-            for a in range(2):
-                values = sbuf("dv%d_%d" % (t, a), [P, HALF], F32, tag=tags[a])
-                copy_out(a, values[:], sums[:, half(a)])
-                dv[t, a] = values[:]
+        def stage_items(t, a, sums, tag=""):
+            values = sbuf("dv%d_%d" % (t, a), [P, HALF], F32, tag=tag)
+            move(a, values[:], sums)
+            dv[t, a] = values[:]
 
         def put_items(t):
             put(out_0, t, dv_window[t], item_list, (dv[t, 0], dv[t, 1]))
 
+        positives = sbuf("positives", [P, 2, HALF], F32)
+        for k in range(2):
+            gradient(k)
+        quantise_gradient(0)
+        early = bank(6)
+        for t in range(2):
+            item_sums(t, quarter(0), early[:, t, :])
+            dv[t, 0] = positives[:, t, :]
+        nc.scalar.copy(positives[:, :, quarter(0)], early[:, 0:2, :])
+        quantise_gradient(1)
+        for t in range(2):
+            nc.scalar.copy(positives[:, t, quarter(1)], item_sums(t, quarter(1), bank(PACK + t)[:, 0, :]))
+
+        gradient(2, parts=PACK)
+        gradient(3)
+        for k in (2, 3):
+            quantise_gradient(k)
+        for t in (0, 1, 3):
+            stage_items(t, 1, item_sums(t, half(1), flat(bank(t)[:, 0:2, :])))
+        w_i_codes.append(sbuf("w_i_codes1", [P, HALF], U32, tag="signed"))
+        quantise(w_i_codes[1][:], w_i_scales[:, half(1)], w_i[1][:], E4M3)
+
+        du_window = [zeroed_window("du_window%d" % t, tag) for t, tag in enumerate(("x_r_codes0", "x_r_scales0"))]
+        for t in range(2):
+            put_items(t)
+
         h_i = sbuf("h_i", [P, N, PACK], BF16)
         h_i_codes = sbuf("h_i_codes", [P, N], U32)
         h_i_scales = sbuf("h_i_scales", [P, N], U8)
-        w_i_codes = [w_i_early[:, 0:P], w_i_early[:, P:]]
+        third = item_sums(2, slice(0, N), flat(bank(2)[:]))
+        h_words = flat(h_r[:]).bitcast(F32).rearrange("p (m k u) -> p k u m", k=PACK, u=2)
+        for u in range(2):
+            turned = bank(u)
+            for k in range(PACK):
+                nc.tensor.transpose(turned[:, k, :], h_words[:, k, u, :], ident_f32[:])
+            move(
+                u,
+                h_i[:, half(u), :].rearrange("p (e c) k -> p e c k", e=2),
+                flat(turned[:]).bitcast(BF16).rearrange("p (k c e) -> p e c k", k=PACK, e=2),
+            )
+        for a, tag in enumerate(("h_r", "ident_f32")):
+            stage_items(2, a, third[:, half(a)], tag)
+        quantise(h_i_codes[:], h_i_scales[:], h_i[:], E5M2)
+        put_items(2)
+        stage_items(3, 0, item_sums(3, half(0), flat(bank(0)[:, 0:2, :])))
+        put_items(3)
+        du_window.extend([zeroed_window("du_window%d" % (2 + e), tag) for e, tag in enumerate(("h_i", "h_i_scales"))])
 
         du = {}
 
         def stage_users(t):
             sums = bank(PACK + t)
-            product(flat(sums[:]), w_i_codes[t], w_i_scales[:, block(t)], h_i_codes[:], h_i_scales[:])
+            codes = w_i_codes[t // 2][:, quarter(t % 2)]
+            multiply(flat(sums[:]), codes, w_i_scales[:, quarter(t)], h_i_codes[:], h_i_scales[:], E5M2)
             for u in range(2):
                 values = sbuf("du%d_%d" % (t, u), [P, HALF], F32, tag="du%d_%d" % (t % 2, u))
                 some = sums[:, :, u * P // 2 : (u + 1) * P // 2].rearrange("p s m -> p m s")
-                copy_out(u, values[:].rearrange("p (m s) -> p m s", s=PACK), some)
+                move(u, values[:].rearrange("p (m s) -> p m s", s=PACK), some)
                 du[t, u] = values[:]
 
-        def put_users(t):
-            put(out_1, t, du_window[t], user_list, (du[t, 0], du[t, 1]))
-
-        def zero_user_window(tag):
-            window = sbuf("du_window%d" % len(du_window), [P, T], F32, tag=tag)
-            nc.gpsimd.memset(window[:].bitcast(I32), 0)
-            du_window.append(window)
-
-        def turn_pairs(u, number):
-            turned = bank(number)
-            words = flat(h_r[:]).bitcast(F32).rearrange("p (m k u) -> p k u m", k=PACK, u=2)
-            for k in range(PACK):
-                nc.tensor.transpose(turned[:, k, :], words[:, k, u, :], ident_f32[:])
-            laid = h_i[:, half(u), :].rearrange("p (e c) k -> p e c k", e=2)
-            pairs = flat(turned[:]).bitcast(BF16).rearrange("p (k c e) -> p e c k", k=PACK, e=2)
-            copy_out(u, laid, pairs)
-
-        for k in (1, 0, 3, 2):
-            finish_items(k)
-            quantise_items(k)
-        for c in range(2):
-            negatives = [scale_negatives(c, u) for u in range(2)]
-            for u in range(2):
-                subtract(c, u, negatives[u])
-            for u in range(2):
-                weigh(c, u)
-        lay_turned(w_i[:, block(PACK - 1), :], turn_plane(w_listed, PACK - 1, score_bank(1, 1, 0)))
-        for k in (0, 2):
-            gradient(k)
-        quantise_gradient(0)
-        stage_first_positives()
-        quantise_gradient(2)
-        for t in range(2):
-            stage_last_positives(t, PACK + t)
-        gradient(1, parts=PACK)
-        gradient(3)
-        for k in (1, 3):
-            quantise_gradient(k)
-        for t in (0, 1, 3):
-            stage_negatives(t)
-        w_i_late = sbuf("w_i_late", [P, HALF], U32, tag="signed")
-        quantise(w_i_late[:], w_i_scales[:, half(1)], w_i[:, half(1), :], E4M3)
-        w_i_codes.extend([w_i_late[:, 0:P], w_i_late[:, P:]])
-        for tag in ("x_r_codes0", "x_r_scales0"):
-            zero_user_window(tag)
-        for t in range(2):
-            put_items(t)
-        for u in range(2):
-            turn_pairs(u, u)
-        third = item_sums(2, slice(0, N), flat(bank(2)[:]))
-        stage_item_plane(2, third, ("h_r", "ident_f32"))
-        quantise(h_i_codes[:], h_i_scales[:], h_i[:], E5M2)
-        put_items(2)
-        last = sbuf("last_positives", [P, HALF], F32)
-        nc.scalar.copy(last[:], item_sums(3, half(0), flat(bank(0)[:, 0:2, :])))
-        dv[3, 0] = last[:]
-        put_items(3)
-        for tag in ("h_i", "h_i_scales"):
-            zero_user_window(tag)
         for t in range(2):
             stage_users(t)
         for t in range(PACK):
-            put_users(t)
-            if t < 2:
+            put(out_1, t, du_window[t], user_list, (du[t, 0], du[t, 1]))
+            if t + 2 < PACK:
                 stage_users(t + 2)

@@ -258,10 +258,10 @@ def tile_attend_gmf_bpr_vu_kernel(tc, uT, vT, us, ts, offs, uoffs, out_0, out_1)
 
         dv = {}
 
-        def stage_items(t, a, sums, tag=""):
-            values = sbuf("dv%d_%d" % (t, a), [P, HALF], F32, tag=tag)
-            move(a, values[:], sums)
-            dv[t, a] = values[:]
+        def stage_negatives(t, sums, on_vector, tag=""):
+            values = sbuf("negatives%d" % t, [P, HALF], F32, tag=tag)
+            move(on_vector, values[:], sums)
+            dv[t, 1] = values[:]
 
         def put_items(t):
             put(out_0, t, dv_window[t], item_list, (dv[t, 0], dv[t, 1]))
@@ -283,8 +283,10 @@ def tile_attend_gmf_bpr_vu_kernel(tc, uT, vT, us, ts, offs, uoffs, out_0, out_1)
         gradient(3)
         for k in (2, 3):
             quantise_gradient(k)
-        for t in (0, 1, 3):
-            stage_items(t, 1, item_sums(t, half(1), flat(bank(t)[:, 0:2, :])))
+        for t in range(2):
+            stage_negatives(t, item_sums(t, half(1), flat(bank(t)[:, 0:2, :])), True)
+        third = item_sums(2, slice(0, N), flat(bank(2)[:]))
+        stage_negatives(2, third[:, half(1)], True)
         w_i_codes.append(sbuf("w_i_codes1", [P, HALF], U32, tag="signed"))
         quantise(w_i_codes[1][:], w_i_scales[:, half(1)], w_i[1][:], E4M3)
 
@@ -295,7 +297,7 @@ def tile_attend_gmf_bpr_vu_kernel(tc, uT, vT, us, ts, offs, uoffs, out_0, out_1)
         h_i = sbuf("h_i", [P, N, PACK], BF16)
         h_i_codes = sbuf("h_i_codes", [P, N], U32)
         h_i_scales = sbuf("h_i_scales", [P, N], U8)
-        third = item_sums(2, slice(0, N), flat(bank(2)[:]))
+        fourth = item_sums(3, slice(0, N), flat(bank(3)[:]))
         h_words = flat(h_r[:]).bitcast(F32).rearrange("p (m k u) -> p k u m", k=PACK, u=2)
         for u in range(2):
             turned = bank(u)
@@ -306,11 +308,14 @@ def tile_attend_gmf_bpr_vu_kernel(tc, uT, vT, us, ts, offs, uoffs, out_0, out_1)
                 h_i[:, half(u), :].rearrange("p (e c) k -> p e c k", e=2),
                 flat(turned[:]).bitcast(BF16).rearrange("p (k c e) -> p e c k", k=PACK, e=2),
             )
-        for a, tag in enumerate(("h_r", "ident_f32")):
-            stage_items(2, a, third[:, half(a)], tag)
-        quantise(h_i_codes[:], h_i_scales[:], h_i[:], E5M2)
+        late_positives = sbuf("late_positives", [P, 2, HALF], F32, tag="h_r")
+        for e, sums in enumerate((third, fourth)):
+            nc.scalar.copy(late_positives[:, e, :], sums[:, half(0)])
+            dv[2 + e, 0] = late_positives[:, e, :]
+        for u in range(2):
+            quantise(h_i_codes[:, half(u)], h_i_scales[:, half(u)], h_i[:, half(u), :], E5M2)
         put_items(2)
-        stage_items(3, 0, item_sums(3, half(0), flat(bank(0)[:, 0:2, :])))
+        stage_negatives(3, fourth[:, half(1)], False, tag="ident_f32")
         put_items(3)
         du_window.extend([zeroed_window("du_window%d" % (2 + e), tag) for e, tag in enumerate(("h_i", "h_i_scales"))])
 

@@ -23,8 +23,6 @@ P = 128
 PACK = 4
 HALF = N // 2
 COLS = N // 16
-QUARTER_COLS = P // 16
-HALF_COLS = COLS // 2
 NEGATIVES_FIRST = (2, 0, 3, 1)
 
 
@@ -43,8 +41,23 @@ def tile_attend_gmf_bpr_vu_kernel(tc, uT, vT, us, ts, offs, uoffs, out_0, out_1)
         def planes(dram):
             return dram.rearrange("(p t) n -> p t n", t=PACK)
 
+        def flat(ap):
+            return ap.rearrange("p a b -> p (a b)")
+
+        def quarter(k):
+            return slice(k * P, (k + 1) * P)
+
+        def half(a):
+            return slice(a * HALF, (a + 1) * HALF)
+
+        def groups(k):
+            return slice(k * P // PACK, (k + 1) * P // PACK)
+
+        def entries(listed, part, parts):
+            return listed[:, part * COLS // parts : (part + 1) * COLS // parts]
+
         def quantise(codes, scales, values, fmt):
-            nc.vector.quantize_mx(out=codes.bitcast(fmt), scales=scales, in_=values.rearrange("p c t -> p (c t)"))
+            nc.vector.quantize_mx(out=codes.bitcast(fmt), scales=scales, in_=flat(values))
 
         def multiply(sums, codes, scales, moving_codes, moving_scales, moving_fmt):
             nc.tensor.matmul_mx(
@@ -70,34 +83,22 @@ def tile_attend_gmf_bpr_vu_kernel(tc, uT, vT, us, ts, offs, uoffs, out_0, out_1)
             else:
                 nc.scalar.activation(dst, src, COPY)
 
-        def flat(ap):
-            return ap.rearrange("p a b -> p (a b)")
-
-        def quarter(k):
-            return slice(k * P, (k + 1) * P)
-
-        def half(u):
-            return slice(u * HALF, (u + 1) * HALF)
-
-        def groups(k):
-            return slice(k * P // PACK, (k + 1) * P // PACK)
-
         warm = sbuf("warm", [P, 8], F32)
         nc.gpsimd.memset(warm[:], 0.0)
         nc.scalar.activation(warm[:], warm[:], SIGMOID)
 
-        ident_f32 = sbuf("ident_f32", [P, P], F32)
-        make_identity(nc, ident_f32[:])
+        ident = sbuf("ident", [P, P], F32)
+        make_identity(nc, ident[:])
 
         user_list = keep.tile([P, COLS], U16, name="user_list")
         item_list = keep.tile([P, COLS], U16, name="item_list")
         u_plane = [sbuf("u_plane%d" % t, [P, T], F32) for t in range(PACK)]
         v_plane = [sbuf("v_plane%d" % t, [P, T], F32) for t in range(PACK)]
+        ts_row = sbuf("ts_row", [P, T], F32)
+        row_scale = sbuf("row_scale", [P, PACK], F32)
         nc.sync.dma_start(item_list[:], offs)
         nc.sync.dma_start(u_plane[0][:], planes(uT)[:, 0, :])
         nc.sync.dma_start(user_list[:], uoffs)
-        ts_row = sbuf("ts_row", [P, T], F32)
-        row_scale = sbuf("row_scale", [P, PACK], F32)
         nc.scalar.dma_start(ts_row[P - 1 : P, :], ts[0:1, :])
         nc.scalar.dma_start(row_scale[:], us.rearrange("b (p t) o -> p (b t o)", t=PACK))
         nc.gpsimd.memset(ts_row[0 : P - 1, :].bitcast(I32), 0)
@@ -117,13 +118,13 @@ def tile_attend_gmf_bpr_vu_kernel(tc, uT, vT, us, ts, offs, uoffs, out_0, out_1)
         nc.vector.tensor_copy(ts_listed[:], ts_row[:].indirect(item_list[:]))
         ts_turned = bank(0)
         for k in range(PACK):
-            nc.tensor.transpose(ts_turned[:, k, :], ts_listed[:, quarter(k)], ident_f32[:])
+            nc.tensor.transpose(ts_turned[:, k, :], ts_listed[:, quarter(k)], ident[:])
         ts_column = sbuf("ts_column", [P, PACK], F32)
         nc.scalar.activation(ts_column[:, 0:2], ts_turned[:, 0:2, P - 1], COPY, scale=-1.0)
         nc.scalar.activation(ts_column[:, 2:PACK], ts_turned[:, 2:PACK, P - 1], COPY)
         ts_spread = bank(1)
         for k in range(PACK):
-            nc.tensor.transpose(ts_spread[:, k, :], ts_column[:, k : k + 1].to_broadcast([P, P]), ident_f32[:])
+            nc.tensor.transpose(ts_spread[:, k, :], ts_column[:, k : k + 1].to_broadcast([P, P]), ident[:])
         signed = sbuf("signed", [P, N // PACK, PACK, PACK], F32)
         for s in range(PACK):
             nc.scalar.activation(
@@ -137,11 +138,12 @@ def tile_attend_gmf_bpr_vu_kernel(tc, uT, vT, us, ts, offs, uoffs, out_0, out_1)
             words = plane.bitcast(F32).rearrange("p (m u) -> p u m", u=2)
             turned = bank(number)
             for u in range(2):
-                nc.tensor.transpose(turned[:, u, :], words[:, u, :], ident_f32[:])
+                nc.tensor.transpose(turned[:, u, :], words[:, u, :], ident[:])
             return turned
 
-        def lay_turned(dst, turned):
-            nc.scalar.copy(
+        def lay_turned(on_vector, dst, turned):
+            move(
+                on_vector,
                 flat(dst).bitcast(F32).rearrange("p (c u) -> p c u", u=2),
                 turned[:, 0:2, :].rearrange("p u c -> p c u"),
             )
@@ -149,10 +151,10 @@ def tile_attend_gmf_bpr_vu_kernel(tc, uT, vT, us, ts, offs, uoffs, out_0, out_1)
         x_planes = sbuf("x_planes", [P, PACK, N], BF16)
         x_d = sbuf("x_d", [P, N, PACK], BF16)
         x_r = sbuf("x_r", [P, D, PACK], BF16)
-        x_by_column = x_d[:].rearrange("p (s m) t -> p m s t", s=PACK)
         for t in range(PACK):
             nc.vector.tensor_copy(x_planes[:, t, :], u_plane[t][:].indirect(user_list[:]))
-            lay_turned(x_r[:, quarter(t), :], turn_plane(x_planes[:, t, :], PACK + t))
+            lay_turned(False, x_r[:, quarter(t), :], turn_plane(x_planes[:, t, :], PACK + t))
+        x_by_column = x_d[:].rearrange("p (s m) t -> p m s t", s=PACK)
         x_by_plane = x_planes[:].rearrange("p t (m s) -> p m s t", s=PACK)
         for k in range(PACK):
             nc.scalar.copy(x_by_column[:, groups(k)], x_by_plane[:, groups(k)])
@@ -164,34 +166,45 @@ def tile_attend_gmf_bpr_vu_kernel(tc, uT, vT, us, ts, offs, uoffs, out_0, out_1)
         w_planes = [sbuf("w_planes%d" % u, [P, 2, N], BF16) for u in range(2)]
         w_d = sbuf("w_d", [P, PACK, P, PACK], BF16)
         w_d_scales = sbuf("w_d_scales", [P, N], U8)
-        w_i = [sbuf("w_i0", [P, HALF, PACK], BF16)]
+        w_i = sbuf("w_i", [P, HALF, PACK], BF16)
+        early_codes = sbuf("early_codes", [P, HALF], U32, tag="v_plane2")
+        w_i_codes = [early_codes[:, quarter(t)] for t in range(2)]
         w_i_scales = sbuf("w_i_scales", [P, D], U8)
         w_by_column = [w_d[:, k].rearrange("p (g i) t -> p g t i", i=PACK) for k in range(PACK)]
         w_by_plane = [pair[:].rearrange("p t (g i) -> p g t i", i=PACK) for pair in w_planes]
         for t in range(2):
             nc.vector.tensor_copy(w_planes[0][:, t, :], v_plane[t][:].indirect(item_list[:]))
-            lay_turned(w_i[0][:, quarter(t), :], turn_plane(w_planes[0][:, t, :], 2 + t))
+            lay_turned(False, w_i[:, quarter(t), :], turn_plane(w_planes[0][:, t, :], 2 + t))
             if t == 0:
                 for u in range(2):
                     quantise(x_r_codes[u][:], x_r_scales[u][:], x_r[:, half(u), :], E4M3)
-        quantise(x_d_codes[:], x_d_scales[:], x_d[:], E4M3)
-        for k in NEGATIVES_FIRST:
-            nc.scalar.copy(w_by_column[k][:, :, 0:2, :], w_by_plane[0][:, groups(k)])
+            if t == 1:
+                quantise(x_d_codes[:], x_d_scales[:], x_d[:], E4M3)
+                for k in NEGATIVES_FIRST:
+                    nc.scalar.copy(w_by_column[k][:, :, 0:2, :], w_by_plane[0][:, groups(k)])
         nc.vector.tensor_copy(w_planes[1][:, 0, :], v_plane[2][:].indirect(item_list[:]))
-        third_turned = turn_plane(w_planes[1][:, 0, :], 6)
+        third_turned = turn_plane(w_planes[1][:, 0, :], 7)
+        quantise(early_codes[:], w_i_scales[:, half(0)], w_i[:], E4M3)
 
         w_d_codes = {}
         for k in NEGATIVES_FIRST:
-            entries = item_list[:, k * QUARTER_COLS : (k + 1) * QUARTER_COLS]
-            move_listed(k // 2, w_planes[1][:, 1, quarter(k)], v_plane[PACK - 1][:].indirect(entries))
+            move_listed(k // 2, w_planes[1][:, 1, quarter(k)], v_plane[PACK - 1][:].indirect(entries(item_list, k, PACK)))
             move(k // 2, w_by_column[k][:, :, 2:PACK, :], w_by_plane[1][:, groups(k)])
             w_d_codes[k] = sbuf("w_d_codes%d" % k, [P, P], U32)
             quantise(w_d_codes[k][:], w_d_scales[:, quarter(k)], w_d[:, k], E4M3)
-        w_i_codes = [sbuf("w_i_codes0", [P, HALF], U32, tag="w_d")]
-        quantise(w_i_codes[0][:], w_i_scales[:, half(0)], w_i[0][:], E4M3)
 
-        def score(k, users, number):
-            sums = flat(bank(number)[:])[:, users]
+        def late_plane(t, on_vector, turned, tag, codes_tag=""):
+            laid = sbuf("w_i%d" % t, [P, P, PACK], BF16, tag=tag)
+            lay_turned(on_vector, laid[:], turned)
+            codes = sbuf("w_i_codes%d" % t, [P, P], U32, tag=codes_tag)
+            quantise(codes[:], w_i_scales[:, quarter(t)], laid[:], E4M3)
+            w_i_codes.append(codes[:])
+
+        late_plane(2, False, third_turned, "", "w_d")
+
+        def score(k, u, number):
+            sums = flat(bank(number)[:, 0:2, :])
+            users = half(u)
             return multiply(
                 sums, w_d_codes[k][:], w_d_scales[:, quarter(k)], x_d_codes[:, users], x_d_scales[:, users], E4M3
             )
@@ -199,39 +212,40 @@ def tile_attend_gmf_bpr_vu_kernel(tc, uT, vT, us, ts, offs, uoffs, out_0, out_1)
         margin = sbuf("margin", [P, 2, N], F32)
         q = [sbuf("q%d" % c, [P, P // PACK, PACK, PACK], F32) for c in range(2)]
 
-        def weigh(c, negative_scores, positive_banks, turn_banks):
-            negative = []
-            for u in range(2):
-                if c + u:
-                    negative.append(sbuf("negative%d" % (2 * c + u), [P, HALF], F32)[:])
-                else:
-                    negative.append(w_planes[1][:, 0, :].bitcast(F32))
-                nc.scalar.activation(negative[u], negative_scores(u), COPY, scale=ts_column[:, 2 + c : 3 + c])
-            for u in range(2):
-                positive = score(c, half(u), positive_banks[u])
-                nc.vector.scalar_tensor_tensor(
-                    margin[:, c, half(u)], positive, ts_column[:, c : c + 1], negative[u], MULT, ADD
+        def scaled_negatives(c, u):
+            if c + u:
+                negative = sbuf("negative%d" % (2 * c + u), [P, HALF], F32)[:]
+            else:
+                negative = w_planes[1][:, 0, :].bitcast(F32)
+            nc.scalar.activation(negative, score(2 + c, u, PACK * c + 2 * u), COPY, scale=ts_column[:, 2 + c : 3 + c])
+            return negative
+
+        def add_positives(c, u, negative):
+            positive = score(c, u, PACK * c + 2 * u + 1)
+            nc.vector.scalar_tensor_tensor(margin[:, c, half(u)], positive, ts_column[:, c : c + 1], negative, MULT, ADD)
+
+        def weigh(c, u):
+            turned = bank(PACK * c + 2 * u)
+            for e in range(2):
+                nc.tensor.transpose(turned[:, e, :], margin[:, c, quarter(2 * u + e)], ident[:])
+            for e in range(2):
+                s = 2 * u + e
+                nc.scalar.activation(
+                    q[c][:, :, s, :],
+                    turned[:, e, :].rearrange("p (g i) -> p g i", i=PACK),
+                    SIGMOID,
+                    scale=row_scale[:, s : s + 1],
                 )
-            for u in range(2):
-                turned = bank(turn_banks[u])
-                for e in range(2):
-                    nc.tensor.transpose(turned[:, e, :], margin[:, c, quarter(2 * u + e)], ident_f32[:])
-                for e in range(2):
-                    s = 2 * u + e
-                    nc.scalar.activation(
-                        q[c][:, :, s, :],
-                        turned[:, e, :].rearrange("p (g i) -> p g i", i=PACK),
-                        SIGMOID,
-                        scale=row_scale[:, s : s + 1],
-                    )
 
-        first_negatives = score(2, slice(0, N), 4)
-        weigh(0, lambda u: first_negatives[:, half(u)], (5, 7), (4, 7))
-        weigh(1, lambda u: score(3, half(u), 2 * u), (1, 3), (0, 2))
-
-        w_i.append(sbuf("w_i1", [P, HALF, PACK], BF16, tag="margin"))
-        lay_turned(w_i[1][:, quarter(0), :], third_turned)
-        lay_turned(w_i[1][:, quarter(1), :], turn_plane(w_planes[1][:, 1, :], 3))
+        for u in range(2):
+            add_positives(0, u, scaled_negatives(0, u))
+        late = [scaled_negatives(1, u) for u in range(2)]
+        for u in range(2):
+            weigh(0, u)
+        for u in range(2):
+            add_positives(1, u, late[u])
+        for u in range(2):
+            weigh(1, u)
 
         h_r = sbuf("h_r", [P, N, PACK], BF16)
         h_r_codes = sbuf("h_r_codes", [P, N], U32)
@@ -251,89 +265,89 @@ def tile_attend_gmf_bpr_vu_kernel(tc, uT, vT, us, ts, offs, uoffs, out_0, out_1)
             codes, scales = x_r_codes[t // 2][:, rows], x_r_scales[t // 2][:, rows]
             return multiply(sums, codes, scales, h_r_codes[:, slots], h_r_scales[:, slots], E5M2)
 
-        def put(dram, t, window, entries, halves):
-            for u in range(2):
-                move_listed(u, window[:].indirect(entries[:, u * HALF_COLS : (u + 1) * HALF_COLS]), halves[u])
-            nc.sync.dma_start(planes(dram)[:, t, :], window[:])
+        def scatter(a, window, listed, values):
+            move_listed(a, window[:].indirect(entries(listed, a, 2)), values)
 
-        dv = {}
-
-        def stage_negatives(t, sums, on_vector, tag=""):
-            values = sbuf("negatives%d" % t, [P, HALF], F32, tag=tag)
-            move(on_vector, values[:], sums)
-            dv[t, 1] = values[:]
-
-        def put_items(t):
-            put(out_0, t, dv_window[t], item_list, (dv[t, 0], dv[t, 1]))
-
-        positives = sbuf("positives", [P, 2, HALF], F32)
+        positives = [sbuf("positives0", [P, 2, HALF], F32)]
         for k in range(2):
             gradient(k)
         quantise_gradient(0)
-        early = bank(6)
+        early = bank(1)
         for t in range(2):
             item_sums(t, quarter(0), early[:, t, :])
-            dv[t, 0] = positives[:, t, :]
-        nc.scalar.copy(positives[:, :, quarter(0)], early[:, 0:2, :])
+        nc.scalar.copy(positives[0][:, :, quarter(0)], early[:, 0:2, :])
         quantise_gradient(1)
         for t in range(2):
-            nc.scalar.copy(positives[:, t, quarter(1)], item_sums(t, quarter(1), bank(PACK + t)[:, 0, :]))
+            nc.scalar.copy(positives[0][:, t, quarter(1)], item_sums(t, quarter(1), bank(5 + 2 * t)[:, 0, :]))
 
         gradient(2, parts=PACK)
         gradient(3)
         for k in (2, 3):
             quantise_gradient(k)
+        negatives = [sbuf("negatives%d" % u, [P, 2, HALF], F32) for u in range(2)]
         for t in range(2):
-            stage_negatives(t, item_sums(t, half(1), flat(bank(t)[:, 0:2, :])), True)
-        third = item_sums(2, slice(0, N), flat(bank(2)[:]))
-        stage_negatives(2, third[:, half(1)], True)
-        w_i_codes.append(sbuf("w_i_codes1", [P, HALF], U32, tag="signed"))
-        quantise(w_i_codes[1][:], w_i_scales[:, half(1)], w_i[1][:], E4M3)
+            nc.vector.tensor_copy(negatives[0][:, t, :], item_sums(t, half(1), flat(bank(2 * t)[:, 0:2, :])))
+        pair = bank(4)
+        for e in range(2):
+            item_sums(2 + e, half(1), flat(pair[:, 2 * e : 2 * e + 2, :]))
+        nc.vector.tensor_copy(flat(negatives[1][:]), flat(pair[:]))
 
+        late_plane(3, False, turn_plane(w_planes[1][:, 1, :], 3), "margin", "signed")
         du_window = [zeroed_window("du_window%d" % t, tag) for t, tag in enumerate(("x_r_codes0", "x_r_scales0"))]
+
+        def put_items(t):
+            scatter(0, dv_window[t], item_list, positives[t // 2][:, t % 2, :])
+            scatter(1, dv_window[t], item_list, negatives[t // 2][:, t % 2, :])
+            nc.sync.dma_start(planes(out_0)[:, t, :], dv_window[t][:])
+
         for t in range(2):
             put_items(t)
 
         h_i = sbuf("h_i", [P, N, PACK], BF16)
         h_i_codes = sbuf("h_i_codes", [P, N], U32)
         h_i_scales = sbuf("h_i_scales", [P, N], U8)
-        fourth = item_sums(3, slice(0, N), flat(bank(3)[:]))
+        last = bank(6)
+        for e in range(2):
+            item_sums(2 + e, half(0), flat(last[:, 2 * e : 2 * e + 2, :]))
         h_words = flat(h_r[:]).bitcast(F32).rearrange("p (m k u) -> p k u m", k=PACK, u=2)
         for u in range(2):
-            turned = bank(u)
+            turned = bank(2 * u)
             for k in range(PACK):
-                nc.tensor.transpose(turned[:, k, :], h_words[:, k, u, :], ident_f32[:])
+                nc.tensor.transpose(turned[:, k, :], h_words[:, k, u, :], ident[:])
             move(
                 u,
                 h_i[:, half(u), :].rearrange("p (e c) k -> p e c k", e=2),
                 flat(turned[:]).bitcast(BF16).rearrange("p (k c e) -> p e c k", k=PACK, e=2),
             )
-        late_positives = sbuf("late_positives", [P, 2, HALF], F32, tag="h_r")
-        for e, sums in enumerate((third, fourth)):
-            nc.scalar.copy(late_positives[:, e, :], sums[:, half(0)])
-            dv[2 + e, 0] = late_positives[:, e, :]
+        positives.append(sbuf("positives1", [P, 2, HALF], F32, tag="h_r"))
+        for e in range(2):
+            nc.scalar.copy(positives[1][:, e, :], flat(last[:, 2 * e : 2 * e + 2, :]))
         for u in range(2):
             quantise(h_i_codes[:, half(u)], h_i_scales[:, half(u)], h_i[:, half(u), :], E5M2)
-        put_items(2)
-        stage_negatives(3, fourth[:, half(1)], False, tag="ident_f32")
-        put_items(3)
+        for t in range(2, PACK):
+            put_items(t)
         du_window.extend([zeroed_window("du_window%d" % (2 + e), tag) for e, tag in enumerate(("h_i", "h_i_scales"))])
 
         du = {}
 
-        def stage_users(t):
-            sums = bank(PACK + t)
-            codes = w_i_codes[t // 2][:, quarter(t % 2)]
-            multiply(flat(sums[:]), codes, w_i_scales[:, quarter(t)], h_i_codes[:], h_i_scales[:], E5M2)
-            for u in range(2):
-                values = sbuf("du%d_%d" % (t, u), [P, HALF], F32, tag="du%d_%d" % (t % 2, u))
-                some = sums[:, :, u * P // 2 : (u + 1) * P // 2].rearrange("p s m -> p m s")
-                move(u, values[:].rearrange("p (m s) -> p m s", s=PACK), some)
-                du[t, u] = values[:]
+        def stage_users(t, number, tags):
+            sums = bank(number)
+            multiply(flat(sums[:]), w_i_codes[t], w_i_scales[:, quarter(t)], h_i_codes[:], h_i_scales[:], E5M2)
+            for a in range(2):
+                values = sbuf("du%d_%d" % (t, a), [P, HALF], F32, tag=tags[a])
+                some = sums[:, :, a * P // 2 : (a + 1) * P // 2].rearrange("p s m -> p m s")
+                move(a, values[:].rearrange("p (m s) -> p m s", s=PACK), some)
+                du[t, a] = values[:]
+
+        def put_users(t):
+            for a in range(2):
+                scatter(a, du_window[t], user_list, du[t, a])
+            nc.sync.dma_start(planes(out_1)[:, t, :], du_window[t][:])
 
         for t in range(2):
-            stage_users(t)
-        for t in range(PACK):
-            put(out_1, t, du_window[t], user_list, (du[t, 0], du[t, 1]))
-            if t + 2 < PACK:
-                stage_users(t + 2)
+            stage_users(t, PACK + t, ("", ""))
+        put_users(0)
+        for t in range(1, PACK):
+            if t + 1 < PACK:
+                stage_users(t + 1, PACK + t + 1, ("du%d_0" % (t - 1), "du%d_1" % (t - 1)))
+            put_users(t)

@@ -209,6 +209,8 @@ def tile_attend_gmf_bpr_vu_kernel(tc, uT, vT, us, ts, offs, uoffs, out_0, out_1)
                 sums, w_d_codes[k][:], w_d_scales[:, quarter(k)], x_d_codes[:, users], x_d_scales[:, users], E4M3
             )
 
+        multiply(flat(bank(7)[:]), x_d_codes[:, quarter(0)], x_d_scales[:, quarter(0)], x_d_codes[:], x_d_scales[:], E4M3)
+
         margin = sbuf("margin", [P, 2, N], F32)
         q = [sbuf("q%d" % c, [P, P // PACK, PACK, PACK], F32) for c in range(2)]
 

@@ -283,16 +283,17 @@ def tile_attend_gmf_bpr_vu_kernel(tc, uT, vT, us, ts, offs, uoffs, out_0, out_1)
             nc.scalar.copy(positives[0][:, t, quarter(1)], item_sums(t, quarter(1), bank(5 + 2 * t)[:, 0, :]))
 
         gradient(2, parts=PACK)
-        gradient(3)
-        for k in (2, 3):
-            quantise_gradient(k)
+        quantise_gradient(2)
+        gradient(3, parts=2)
+        quantise_gradient(3)
         negatives = [sbuf("negatives%d" % u, [P, 2, HALF], F32) for u in range(2)]
+        negative_sums = [bank(0), bank(2), bank(4)]
+        for c in range(2):
+            for t in range(PACK):
+                item_sums(t, quarter(2 + c), negative_sums[min(t, 2)][:, 2 * (t // 3) + c, :])
         for t in range(2):
-            nc.vector.tensor_copy(negatives[0][:, t, :], item_sums(t, half(1), flat(bank(2 * t)[:, 0:2, :])))
-        pair = bank(4)
-        for e in range(2):
-            item_sums(2 + e, half(1), flat(pair[:, 2 * e : 2 * e + 2, :]))
-        nc.vector.tensor_copy(flat(negatives[1][:]), flat(pair[:]))
+            nc.vector.tensor_copy(negatives[0][:, t, :], flat(negative_sums[t][:, 0:2, :]))
+        nc.vector.tensor_copy(flat(negatives[1][:]), flat(negative_sums[2][:]))
 
         late_plane(3, False, turn_plane(w_planes[1][:, 1, :], 3), "margin", "signed")
         du_window = [zeroed_window("du_window%d" % t, tag) for t, tag in enumerate(("x_r_codes0", "x_r_scales0"))]

@@ -101,18 +101,18 @@ def tile_attend_gmf_bpr_vu_kernel(tc, uT, vT, us, ts, offs, uoffs, out_0, out_1)
         nc.sync.dma_start(user_list[:], uoffs)
         nc.scalar.dma_start(ts_row[P - 1 : P, :], ts[0:1, :])
         nc.scalar.dma_start(row_scale[:], us.rearrange("b (p t) o -> p (b t o)", t=PACK))
-        nc.gpsimd.memset(ts_row[0 : P - 1, :].bitcast(I32), 0)
+        nc.vector.memset(ts_row[0 : P - 1, :].bitcast(I32), 0)
         for t in range(1, PACK):
             nc.sync.dma_start(u_plane[t][:], planes(uT)[:, t, :])
         for t in range(PACK):
             nc.sync.dma_start(v_plane[t][:], planes(vT)[:, t, :])
 
-        def zeroed_window(name, tag=""):
+        def zeroed_window(name, tag="", engine=nc.gpsimd):
             window = sbuf(name, [P, T], F32, tag=tag)
-            nc.gpsimd.memset(window[:].bitcast(I32), 0)
+            engine.memset(window[:].bitcast(I32), 0)
             return window
 
-        dv_window = [zeroed_window("dv_window%d" % t) for t in range(PACK)]
+        dv_window = [zeroed_window("dv_window%d" % t, "", nc.vector if t < 1 else nc.gpsimd) for t in range(PACK)]
 
         ts_listed = sbuf("ts_listed", [P, N], F32)
         nc.vector.tensor_copy(ts_listed[:], ts_row[:].indirect(item_list[:]))

@@ -151,74 +151,64 @@ def tile_attend_gmf_bpr_vu_kernel(tc, uT, vT, us, ts, offs, uoffs, out_0, out_1)
         x_planes = sbuf("x_planes", [P, PACK, N], BF16)
         x_d = sbuf("x_d", [P, N, PACK], BF16)
         x_r = sbuf("x_r", [P, D, PACK], BF16)
+        x_by_column = x_d[:].rearrange("p (s m) t -> p m s t", s=PACK)
+        x_by_plane = x_planes[:].rearrange("p t (m s) -> p m s t", s=PACK)
+        x_d_codes = [sbuf("x_d_codes0", [P, HALF], U32), sbuf("x_d_codes1", [P, HALF], U32, tag="v_plane2")]
+        x_d_scales = [sbuf("x_d_scales%d" % u, [P, HALF], U8) for u in range(2)]
+        x_r_codes = [sbuf("x_r_codes0", [P, HALF], U32), sbuf("x_r_codes1", [P, HALF], U32, tag="v_plane0")]
+        x_r_scales = [sbuf("x_r_scales%d" % u, [P, HALF], U8) for u in range(2)]
         for t in range(PACK):
             nc.vector.tensor_copy(x_planes[:, t, :], u_plane[t][:].indirect(user_list[:]))
             lay_turned(False, x_r[:, quarter(t), :], turn_plane(x_planes[:, t, :], PACK + t))
-        x_by_column = x_d[:].rearrange("p (s m) t -> p m s t", s=PACK)
-        x_by_plane = x_planes[:].rearrange("p t (m s) -> p m s t", s=PACK)
-        for k in range(PACK):
-            nc.scalar.copy(x_by_column[:, groups(k)], x_by_plane[:, groups(k)])
-        x_d_codes = sbuf("x_d_codes", [P, N], U32, tag="v_plane1")
-        x_d_scales = sbuf("x_d_scales", [P, N], U8)
-        x_r_codes = [sbuf("x_r_codes0", [P, HALF], U32), sbuf("x_r_codes1", [P, HALF], U32, tag="v_plane0")]
-        x_r_scales = [sbuf("x_r_scales%d" % u, [P, HALF], U8) for u in range(2)]
+            if t % 2:
+                nc.vector.tensor_copy(x_by_column[:, :, :, t - 1 : t + 1], x_by_plane[:, :, :, t - 1 : t + 1])
+            if t == 1:
+                quantise(x_r_codes[0][:], x_r_scales[0][:], x_r[:, half(0), :], E4M3)
 
-        w_planes = [sbuf("w_planes%d" % u, [P, 2, N], BF16) for u in range(2)]
-        w_d = sbuf("w_d", [P, PACK, P, PACK], BF16)
+        w_planes = sbuf("w_planes", [P, 2, N], BF16)
+        w_d = sbuf("w_d", [P, N, PACK], BF16)
         w_d_scales = sbuf("w_d_scales", [P, N], U8)
         w_i = sbuf("w_i", [P, HALF, PACK], BF16)
-        early_codes = sbuf("early_codes", [P, HALF], U32, tag="v_plane2")
+        early_codes = sbuf("early_codes", [P, HALF], U32)
         w_i_codes = [early_codes[:, quarter(t)] for t in range(2)]
         w_i_scales = sbuf("w_i_scales", [P, D], U8)
-        w_by_column = [w_d[:, k].rearrange("p (g i) t -> p g t i", i=PACK) for k in range(PACK)]
-        w_by_plane = [pair[:].rearrange("p t (g i) -> p g t i", i=PACK) for pair in w_planes]
         for t in range(2):
-            nc.vector.tensor_copy(w_planes[0][:, t, :], v_plane[t][:].indirect(item_list[:]))
-            lay_turned(False, w_i[:, quarter(t), :], turn_plane(w_planes[0][:, t, :], 2 + t))
+            nc.vector.tensor_copy(w_planes[:, t, :], v_plane[t][:].indirect(item_list[:]))
+            lay_turned(False, w_i[:, quarter(t), :], turn_plane(w_planes[:, t, :], 2 + t))
             if t == 0:
-                for u in range(2):
-                    quantise(x_r_codes[u][:], x_r_scales[u][:], x_r[:, half(u), :], E4M3)
-            if t == 1:
-                quantise(x_d_codes[:], x_d_scales[:], x_d[:], E4M3)
-                for k in NEGATIVES_FIRST:
-                    nc.scalar.copy(w_by_column[k][:, :, 0:2, :], w_by_plane[0][:, groups(k)])
-        nc.vector.tensor_copy(w_planes[1][:, 0, :], v_plane[2][:].indirect(item_list[:]))
-        third_turned = turn_plane(w_planes[1][:, 0, :], 7)
+                quantise(x_r_codes[1][:], x_r_scales[1][:], x_r[:, half(1), :], E4M3)
+                quantise(x_d_codes[0][:], x_d_scales[0][:], x_d[:, half(0), :], E4M3)
+        for a in (1, 0):
+            nc.vector.tensor_copy(
+                w_d[:, half(a), :].rearrange("p (g i) t -> p g t i", i=PACK)[:, :, 0:2, :],
+                w_planes[:, :, half(a)].rearrange("p t (g i) -> p g t i", i=PACK),
+            )
+            nc.scalar.activation(w_d[:, half(a), 2], v_plane[2][:].indirect(entries(item_list, a, 2)), COPY)
         quantise(early_codes[:], w_i_scales[:, half(0)], w_i[:], E4M3)
+        quantise(x_d_codes[1][:], x_d_scales[1][:], x_d[:, half(1), :], E4M3)
 
         w_d_codes = {}
         for k in NEGATIVES_FIRST:
-            move_listed(k // 2, w_planes[1][:, 1, quarter(k)], v_plane[PACK - 1][:].indirect(entries(item_list, k, PACK)))
-            move(k // 2, w_by_column[k][:, :, 2:PACK, :], w_by_plane[1][:, groups(k)])
+            nc.scalar.activation(
+                w_d[:, quarter(k), PACK - 1], v_plane[PACK - 1][:].indirect(entries(item_list, k, PACK)), COPY
+            )
             w_d_codes[k] = sbuf("w_d_codes%d" % k, [P, P], U32)
-            quantise(w_d_codes[k][:], w_d_scales[:, quarter(k)], w_d[:, k], E4M3)
-
-        def late_plane(t, on_vector, turned, tag, codes_tag=""):
-            laid = sbuf("w_i%d" % t, [P, P, PACK], BF16, tag=tag)
-            lay_turned(on_vector, laid[:], turned)
-            codes = sbuf("w_i_codes%d" % t, [P, P], U32, tag=codes_tag)
-            quantise(codes[:], w_i_scales[:, quarter(t)], laid[:], E4M3)
-            w_i_codes.append(codes[:])
-
-        late_plane(2, False, third_turned, "", "w_d")
+            quantise(w_d_codes[k][:], w_d_scales[:, quarter(k)], w_d[:, quarter(k), :], E4M3)
 
         def score(k, u, number):
             sums = flat(bank(number)[:, 0:2, :])
-            users = half(u)
-            return multiply(
-                sums, w_d_codes[k][:], w_d_scales[:, quarter(k)], x_d_codes[:, users], x_d_scales[:, users], E4M3
-            )
+            return multiply(sums, w_d_codes[k][:], w_d_scales[:, quarter(k)], x_d_codes[u][:], x_d_scales[u][:], E4M3)
 
-        multiply(flat(bank(7)[:]), x_d_codes[:, quarter(0)], x_d_scales[:, quarter(0)], x_d_codes[:], x_d_scales[:], E4M3)
+        idle = bank(7)
+        for u in range(2):
+            stationary = (x_d_codes[1][:, quarter(0)], x_d_scales[1][:, quarter(0)])
+            multiply(flat(idle[:, 2 * u : 2 * u + 2, :]), *stationary, x_d_codes[u][:], x_d_scales[u][:], E4M3)
 
         margin = sbuf("margin", [P, 2, N], F32)
         q = [sbuf("q%d" % c, [P, P // PACK, PACK, PACK], F32) for c in range(2)]
 
         def scaled_negatives(c, u):
-            if c + u:
-                negative = sbuf("negative%d" % (2 * c + u), [P, HALF], F32)[:]
-            else:
-                negative = w_planes[1][:, 0, :].bitcast(F32)
+            negative = sbuf("negative%d" % (2 * c + u), [P, HALF], F32)[:]
             nc.scalar.activation(negative, score(2 + c, u, PACK * c + 2 * u), COPY, scale=ts_column[:, 2 + c : 3 + c])
             return negative
 
@@ -239,15 +229,13 @@ def tile_attend_gmf_bpr_vu_kernel(tc, uT, vT, us, ts, offs, uoffs, out_0, out_1)
                     scale=row_scale[:, s : s + 1],
                 )
 
-        for u in range(2):
-            add_positives(0, u, scaled_negatives(0, u))
-        late = [scaled_negatives(1, u) for u in range(2)]
-        for u in range(2):
-            weigh(0, u)
-        for u in range(2):
-            add_positives(1, u, late[u])
-        for u in range(2):
-            weigh(1, u)
+        for c in range(2):
+            negatives_scaled = [scaled_negatives(c, u) for u in range(2)]
+            for u in range(2):
+                add_positives(c, u, negatives_scaled[u])
+        for c in range(2):
+            for u in range(2):
+                weigh(c, u)
 
         h_r = sbuf("h_r", [P, N, PACK], BF16)
         h_r_codes = sbuf("h_r_codes", [P, N], U32)
@@ -270,6 +258,18 @@ def tile_attend_gmf_bpr_vu_kernel(tc, uT, vT, us, ts, offs, uoffs, out_0, out_1)
         def scatter(a, window, listed, values):
             move_listed(a, window[:].indirect(entries(listed, a, 2)), values)
 
+        w_words = flat(w_d[:]).bitcast(F32).rearrange("p (m j u) -> p j u m", j=PACK, u=2)
+        late_turned = bank(7)
+        for j in range(PACK):
+            nc.tensor.transpose(late_turned[:, j, :], w_words[:, j, 1, :], ident[:])
+        late_w_i = sbuf("late_w_i", [P, 2, P, PACK], BF16, tag="margin")
+        late_codes = sbuf("late_codes", [P, HALF], U32, tag="signed")
+        for e in range(2):
+            nc.scalar.copy(
+                late_w_i[:, e], flat(late_turned[:]).bitcast(BF16).rearrange("p (j c e) -> p e c j", j=PACK, e=2)[:, e]
+            )
+            w_i_codes.append(late_codes[:, quarter(e)])
+
         positives = [sbuf("positives0", [P, 2, HALF], F32)]
         for k in range(2):
             gradient(k)
@@ -280,12 +280,13 @@ def tile_attend_gmf_bpr_vu_kernel(tc, uT, vT, us, ts, offs, uoffs, out_0, out_1)
         nc.scalar.copy(positives[0][:, :, quarter(0)], early[:, 0:2, :])
         quantise_gradient(1)
         for t in range(2):
-            nc.scalar.copy(positives[0][:, t, quarter(1)], item_sums(t, quarter(1), bank(5 + 2 * t)[:, 0, :]))
+            nc.scalar.copy(positives[0][:, t, quarter(1)], item_sums(t, quarter(1), bank(5 - 2 * t)[:, 0, :]))
 
         gradient(2, parts=PACK)
-        quantise_gradient(2)
         gradient(3, parts=2)
+        quantise_gradient(2)
         quantise_gradient(3)
+        quantise(late_codes[:], w_i_scales[:, half(1)], late_w_i[:].rearrange("p e c j -> p (e c) j"), E4M3)
         negatives = [sbuf("negatives%d" % u, [P, 2, HALF], F32) for u in range(2)]
         negative_sums = [bank(0), bank(2), bank(4)]
         for c in range(2):
@@ -295,8 +296,10 @@ def tile_attend_gmf_bpr_vu_kernel(tc, uT, vT, us, ts, offs, uoffs, out_0, out_1)
             nc.vector.tensor_copy(negatives[0][:, t, :], flat(negative_sums[t][:, 0:2, :]))
         nc.vector.tensor_copy(flat(negatives[1][:]), flat(negative_sums[2][:]))
 
-        late_plane(3, False, turn_plane(w_planes[1][:, 1, :], 3), "margin", "signed")
-        du_window = [zeroed_window("du_window%d" % t, tag) for t, tag in enumerate(("x_r_codes0", "x_r_scales0"))]
+        h_planes = sbuf("h_planes", [P, PACK, N], BF16, tag="margin")
+        for s in range(PACK):
+            nc.gpsimd.tensor_scalar(h_planes[:, s, :], h_r[:, :, s], 1.0, 0.0, MULT, ADD)
+        du_window = [zeroed_window("du_window0", "h_r")]
 
         def put_items(t):
             scatter(0, dv_window[t], item_list, positives[t // 2][:, t % 2, :])
@@ -312,24 +315,27 @@ def tile_attend_gmf_bpr_vu_kernel(tc, uT, vT, us, ts, offs, uoffs, out_0, out_1)
         last = bank(6)
         for e in range(2):
             item_sums(2 + e, half(0), flat(last[:, 2 * e : 2 * e + 2, :]))
-        h_words = flat(h_r[:]).bitcast(F32).rearrange("p (m k u) -> p k u m", k=PACK, u=2)
-        for u in range(2):
-            turned = bank(2 * u)
-            for k in range(PACK):
-                nc.tensor.transpose(turned[:, k, :], h_words[:, k, u, :], ident[:])
+        h_words = flat(h_planes[:]).bitcast(F32).rearrange("p (s m u) -> p s u m", s=PACK, u=2)
+        for a in range(2):
+            turned = bank(1 + 6 * a)
+            for e in range(2):
+                for u in range(2):
+                    nc.tensor.transpose(turned[:, 2 * e + u, :], h_words[:, 2 * a + e, u, :], ident[:])
             move(
-                u,
-                h_i[:, half(u), :].rearrange("p (e c) k -> p e c k", e=2),
-                flat(turned[:]).bitcast(BF16).rearrange("p (k c e) -> p e c k", k=PACK, e=2),
+                a,
+                flat(h_i[:, half(a), :]).bitcast(F32).rearrange("p (e c u) -> p e c u", e=2, u=2),
+                turned[:].rearrange("p (e u) c -> p e c u", e=2),
             )
-        positives.append(sbuf("positives1", [P, 2, HALF], F32, tag="h_r"))
+        positives.append(sbuf("positives1", [P, 2, HALF], F32, tag="margin"))
         for e in range(2):
             nc.scalar.copy(positives[1][:, e, :], flat(last[:, 2 * e : 2 * e + 2, :]))
         for u in range(2):
             quantise(h_i_codes[:, half(u)], h_i_scales[:, half(u)], h_i[:, half(u), :], E5M2)
         for t in range(2, PACK):
             put_items(t)
-        du_window.extend([zeroed_window("du_window%d" % (2 + e), tag) for e, tag in enumerate(("h_i", "h_i_scales"))])
+        du_window.extend(
+            [zeroed_window("du_window%d" % (1 + e), tag) for e, tag in enumerate(("h_i", "h_i_scales", "h_i_codes"))]
+        )
 
         du = {}
 
@@ -347,10 +353,11 @@ def tile_attend_gmf_bpr_vu_kernel(tc, uT, vT, us, ts, offs, uoffs, out_0, out_1)
                 scatter(a, du_window[t], user_list, du[t, a])
             nc.sync.dma_start(planes(out_1)[:, t, :], du_window[t][:])
 
+        user_banks = (5, 3, 0, 2)
         for t in range(2):
-            stage_users(t, PACK + t, ("", ""))
+            stage_users(t, user_banks[t], ("", ""))
         put_users(0)
         for t in range(1, PACK):
             if t + 1 < PACK:
-                stage_users(t + 1, PACK + t + 1, ("du%d_0" % (t - 1), "du%d_1" % (t - 1)))
+                stage_users(t + 1, user_banks[t + 1], ("du%d_0" % (t - 1), "du%d_1" % (t - 1)))
             put_users(t)

@@ -23,6 +23,7 @@ P = 128
 PACK = 4
 HALF = N // 2
 COLS = N // 16
+ROW = N + HALF
 NEGATIVES_FIRST = (2, 0, 3, 1)
 
 
@@ -151,64 +152,74 @@ def tile_attend_gmf_bpr_vu_kernel(tc, uT, vT, us, ts, offs, uoffs, out_0, out_1)
         x_planes = sbuf("x_planes", [P, PACK, N], BF16)
         x_d = sbuf("x_d", [P, N, PACK], BF16)
         x_r = sbuf("x_r", [P, D, PACK], BF16)
-        x_by_column = x_d[:].rearrange("p (s m) t -> p m s t", s=PACK)
-        x_by_plane = x_planes[:].rearrange("p t (m s) -> p m s t", s=PACK)
-        x_d_codes = [sbuf("x_d_codes0", [P, HALF], U32), sbuf("x_d_codes1", [P, HALF], U32, tag="v_plane2")]
-        x_d_scales = [sbuf("x_d_scales%d" % u, [P, HALF], U8) for u in range(2)]
-        x_r_codes = [sbuf("x_r_codes0", [P, HALF], U32), sbuf("x_r_codes1", [P, HALF], U32, tag="v_plane0")]
-        x_r_scales = [sbuf("x_r_scales%d" % u, [P, HALF], U8) for u in range(2)]
         for t in range(PACK):
             nc.vector.tensor_copy(x_planes[:, t, :], u_plane[t][:].indirect(user_list[:]))
             lay_turned(False, x_r[:, quarter(t), :], turn_plane(x_planes[:, t, :], PACK + t))
-            if t % 2:
-                nc.vector.tensor_copy(x_by_column[:, :, :, t - 1 : t + 1], x_by_plane[:, :, :, t - 1 : t + 1])
-            if t == 1:
-                quantise(x_r_codes[0][:], x_r_scales[0][:], x_r[:, half(0), :], E4M3)
+        x_by_column = x_d[:].rearrange("p (s m) t -> p m s t", s=PACK)
+        x_by_plane = x_planes[:].rearrange("p t (m s) -> p m s t", s=PACK)
+        for k in range(PACK):
+            nc.scalar.copy(x_by_column[:, groups(k)], x_by_plane[:, groups(k)])
+        x_d_codes = sbuf("x_d_codes", [P, N], U32, tag="v_plane1")
+        x_d_scales = sbuf("x_d_scales", [P, N], U8)
+        x_r_codes = [sbuf("x_r_codes0", [P, HALF], U32), sbuf("x_r_codes1", [P, HALF], U32, tag="v_plane0")]
+        x_r_scales = [sbuf("x_r_scales%d" % u, [P, HALF], U8) for u in range(2)]
 
-        w_planes = sbuf("w_planes", [P, 2, N], BF16)
-        w_d = sbuf("w_d", [P, N, PACK], BF16)
+        w_planes = [sbuf("w_planes%d" % u, [P, 2, N], BF16) for u in range(2)]
+        w_d = sbuf("w_d", [P, PACK, P, PACK], BF16)
         w_d_scales = sbuf("w_d_scales", [P, N], U8)
         w_i = sbuf("w_i", [P, HALF, PACK], BF16)
-        early_codes = sbuf("early_codes", [P, HALF], U32)
+        early_codes = sbuf("early_codes", [P, HALF], U32, tag="v_plane2")
         w_i_codes = [early_codes[:, quarter(t)] for t in range(2)]
         w_i_scales = sbuf("w_i_scales", [P, D], U8)
+        w_by_column = [w_d[:, k].rearrange("p (g i) t -> p g t i", i=PACK) for k in range(PACK)]
+        w_by_plane = [pair[:].rearrange("p t (g i) -> p g t i", i=PACK) for pair in w_planes]
         for t in range(2):
-            nc.vector.tensor_copy(w_planes[:, t, :], v_plane[t][:].indirect(item_list[:]))
-            lay_turned(False, w_i[:, quarter(t), :], turn_plane(w_planes[:, t, :], 2 + t))
+            nc.vector.tensor_copy(w_planes[0][:, t, :], v_plane[t][:].indirect(item_list[:]))
+            lay_turned(False, w_i[:, quarter(t), :], turn_plane(w_planes[0][:, t, :], 2 + t))
             if t == 0:
-                quantise(x_r_codes[1][:], x_r_scales[1][:], x_r[:, half(1), :], E4M3)
-                quantise(x_d_codes[0][:], x_d_scales[0][:], x_d[:, half(0), :], E4M3)
-        for a in (1, 0):
-            nc.vector.tensor_copy(
-                w_d[:, half(a), :].rearrange("p (g i) t -> p g t i", i=PACK)[:, :, 0:2, :],
-                w_planes[:, :, half(a)].rearrange("p t (g i) -> p g t i", i=PACK),
-            )
-            nc.scalar.activation(w_d[:, half(a), 2], v_plane[2][:].indirect(entries(item_list, a, 2)), COPY)
+                for u in range(2):
+                    quantise(x_r_codes[u][:], x_r_scales[u][:], x_r[:, half(u), :], E4M3)
+            if t == 1:
+                quantise(x_d_codes[:], x_d_scales[:], x_d[:], E4M3)
+                for k in NEGATIVES_FIRST:
+                    nc.scalar.copy(w_by_column[k][:, :, 0:2, :], w_by_plane[0][:, groups(k)])
+        nc.vector.tensor_copy(w_planes[1][:, 0, :], v_plane[2][:].indirect(item_list[:]))
+        third_turned = turn_plane(w_planes[1][:, 0, :], 7)
         quantise(early_codes[:], w_i_scales[:, half(0)], w_i[:], E4M3)
-        quantise(x_d_codes[1][:], x_d_scales[1][:], x_d[:, half(1), :], E4M3)
 
         w_d_codes = {}
         for k in NEGATIVES_FIRST:
-            nc.scalar.activation(
-                w_d[:, quarter(k), PACK - 1], v_plane[PACK - 1][:].indirect(entries(item_list, k, PACK)), COPY
-            )
+            move_listed(k // 2, w_planes[1][:, 1, quarter(k)], v_plane[PACK - 1][:].indirect(entries(item_list, k, PACK)))
+            move(k // 2, w_by_column[k][:, :, 2:PACK, :], w_by_plane[1][:, groups(k)])
             w_d_codes[k] = sbuf("w_d_codes%d" % k, [P, P], U32)
-            quantise(w_d_codes[k][:], w_d_scales[:, quarter(k)], w_d[:, quarter(k), :], E4M3)
+            quantise(w_d_codes[k][:], w_d_scales[:, quarter(k)], w_d[:, k], E4M3)
+
+        def late_plane(t, on_vector, turned, tag, codes_tag=""):
+            laid = sbuf("w_i%d" % t, [P, P, PACK], BF16, tag=tag)
+            lay_turned(on_vector, laid[:], turned)
+            codes = sbuf("w_i_codes%d" % t, [P, P], U32, tag=codes_tag)
+            quantise(codes[:], w_i_scales[:, quarter(t)], laid[:], E4M3)
+            w_i_codes.append(codes[:])
+
+        late_plane(2, False, third_turned, "", "w_d")
 
         def score(k, u, number):
             sums = flat(bank(number)[:, 0:2, :])
-            return multiply(sums, w_d_codes[k][:], w_d_scales[:, quarter(k)], x_d_codes[u][:], x_d_scales[u][:], E4M3)
+            users = half(u)
+            return multiply(
+                sums, w_d_codes[k][:], w_d_scales[:, quarter(k)], x_d_codes[:, users], x_d_scales[:, users], E4M3
+            )
 
-        idle = bank(7)
-        for u in range(2):
-            stationary = (x_d_codes[1][:, quarter(0)], x_d_scales[1][:, quarter(0)])
-            multiply(flat(idle[:, 2 * u : 2 * u + 2, :]), *stationary, x_d_codes[u][:], x_d_scales[u][:], E4M3)
+        multiply(flat(bank(7)[:]), x_d_codes[:, quarter(0)], x_d_scales[:, quarter(0)], x_d_codes[:], x_d_scales[:], E4M3)
 
         margin = sbuf("margin", [P, 2, N], F32)
         q = [sbuf("q%d" % c, [P, P // PACK, PACK, PACK], F32) for c in range(2)]
 
         def scaled_negatives(c, u):
-            negative = sbuf("negative%d" % (2 * c + u), [P, HALF], F32)[:]
+            if c + u:
+                negative = sbuf("negative%d" % (2 * c + u), [P, HALF], F32)[:]
+            else:
+                negative = w_planes[1][:, 0, :].bitcast(F32)
             nc.scalar.activation(negative, score(2 + c, u, PACK * c + 2 * u), COPY, scale=ts_column[:, 2 + c : 3 + c])
             return negative
 
@@ -229,13 +240,15 @@ def tile_attend_gmf_bpr_vu_kernel(tc, uT, vT, us, ts, offs, uoffs, out_0, out_1)
                     scale=row_scale[:, s : s + 1],
                 )
 
-        for c in range(2):
-            negatives_scaled = [scaled_negatives(c, u) for u in range(2)]
-            for u in range(2):
-                add_positives(c, u, negatives_scaled[u])
-        for c in range(2):
-            for u in range(2):
-                weigh(c, u)
+        for u in range(2):
+            add_positives(0, u, scaled_negatives(0, u))
+        late = [scaled_negatives(1, u) for u in range(2)]
+        for u in range(2):
+            weigh(0, u)
+        for u in range(2):
+            add_positives(1, u, late[u])
+        for u in range(2):
+            weigh(1, u)
 
         h_r = sbuf("h_r", [P, N, PACK], BF16)
         h_r_codes = sbuf("h_r_codes", [P, N], U32)
@@ -258,17 +271,16 @@ def tile_attend_gmf_bpr_vu_kernel(tc, uT, vT, us, ts, offs, uoffs, out_0, out_1)
         def scatter(a, window, listed, values):
             move_listed(a, window[:].indirect(entries(listed, a, 2)), values)
 
-        w_words = flat(w_d[:]).bitcast(F32).rearrange("p (m j u) -> p j u m", j=PACK, u=2)
-        late_turned = bank(7)
-        for j in range(PACK):
-            nc.tensor.transpose(late_turned[:, j, :], w_words[:, j, 1, :], ident[:])
-        late_w_i = sbuf("late_w_i", [P, 2, P, PACK], BF16, tag="margin")
-        late_codes = sbuf("late_codes", [P, HALF], U32, tag="signed")
-        for e in range(2):
+        h_rows = sbuf("h_planes", [P, PACK * ROW], BF16, tag="margin")
+        h_planes = h_rows[:].rearrange("p (s n) -> p s n", s=PACK)[:, :, 0:N]
+        last_plane = h_rows[:, HALF : HALF + N].rearrange("p (c j) -> p c j", j=PACK)
+        lay_turned(False, last_plane, turn_plane(w_planes[1][:, 1, :], 3))
+
+        def part(k):
             nc.scalar.copy(
-                late_w_i[:, e], flat(late_turned[:]).bitcast(BF16).rearrange("p (j c e) -> p e c j", j=PACK, e=2)[:, e]
+                h_planes[:, :, quarter(k)].rearrange("p s (g i) -> p g s i", i=8),
+                h_r[:, quarter(k), :].rearrange("p (g i) s -> p g s i", i=8),
             )
-            w_i_codes.append(late_codes[:, quarter(e)])
 
         positives = [sbuf("positives0", [P, 2, HALF], F32)]
         for k in range(2):
@@ -280,13 +292,14 @@ def tile_attend_gmf_bpr_vu_kernel(tc, uT, vT, us, ts, offs, uoffs, out_0, out_1)
         nc.scalar.copy(positives[0][:, :, quarter(0)], early[:, 0:2, :])
         quantise_gradient(1)
         for t in range(2):
-            nc.scalar.copy(positives[0][:, t, quarter(1)], item_sums(t, quarter(1), bank(5 - 2 * t)[:, 0, :]))
+            nc.scalar.copy(positives[0][:, t, quarter(1)], item_sums(t, quarter(1), bank(5 + 2 * t)[:, 0, :]))
+        for k in range(2):
+            part(k)
 
         gradient(2, parts=PACK)
-        gradient(3, parts=2)
         quantise_gradient(2)
+        gradient(3, parts=2)
         quantise_gradient(3)
-        quantise(late_codes[:], w_i_scales[:, half(1)], late_w_i[:].rearrange("p e c j -> p (e c) j"), E4M3)
         negatives = [sbuf("negatives%d" % u, [P, 2, HALF], F32) for u in range(2)]
         negative_sums = [bank(0), bank(2), bank(4)]
         for c in range(2):
@@ -296,9 +309,13 @@ def tile_attend_gmf_bpr_vu_kernel(tc, uT, vT, us, ts, offs, uoffs, out_0, out_1)
             nc.vector.tensor_copy(negatives[0][:, t, :], flat(negative_sums[t][:, 0:2, :]))
         nc.vector.tensor_copy(flat(negatives[1][:]), flat(negative_sums[2][:]))
 
-        h_planes = sbuf("h_planes", [P, PACK, N], BF16, tag="margin")
-        for s in range(PACK):
-            nc.gpsimd.tensor_scalar(h_planes[:, s, :], h_r[:, :, s], 1.0, 0.0, MULT, ADD)
+        last_codes = sbuf("w_i_codes3", [P, P], U32, tag="signed")
+        quantise(last_codes[:], w_i_scales[:, quarter(PACK - 1)], last_plane, E4M3)
+        w_i_codes.append(last_codes[:])
+
+        nc.gpsimd.tensor_scalar(
+            h_planes[:, :, half(1)], h_r[:, half(1), :].rearrange("p i s -> p s i"), 1.0, 0.0, MULT, ADD
+        )
         du_window = [zeroed_window("du_window0", "h_r")]
 
         def put_items(t):
@@ -309,43 +326,58 @@ def tile_attend_gmf_bpr_vu_kernel(tc, uT, vT, us, ts, offs, uoffs, out_0, out_1)
         for t in range(2):
             put_items(t)
 
-        h_i = sbuf("h_i", [P, N, PACK], BF16)
-        h_i_codes = sbuf("h_i_codes", [P, N], U32)
-        h_i_scales = sbuf("h_i_scales", [P, N], U8)
+        h_i = [sbuf("h_i%d" % a, [P, HALF, PACK], BF16) for a in range(2)]
+        h_i_codes = [sbuf("h_i_codes%d" % a, [P, HALF], U32) for a in range(2)]
+        h_i_scales = [sbuf("h_i_scales%d" % a, [P, HALF], U8) for a in range(2)]
         last = bank(6)
         for e in range(2):
             item_sums(2 + e, half(0), flat(last[:, 2 * e : 2 * e + 2, :]))
-        h_words = flat(h_planes[:]).bitcast(F32).rearrange("p (s m u) -> p s u m", s=PACK, u=2)
-        for a in range(2):
-            turned = bank(1 + 6 * a)
+        h_words = h_rows[:].bitcast(F32).rearrange("p (s m u) -> p s u m", s=PACK, u=2)[:, :, :, 0:P]
+        for pair in range(2):
+            turned = bank(1 + 2 * pair)
             for e in range(2):
                 for u in range(2):
-                    nc.tensor.transpose(turned[:, 2 * e + u, :], h_words[:, 2 * a + e, u, :], ident[:])
-            move(
-                a,
-                flat(h_i[:, half(a), :]).bitcast(F32).rearrange("p (e c u) -> p e c u", e=2, u=2),
-                turned[:].rearrange("p (e u) c -> p e c u", e=2),
-            )
+                    nc.tensor.transpose(turned[:, 2 * e + u, :], h_words[:, 2 * pair + e, u, :], ident[:])
+            for a in range(2):
+                move(
+                    a,
+                    flat(h_i[a][:, quarter(pair), :]).bitcast(F32).rearrange("p (e c u) -> p e c u", e=2, u=2),
+                    turned[:, :, a * P // 2 : (a + 1) * P // 2].rearrange("p (e u) c -> p e c u", e=2),
+                )
         positives.append(sbuf("positives1", [P, 2, HALF], F32, tag="margin"))
-        for e in range(2):
-            nc.scalar.copy(positives[1][:, e, :], flat(last[:, 2 * e : 2 * e + 2, :]))
-        for u in range(2):
-            quantise(h_i_codes[:, half(u)], h_i_scales[:, half(u)], h_i[:, half(u), :], E5M2)
-        for t in range(2, PACK):
-            put_items(t)
+        quantise(h_i_codes[0][:], h_i_scales[0][:], h_i[0][:], E5M2)
+        nc.scalar.copy(positives[1][:, 0, :], flat(last[:, 0:2, :]))
+        put_items(2)
+        quantise(h_i_codes[1][:], h_i_scales[1][:], h_i[1][:], E5M2)
+        nc.scalar.copy(positives[1][:, 1, :], flat(last[:, 2:PACK, :]))
+        put_items(3)
         du_window.extend(
-            [zeroed_window("du_window%d" % (1 + e), tag) for e, tag in enumerate(("h_i", "h_i_scales", "h_i_codes"))]
+            [zeroed_window("du_window%d" % (1 + e), tag) for e, tag in enumerate(("h_i1", "h_i_scales1", "h_i_codes1"))]
         )
+
+        user_banks = ((5, 7), (0, 2))
+        user_sums = {}
+        for a in range(2):
+            for pair in range(2):
+                sums = bank(user_banks[a][pair])
+                for e in range(2):
+                    t = 2 * pair + e
+                    user_sums[t, a] = multiply(
+                        flat(sums[:, 2 * e : 2 * e + 2, :]),
+                        w_i_codes[t],
+                        w_i_scales[:, quarter(t)],
+                        h_i_codes[a][:],
+                        h_i_scales[a][:],
+                        E5M2,
+                    )
 
         du = {}
 
-        def stage_users(t, number, tags):
-            sums = bank(number)
-            multiply(flat(sums[:]), w_i_codes[t], w_i_scales[:, quarter(t)], h_i_codes[:], h_i_scales[:], E5M2)
+        def stage_users(t, tags):
             for a in range(2):
                 values = sbuf("du%d_%d" % (t, a), [P, HALF], F32, tag=tags[a])
-                some = sums[:, :, a * P // 2 : (a + 1) * P // 2].rearrange("p s m -> p m s")
-                move(a, values[:].rearrange("p (m s) -> p m s", s=PACK), some)
+                some = user_sums[t, a].rearrange("p (s c) -> p c s", s=PACK)
+                move(a, values[:].rearrange("p (c s) -> p c s", s=PACK), some)
                 du[t, a] = values[:]
 
         def put_users(t):
@@ -353,11 +385,10 @@ def tile_attend_gmf_bpr_vu_kernel(tc, uT, vT, us, ts, offs, uoffs, out_0, out_1)
                 scatter(a, du_window[t], user_list, du[t, a])
             nc.sync.dma_start(planes(out_1)[:, t, :], du_window[t][:])
 
-        user_banks = (5, 3, 0, 2)
         for t in range(2):
-            stage_users(t, user_banks[t], ("", ""))
+            stage_users(t, ("", ""))
         put_users(0)
         for t in range(1, PACK):
             if t + 1 < PACK:
-                stage_users(t + 1, user_banks[t + 1], ("du%d_0" % (t - 1), "du%d_1" % (t - 1)))
+                stage_users(t + 1, ("du%d_0" % (t - 1), "du%d_1" % (t - 1)))
             put_users(t)

@@ -24,6 +24,7 @@ PACK = 4
 HALF = N // 2
 COLS = N // 16
 ROW = N + HALF
+KIB = 1024
 NEGATIVES_FIRST = (2, 0, 3, 1)
 
 
@@ -31,10 +32,14 @@ def tile_attend_gmf_bpr_vu_kernel(tc, uT, vT, us, ts, offs, uoffs, out_0, out_1)
     nc = tc.nc
     with ExitStack() as ctx:
         keep = ctx.enter_context(tc.tile_pool(name="keep", bufs=1))
+        shared = ctx.enter_context(tc.tile_pool(name="shared", bufs=1))
         psum = ctx.enter_context(tc.psum_pool(name="psum", bufs=1))
 
         def sbuf(name, shape, dtype, tag=""):
             return keep.tile(shape, dtype, name=name, tag=tag or name, align_bytes=256)
+
+        def placed(name, shape, dtype, offset):
+            return shared.tile(shape, dtype, name=name, offset=offset, align_bytes=256)
 
         def bank(number):
             return psum.tile([P, PACK, P], F32, name="bank%d" % number)
@@ -212,7 +217,7 @@ def tile_attend_gmf_bpr_vu_kernel(tc, uT, vT, us, ts, offs, uoffs, out_0, out_1)
 
         multiply(flat(bank(7)[:]), x_d_codes[:, quarter(0)], x_d_scales[:, quarter(0)], x_d_codes[:], x_d_scales[:], E4M3)
 
-        margin = sbuf("margin", [P, 2, N], F32)
+        margin = placed("margin", [P, 2, N], F32, 0)
         q = [sbuf("q%d" % c, [P, P // PACK, PACK, PACK], F32) for c in range(2)]
 
         def scaled_negatives(c, u):
@@ -271,10 +276,10 @@ def tile_attend_gmf_bpr_vu_kernel(tc, uT, vT, us, ts, offs, uoffs, out_0, out_1)
         def scatter(a, window, listed, values):
             move_listed(a, window[:].indirect(entries(listed, a, 2)), values)
 
-        h_rows = sbuf("h_planes", [P, PACK * ROW], BF16, tag="margin")
+        h_rows = placed("h_planes", [P, PACK * ROW], BF16, 0)
         h_planes = h_rows[:].rearrange("p (s n) -> p s n", s=PACK)[:, :, 0:N]
         last_plane = h_rows[:, HALF : HALF + N].rearrange("p (c j) -> p c j", j=PACK)
-        lay_turned(False, last_plane, turn_plane(w_planes[1][:, 1, :], 3))
+        lay_turned(False, last_plane, turn_plane(w_planes[1][:, 1, :], 7))
 
         def part(k):
             nc.scalar.copy(
@@ -282,17 +287,18 @@ def tile_attend_gmf_bpr_vu_kernel(tc, uT, vT, us, ts, offs, uoffs, out_0, out_1)
                 h_r[:, quarter(k), :].rearrange("p (g i) s -> p g s i", i=8),
             )
 
-        positives = [sbuf("positives0", [P, 2, HALF], F32)]
+        first_positives = sbuf("positives0", [P, 2, HALF], F32)
+        positives = [first_positives[:, t, :] for t in range(2)]
         for k in range(2):
             gradient(k)
         quantise_gradient(0)
         early = bank(1)
         for t in range(2):
             item_sums(t, quarter(0), early[:, t, :])
-        nc.scalar.copy(positives[0][:, :, quarter(0)], early[:, 0:2, :])
+        nc.scalar.copy(first_positives[:, :, quarter(0)], early[:, 0:2, :])
         quantise_gradient(1)
         for t in range(2):
-            nc.scalar.copy(positives[0][:, t, quarter(1)], item_sums(t, quarter(1), bank(5 + 2 * t)[:, 0, :]))
+            nc.scalar.copy(first_positives[:, t, quarter(1)], item_sums(t, quarter(1), bank(5 + 2 * t)[:, 0, :]))
         for k in range(2):
             part(k)
 
@@ -316,10 +322,10 @@ def tile_attend_gmf_bpr_vu_kernel(tc, uT, vT, us, ts, offs, uoffs, out_0, out_1)
         nc.gpsimd.tensor_scalar(
             h_planes[:, :, half(1)], h_r[:, half(1), :].rearrange("p i s -> p s i"), 1.0, 0.0, MULT, ADD
         )
-        du_window = [zeroed_window("du_window0", "h_r")]
+        du_window = [zeroed_window("du_window%d" % t, tag) for t, tag in enumerate(("x_r_scales1", "h_r"))]
 
         def put_items(t):
-            scatter(0, dv_window[t], item_list, positives[t // 2][:, t % 2, :])
+            scatter(0, dv_window[t], item_list, positives[t])
             scatter(1, dv_window[t], item_list, negatives[t // 2][:, t % 2, :])
             nc.sync.dma_start(planes(out_0)[:, t, :], dv_window[t][:])
 
@@ -327,32 +333,39 @@ def tile_attend_gmf_bpr_vu_kernel(tc, uT, vT, us, ts, offs, uoffs, out_0, out_1)
             put_items(t)
 
         h_i = [sbuf("h_i%d" % a, [P, HALF, PACK], BF16) for a in range(2)]
-        h_i_codes = [sbuf("h_i_codes%d" % a, [P, HALF], U32) for a in range(2)]
+        h_i_codes = [sbuf("h_i_codes0", [P, HALF], U32)]
         h_i_scales = [sbuf("h_i_scales%d" % a, [P, HALF], U8) for a in range(2)]
         last = bank(6)
         for e in range(2):
             item_sums(2 + e, half(0), flat(last[:, 2 * e : 2 * e + 2, :]))
         h_words = h_rows[:].bitcast(F32).rearrange("p (s m u) -> p s u m", s=PACK, u=2)[:, :, :, 0:P]
-        for pair in range(2):
-            turned = bank(1 + 2 * pair)
-            for e in range(2):
-                for u in range(2):
-                    nc.tensor.transpose(turned[:, 2 * e + u, :], h_words[:, 2 * pair + e, u, :], ident[:])
-            for a in range(2):
-                move(
-                    a,
-                    flat(h_i[a][:, quarter(pair), :]).bitcast(F32).rearrange("p (e c u) -> p e c u", e=2, u=2),
-                    turned[:, :, a * P // 2 : (a + 1) * P // 2].rearrange("p (e u) c -> p e c u", e=2),
-                )
-        positives.append(sbuf("positives1", [P, 2, HALF], F32, tag="margin"))
+        turned = [bank(1 + 2 * pair) for pair in range(2)]
+        for s in range(PACK):
+            for u in range(2):
+                nc.tensor.transpose(turned[s // 2][:, 2 * (s % 2) + u, :], h_words[:, s, u, :], ident[:])
+
+        def lay_users(a, pair):
+            move(
+                a,
+                flat(h_i[a][:, quarter(pair), :]).bitcast(F32).rearrange("p (e c u) -> p e c u", e=2, u=2),
+                turned[pair][:, :, a * P // 2 : (a + 1) * P // 2].rearrange("p (e u) c -> p e c u", e=2),
+            )
+
+        for a in range(2):
+            lay_users(a, 0)
+        positives.append(placed("positives2", [P, HALF], F32, 0)[:])
+        nc.scalar.copy(positives[2], flat(last[:, 0:2, :]))
+        for a in range(2):
+            lay_users(a, 1)
         quantise(h_i_codes[0][:], h_i_scales[0][:], h_i[0][:], E5M2)
-        nc.scalar.copy(positives[1][:, 0, :], flat(last[:, 0:2, :]))
         put_items(2)
+        h_i_codes.append(placed("h_i_codes1", [P, HALF], U32, 0))
         quantise(h_i_codes[1][:], h_i_scales[1][:], h_i[1][:], E5M2)
-        nc.scalar.copy(positives[1][:, 1, :], flat(last[:, 2:PACK, :]))
+        positives.append(placed("positives3", [P, HALF], F32, 2 * KIB)[:])
+        nc.scalar.copy(positives[3], flat(last[:, 2:PACK, :]))
         put_items(3)
         du_window.extend(
-            [zeroed_window("du_window%d" % (1 + e), tag) for e, tag in enumerate(("h_i1", "h_i_scales1", "h_i_codes1"))]
+            [zeroed_window("du_window%d" % (2 + e), tag) for e, tag in enumerate(("h_i1", "h_i_scales1"))]
         )
 
         user_banks = ((5, 7), (0, 2))
@@ -373,12 +386,15 @@ def tile_attend_gmf_bpr_vu_kernel(tc, uT, vT, us, ts, offs, uoffs, out_0, out_1)
 
         du = {}
 
-        def stage_users(t, tags):
+        def stage_users(t):
+            tiles = (
+                sbuf("du%d_0" % t, [P, HALF], F32, tag="du%d_0" % (t % 2)),
+                placed("du%d_1" % t, [P, HALF], F32, 3 * KIB // 2 + t % 2 * KIB),
+            )
             for a in range(2):
-                values = sbuf("du%d_%d" % (t, a), [P, HALF], F32, tag=tags[a])
                 some = user_sums[t, a].rearrange("p (s c) -> p c s", s=PACK)
-                move(a, values[:].rearrange("p (c s) -> p c s", s=PACK), some)
-                du[t, a] = values[:]
+                move(a, tiles[a][:].rearrange("p (c s) -> p c s", s=PACK), some)
+                du[t, a] = tiles[a][:]
 
         def put_users(t):
             for a in range(2):
@@ -386,9 +402,9 @@ def tile_attend_gmf_bpr_vu_kernel(tc, uT, vT, us, ts, offs, uoffs, out_0, out_1)
             nc.sync.dma_start(planes(out_1)[:, t, :], du_window[t][:])
 
         for t in range(2):
-            stage_users(t, ("", ""))
+            stage_users(t)
         put_users(0)
         for t in range(1, PACK):
             if t + 1 < PACK:
-                stage_users(t + 1, ("du%d_0" % (t - 1), "du%d_1" % (t - 1)))
+                stage_users(t + 1)
             put_users(t)

@@ -298,7 +298,7 @@ def tile_attend_gmf_bpr_vu_kernel(tc, uT, vT, us, ts, offs, uoffs, out_0, out_1)
         nc.scalar.copy(first_positives[:, :, quarter(0)], early[:, 0:2, :])
         quantise_gradient(1)
         for t in range(2):
-            nc.scalar.copy(first_positives[:, t, quarter(1)], item_sums(t, quarter(1), bank(5 + 2 * t)[:, 0, :]))
+            move(t == 0, first_positives[:, t, quarter(1)], item_sums(t, quarter(1), bank(5 + 2 * t)[:, 0, :]))
         for k in range(2):
             part(k)
 
@@ -306,18 +306,20 @@ def tile_attend_gmf_bpr_vu_kernel(tc, uT, vT, us, ts, offs, uoffs, out_0, out_1)
         quantise_gradient(2)
         gradient(3, parts=2)
         quantise_gradient(3)
-        negatives = [sbuf("negatives%d" % u, [P, 2, HALF], F32) for u in range(2)]
-        negative_sums = [bank(0), bank(2), bank(4)]
-        for c in range(2):
-            for t in range(PACK):
-                item_sums(t, quarter(2 + c), negative_sums[min(t, 2)][:, 2 * (t // 3) + c, :])
-        for t in range(2):
-            nc.vector.tensor_copy(negatives[0][:, t, :], flat(negative_sums[t][:, 0:2, :]))
-        nc.vector.tensor_copy(flat(negatives[1][:]), flat(negative_sums[2][:]))
-
         last_codes = sbuf("w_i_codes3", [P, P], U32, tag="signed")
         quantise(last_codes[:], w_i_scales[:, quarter(PACK - 1)], last_plane, E4M3)
         w_i_codes.append(last_codes[:])
+        negatives = sbuf("negatives", [P, PACK, HALF], F32)
+        early_negatives = bank(0)
+        late_negatives = [bank(2), bank(4)]
+        for t in range(PACK):
+            item_sums(t, quarter(2), early_negatives[:, t, :])
+        for t in range(PACK):
+            item_sums(t, quarter(3), late_negatives[t // 2][:, t % 2, :])
+        nc.vector.tensor_copy(negatives[:, :, quarter(0)], early_negatives[:])
+        for u in range(2):
+            nc.vector.tensor_copy(negatives[:, 2 * u : 2 * u + 2, quarter(1)], late_negatives[u][:, 0:2, :])
+
 
         nc.gpsimd.tensor_scalar(
             h_planes[:, :, half(1)], h_r[:, half(1), :].rearrange("p i s -> p s i"), 1.0, 0.0, MULT, ADD
@@ -326,7 +328,7 @@ def tile_attend_gmf_bpr_vu_kernel(tc, uT, vT, us, ts, offs, uoffs, out_0, out_1)
 
         def put_items(t):
             scatter(0, dv_window[t], item_list, positives[t])
-            scatter(1, dv_window[t], item_list, negatives[t // 2][:, t % 2, :])
+            scatter(1, dv_window[t], item_list, negatives[:, t, :])
             nc.sync.dma_start(planes(out_0)[:, t, :], dv_window[t][:])
 
         for t in range(2):
@@ -344,25 +346,25 @@ def tile_attend_gmf_bpr_vu_kernel(tc, uT, vT, us, ts, offs, uoffs, out_0, out_1)
             for u in range(2):
                 nc.tensor.transpose(turned[s // 2][:, 2 * (s % 2) + u, :], h_words[:, s, u, :], ident[:])
 
-        def lay_users(a, pair):
+        def lay_users(a, pair, on_vector):
             move(
-                a,
+                on_vector,
                 flat(h_i[a][:, quarter(pair), :]).bitcast(F32).rearrange("p (e c u) -> p e c u", e=2, u=2),
                 turned[pair][:, :, a * P // 2 : (a + 1) * P // 2].rearrange("p (e u) c -> p e c u", e=2),
             )
 
         for a in range(2):
-            lay_users(a, 0)
+            lay_users(a, 0, a)
         positives.append(placed("positives2", [P, HALF], F32, 0)[:])
         nc.scalar.copy(positives[2], flat(last[:, 0:2, :]))
-        for a in range(2):
-            lay_users(a, 1)
+        lay_users(0, 1, False)
+        positives.append(placed("positives3", [P, HALF], F32, 2 * KIB)[:])
+        nc.vector.tensor_copy(positives[3], flat(last[:, 2:PACK, :]))
         quantise(h_i_codes[0][:], h_i_scales[0][:], h_i[0][:], E5M2)
         put_items(2)
+        lay_users(1, 1, False)
         h_i_codes.append(placed("h_i_codes1", [P, HALF], U32, 0))
         quantise(h_i_codes[1][:], h_i_scales[1][:], h_i[1][:], E5M2)
-        positives.append(placed("positives3", [P, HALF], F32, 2 * KIB)[:])
-        nc.scalar.copy(positives[3], flat(last[:, 2:PACK, :]))
         put_items(3)
         du_window.extend(
             [zeroed_window("du_window%d" % (2 + e), tag) for e, tag in enumerate(("h_i1", "h_i_scales1"))]

@@ -119,6 +119,7 @@ def tile_attend_gmf_bpr_vu_kernel(tc, uT, vT, us, ts, offs, uoffs, out_0, out_1)
             return window
 
         dv_window = [zeroed_window("dv_window%d" % t, "", nc.vector if t < 1 else nc.gpsimd) for t in range(PACK)]
+        du_window = [zeroed_window("du_window0")]
 
         ts_listed = sbuf("ts_listed", [P, N], F32)
         nc.vector.tensor_copy(ts_listed[:], ts_row[:].indirect(item_list[:]))
@@ -324,7 +325,7 @@ def tile_attend_gmf_bpr_vu_kernel(tc, uT, vT, us, ts, offs, uoffs, out_0, out_1)
         nc.gpsimd.tensor_scalar(
             h_planes[:, :, half(1)], h_r[:, half(1), :].rearrange("p i s -> p s i"), 1.0, 0.0, MULT, ADD
         )
-        du_window = [zeroed_window("du_window%d" % t, tag) for t, tag in enumerate(("x_r_scales1", "h_r"))]
+        du_window.append(zeroed_window("du_window1", "h_r"))
 
         def put_items(t):
             scatter(0, dv_window[t], item_list, positives[t])

@@ -299,7 +299,7 @@ def tile_attend_gmf_bpr_vu_kernel(tc, uT, vT, us, ts, offs, uoffs, out_0, out_1)
         nc.scalar.copy(first_positives[:, :, quarter(0)], early[:, 0:2, :])
         quantise_gradient(1)
         for t in range(2):
-            move(t == 0, first_positives[:, t, quarter(1)], item_sums(t, quarter(1), bank(5 + 2 * t)[:, 0, :]))
+            nc.scalar.copy(first_positives[:, t, quarter(1)], item_sums(t, quarter(1), bank(5 + 2 * t)[:, 0, :]))
         for k in range(2):
             part(k)
 

from contextlib import ExitStack

import concourse.mybir as mybir
from concourse.masks import make_identity

D, T, N = 512, 2048, 512
FLOPS = 3 * 2 * D * N * N

F32 = mybir.dt.float32
BF16 = mybir.dt.bfloat16
I32 = mybir.dt.int32
U32 = mybir.dt.uint32
U16 = mybir.dt.uint16
U8 = mybir.dt.uint8
E4M3 = mybir.dt.float8_e4m3fn_x4
E5M2 = mybir.dt.float8_e5m2_x4
MULT = mybir.AluOpType.mult
ADD = mybir.AluOpType.add
COPY = mybir.ActivationFunctionType.Copy
SIGMOID = mybir.ActivationFunctionType.Sigmoid

P = 128
PACK = 4
HALF = N // 2
COLS = N // 16
ROW = N + HALF
KIB = 1024
NEGATIVES_FIRST = (2, 0, 3, 1)


def tile_attend_gmf_bpr_vu_kernel(tc, uT, vT, us, ts, offs, uoffs, out_0, out_1):
    nc = tc.nc
    with ExitStack() as ctx:
        keep = ctx.enter_context(tc.tile_pool(name="keep", bufs=1))
        shared = ctx.enter_context(tc.tile_pool(name="shared", bufs=1))
        psum = ctx.enter_context(tc.psum_pool(name="psum", bufs=1))

        def sbuf(name, shape, dtype, tag=""):
            return keep.tile(shape, dtype, name=name, tag=tag or name, align_bytes=256)

        def placed(name, shape, dtype, offset):
            return shared.tile(shape, dtype, name=name, offset=offset, align_bytes=256)

        def bank(number):
            return psum.tile([P, PACK, P], F32, name="bank%d" % number)

        def planes(dram):
            return dram.rearrange("(p t) n -> p t n", t=PACK)

        def flat(ap):
            return ap.rearrange("p a b -> p (a b)")

        def quarter(k):
            return slice(k * P, (k + 1) * P)

        def half(a):
            return slice(a * HALF, (a + 1) * HALF)

        def groups(k):
            return slice(k * P // PACK, (k + 1) * P // PACK)

        def entries(listed, part, parts):
            return listed[:, part * COLS // parts : (part + 1) * COLS // parts]

        def quantise(codes, scales, values, fmt):
            nc.vector.quantize_mx(out=codes.bitcast(fmt), scales=scales, in_=flat(values))

        def multiply(sums, codes, scales, moving_codes, moving_scales, moving_fmt):
            nc.tensor.matmul_mx(
                out=sums,
                lhsT=codes.bitcast(E4M3),
                lhsT_scale=scales,
                rhs=moving_codes.bitcast(moving_fmt),
                rhs_scale=moving_scales,
                start=True,
                stop=True,
            )
            return sums

        def move(on_vector, dst, src):
            if on_vector:
                nc.vector.tensor_copy(dst, src)
            else:
                nc.scalar.copy(dst, src)

        def move_listed(on_vector, dst, src):
            if on_vector:
                nc.vector.tensor_copy(dst, src)
            else:
                nc.scalar.activation(dst, src, COPY)

        warm = sbuf("warm", [P, 8], F32)
        nc.gpsimd.memset(warm[:], 0.0)
        nc.scalar.activation(warm[:], warm[:], SIGMOID)

        ident = sbuf("ident", [P, P], F32)
        make_identity(nc, ident[:])

        user_list = keep.tile([P, COLS], U16, name="user_list")
        item_list = keep.tile([P, COLS], U16, name="item_list")
        u_plane = [sbuf("u_plane%d" % t, [P, T], F32) for t in range(PACK)]
        v_plane = [sbuf("v_plane%d" % t, [P, T], F32) for t in range(PACK)]
        ts_row = sbuf("ts_row", [P, T], F32)
        row_scale = sbuf("row_scale", [P, PACK], F32)
        nc.sync.dma_start(item_list[:], offs)
        nc.sync.dma_start(u_plane[0][:], planes(uT)[:, 0, :])
        nc.sync.dma_start(user_list[:], uoffs)
        nc.scalar.dma_start(ts_row[P - 1 : P, :], ts[0:1, :])
        nc.scalar.dma_start(row_scale[:], us.rearrange("b (p t) o -> p (b t o)", t=PACK))
        nc.vector.memset(ts_row[0 : P - 1, :].bitcast(I32), 0)
        for t in range(1, PACK):
            nc.sync.dma_start(u_plane[t][:], planes(uT)[:, t, :])
        for t in range(PACK):
            nc.sync.dma_start(v_plane[t][:], planes(vT)[:, t, :])

        def zeroed_window(name, tag="", engine=nc.gpsimd):
            window = sbuf(name, [P, T], F32, tag=tag)
            engine.memset(window[:].bitcast(I32), 0)
            return window

        dv_window = [zeroed_window("dv_window%d" % t, "", nc.vector if t < 1 else nc.gpsimd) for t in range(PACK)]
        du_window = [zeroed_window("du_window0")]

        ts_listed = sbuf("ts_listed", [P, N], F32)
        nc.vector.tensor_copy(ts_listed[:], ts_row[:].indirect(item_list[:]))
        ts_turned = bank(0)
        for k in range(PACK):
            nc.tensor.transpose(ts_turned[:, k, :], ts_listed[:, quarter(k)], ident[:])
        ts_column = sbuf("ts_column", [P, PACK], F32)
        nc.scalar.activation(ts_column[:, 0:2], ts_turned[:, 0:2, P - 1], COPY, scale=-1.0)
        nc.scalar.activation(ts_column[:, 2:PACK], ts_turned[:, 2:PACK, P - 1], COPY)
        ts_spread = bank(1)
        for k in range(PACK):
            nc.tensor.transpose(ts_spread[:, k, :], ts_column[:, k : k + 1].to_broadcast([P, P]), ident[:])
        signed = sbuf("signed", [P, N // PACK, PACK, PACK], F32)
        for s in range(PACK):
            nc.scalar.activation(
                signed[:, :, s, :],
                flat(ts_spread[:]).rearrange("p (g i) -> p g i", i=PACK),
                COPY,
                scale=row_scale[:, s : s + 1],
            )

        def turn_plane(plane, number):
            words = plane.bitcast(F32).rearrange("p (m u) -> p u m", u=2)
            turned = bank(number)
            for u in range(2):
                nc.tensor.transpose(turned[:, u, :], words[:, u, :], ident[:])
            return turned

        def lay_turned(on_vector, dst, turned):
            move(
                on_vector,
                flat(dst).bitcast(F32).rearrange("p (c u) -> p c u", u=2),
                turned[:, 0:2, :].rearrange("p u c -> p c u"),
            )

        x_planes = sbuf("x_planes", [P, PACK, N], BF16)
        x_d = sbuf("x_d", [P, N, PACK], BF16)
        x_r = sbuf("x_r", [P, D, PACK], BF16)
        for t in range(PACK):
            nc.vector.tensor_copy(x_planes[:, t, :], u_plane[t][:].indirect(user_list[:]))
            lay_turned(False, x_r[:, quarter(t), :], turn_plane(x_planes[:, t, :], PACK + t))
        x_by_column = x_d[:].rearrange("p (s m) t -> p m s t", s=PACK)
        x_by_plane = x_planes[:].rearrange("p t (m s) -> p m s t", s=PACK)
        for k in range(PACK):
            nc.scalar.copy(x_by_column[:, groups(k)], x_by_plane[:, groups(k)])
        x_d_codes = sbuf("x_d_codes", [P, N], U32, tag="v_plane1")
        x_d_scales = sbuf("x_d_scales", [P, N], U8)
        x_r_codes = [sbuf("x_r_codes0", [P, HALF], U32), sbuf("x_r_codes1", [P, HALF], U32, tag="v_plane0")]
        x_r_scales = [sbuf("x_r_scales%d" % u, [P, HALF], U8) for u in range(2)]

        w_planes = [sbuf("w_planes%d" % u, [P, 2, N], BF16) for u in range(2)]
        w_d = sbuf("w_d", [P, PACK, P, PACK], BF16)
        w_d_scales = sbuf("w_d_scales", [P, N], U8)
        w_i = sbuf("w_i", [P, HALF, PACK], BF16)
        early_codes = sbuf("early_codes", [P, HALF], U32, tag="v_plane2")
        w_i_codes = [early_codes[:, quarter(t)] for t in range(2)]
        w_i_scales = sbuf("w_i_scales", [P, D], U8)
        w_by_column = [w_d[:, k].rearrange("p (g i) t -> p g t i", i=PACK) for k in range(PACK)]
        w_by_plane = [pair[:].rearrange("p t (g i) -> p g t i", i=PACK) for pair in w_planes]
        for t in range(2):
            nc.vector.tensor_copy(w_planes[0][:, t, :], v_plane[t][:].indirect(item_list[:]))
            lay_turned(False, w_i[:, quarter(t), :], turn_plane(w_planes[0][:, t, :], 2 + t))
            if t == 0:
                for u in range(2):
                    quantise(x_r_codes[u][:], x_r_scales[u][:], x_r[:, half(u), :], E4M3)
            if t == 1:
                quantise(x_d_codes[:], x_d_scales[:], x_d[:], E4M3)
                for k in NEGATIVES_FIRST:
                    nc.scalar.copy(w_by_column[k][:, :, 0:2, :], w_by_plane[0][:, groups(k)])
        nc.vector.tensor_copy(w_planes[1][:, 0, :], v_plane[2][:].indirect(item_list[:]))
        third_turned = turn_plane(w_planes[1][:, 0, :], 7)
        quantise(early_codes[:], w_i_scales[:, half(0)], w_i[:], E4M3)

        w_d_codes = {}
        for k in NEGATIVES_FIRST:
            move_listed(k // 2, w_planes[1][:, 1, quarter(k)], v_plane[PACK - 1][:].indirect(entries(item_list, k, PACK)))
            move(k // 2, w_by_column[k][:, :, 2:PACK, :], w_by_plane[1][:, groups(k)])
            w_d_codes[k] = sbuf("w_d_codes%d" % k, [P, P], U32)
            quantise(w_d_codes[k][:], w_d_scales[:, quarter(k)], w_d[:, k], E4M3)

        def late_plane(t, on_vector, turned, tag, codes_tag=""):
            laid = sbuf("w_i%d" % t, [P, P, PACK], BF16, tag=tag)
            lay_turned(on_vector, laid[:], turned)
            codes = sbuf("w_i_codes%d" % t, [P, P], U32, tag=codes_tag)
            quantise(codes[:], w_i_scales[:, quarter(t)], laid[:], E4M3)
            w_i_codes.append(codes[:])

        late_plane(2, False, third_turned, "", "w_d")

        def score(k, u, number):
            sums = flat(bank(number)[:, 0:2, :])
            users = half(u)
            return multiply(
                sums, w_d_codes[k][:], w_d_scales[:, quarter(k)], x_d_codes[:, users], x_d_scales[:, users], E4M3
            )

        multiply(flat(bank(7)[:]), x_d_codes[:, quarter(0)], x_d_scales[:, quarter(0)], x_d_codes[:], x_d_scales[:], E4M3)

        margin = placed("margin", [P, 2, N], F32, 0)
        q = [sbuf("q%d" % c, [P, P // PACK, PACK, PACK], F32) for c in range(2)]

        def scaled_negatives(c, u):
            if c + u:
                negative = sbuf("negative%d" % (2 * c + u), [P, HALF], F32)[:]
            else:
                negative = w_planes[1][:, 0, :].bitcast(F32)
            nc.scalar.activation(negative, score(2 + c, u, PACK * c + 2 * u), COPY, scale=ts_column[:, 2 + c : 3 + c])
            return negative

        def add_positives(c, u, negative):
            positive = score(c, u, PACK * c + 2 * u + 1)
            nc.vector.scalar_tensor_tensor(margin[:, c, half(u)], positive, ts_column[:, c : c + 1], negative, MULT, ADD)

        def weigh(c, u):
            turned = bank(PACK * c + 2 * u)
            for e in range(2):
                nc.tensor.transpose(turned[:, e, :], margin[:, c, quarter(2 * u + e)], ident[:])
            for e in range(2):
                s = 2 * u + e
                nc.scalar.activation(
                    q[c][:, :, s, :],
                    turned[:, e, :].rearrange("p (g i) -> p g i", i=PACK),
                    SIGMOID,
                    scale=row_scale[:, s : s + 1],
                )

        for u in range(2):
            add_positives(0, u, scaled_negatives(0, u))
        late = [scaled_negatives(1, u) for u in range(2)]
        for u in range(2):
            weigh(0, u)
        for u in range(2):
            add_positives(1, u, late[u])
        for u in range(2):
            weigh(1, u)

        h_r = sbuf("h_r", [P, N, PACK], BF16)
        h_r_codes = sbuf("h_r_codes", [P, N], U32)
        h_r_scales = sbuf("h_r_scales", [P, N], U8)

        def gradient(k, parts=1):
            columns = h_r[:, quarter(k), :].rearrange("p (g i) s -> p g s i", i=PACK)
            for part in range(parts):
                some = slice(part * P // PACK // parts, (part + 1) * P // PACK // parts)
                nc.vector.tensor_tensor(columns[:, some], q[k % 2][:, some], signed[:, groups(k)][:, some], MULT)

        def quantise_gradient(k):
            quantise(h_r_codes[:, quarter(k)], h_r_scales[:, quarter(k)], h_r[:, quarter(k), :], E5M2)

        def item_sums(t, slots, sums):
            rows = quarter(t % 2)
            codes, scales = x_r_codes[t // 2][:, rows], x_r_scales[t // 2][:, rows]
            return multiply(sums, codes, scales, h_r_codes[:, slots], h_r_scales[:, slots], E5M2)

        def scatter(a, window, listed, values):
            move_listed(a, window[:].indirect(entries(listed, a, 2)), values)

        h_rows = placed("h_planes", [P, PACK * ROW], BF16, 0)
        h_planes = h_rows[:].rearrange("p (s n) -> p s n", s=PACK)[:, :, 0:N]
        last_plane = h_rows[:, HALF : HALF + N].rearrange("p (c j) -> p c j", j=PACK)
        lay_turned(False, last_plane, turn_plane(w_planes[1][:, 1, :], 7))

        def part(k):
            nc.scalar.copy(
                h_planes[:, :, quarter(k)].rearrange("p s (g i) -> p g s i", i=8),
                h_r[:, quarter(k), :].rearrange("p (g i) s -> p g s i", i=8),
            )

        first_positives = sbuf("positives0", [P, 2, HALF], F32)
        positives = [first_positives[:, t, :] for t in range(2)]
        for k in range(2):
            gradient(k)
        quantise_gradient(0)
        early = bank(1)
        for t in range(2):
            item_sums(t, quarter(0), early[:, t, :])
        nc.scalar.copy(first_positives[:, :, quarter(0)], early[:, 0:2, :])
        quantise_gradient(1)
        for t in range(2):
            nc.scalar.copy(first_positives[:, t, quarter(1)], item_sums(t, quarter(1), bank(5 + 2 * t)[:, 0, :]))
        for k in range(2):
            part(k)

        gradient(2, parts=PACK)
        quantise_gradient(2)
        gradient(3, parts=2)
        quantise_gradient(3)
        last_codes = sbuf("w_i_codes3", [P, P], U32, tag="signed")
        quantise(last_codes[:], w_i_scales[:, quarter(PACK - 1)], last_plane, E4M3)
        w_i_codes.append(last_codes[:])
        negatives = sbuf("negatives", [P, PACK, HALF], F32)
        early_negatives = bank(0)
        late_negatives = [bank(2), bank(4)]
        for t in range(PACK):
            item_sums(t, quarter(2), early_negatives[:, t, :])
        for t in range(PACK):
            item_sums(t, quarter(3), late_negatives[t // 2][:, t % 2, :])
        nc.vector.tensor_copy(negatives[:, :, quarter(0)], early_negatives[:])
        for u in range(2):
            nc.vector.tensor_copy(negatives[:, 2 * u : 2 * u + 2, quarter(1)], late_negatives[u][:, 0:2, :])


        nc.gpsimd.tensor_scalar(
            h_planes[:, :, half(1)], h_r[:, half(1), :].rearrange("p i s -> p s i"), 1.0, 0.0, MULT, ADD
        )
        du_window.append(zeroed_window("du_window1", "h_r"))

        def put_items(t):
            scatter(0, dv_window[t], item_list, positives[t])
            scatter(1, dv_window[t], item_list, negatives[:, t, :])
            nc.sync.dma_start(planes(out_0)[:, t, :], dv_window[t][:])

        for t in range(2):
            put_items(t)

        h_i = [sbuf("h_i%d" % a, [P, HALF, PACK], BF16) for a in range(2)]
        h_i_codes = [sbuf("h_i_codes0", [P, HALF], U32)]
        h_i_scales = [sbuf("h_i_scales%d" % a, [P, HALF], U8) for a in range(2)]
        last = bank(6)
        for e in range(2):
            item_sums(2 + e, half(0), flat(last[:, 2 * e : 2 * e + 2, :]))
        h_words = h_rows[:].bitcast(F32).rearrange("p (s m u) -> p s u m", s=PACK, u=2)[:, :, :, 0:P]
        turned = [bank(1 + 2 * pair) for pair in range(2)]
        for s in range(PACK):
            for u in range(2):
                nc.tensor.transpose(turned[s // 2][:, 2 * (s % 2) + u, :], h_words[:, s, u, :], ident[:])

        def lay_users(a, pair, on_vector):
            move(
                on_vector,
                flat(h_i[a][:, quarter(pair), :]).bitcast(F32).rearrange("p (e c u) -> p e c u", e=2, u=2),
                turned[pair][:, :, a * P // 2 : (a + 1) * P // 2].rearrange("p (e u) c -> p e c u", e=2),
            )

        for a in range(2):
            lay_users(a, 0, a)
        positives.append(placed("positives2", [P, HALF], F32, 0)[:])
        nc.scalar.copy(positives[2], flat(last[:, 0:2, :]))
        lay_users(0, 1, False)
        positives.append(placed("positives3", [P, HALF], F32, 2 * KIB)[:])
        nc.vector.tensor_copy(positives[3], flat(last[:, 2:PACK, :]))
        quantise(h_i_codes[0][:], h_i_scales[0][:], h_i[0][:], E5M2)
        put_items(2)
        lay_users(1, 1, False)
        h_i_codes.append(placed("h_i_codes1", [P, HALF], U32, 0))
        quantise(h_i_codes[1][:], h_i_scales[1][:], h_i[1][:], E5M2)
        put_items(3)
        du_window.extend(
            [zeroed_window("du_window%d" % (2 + e), tag) for e, tag in enumerate(("h_i1", "h_i_scales1"))]
        )

        user_banks = ((5, 7), (0, 2))
        user_sums = {}
        for a in range(2):
            for pair in range(2):
                sums = bank(user_banks[a][pair])
                for e in range(2):
                    t = 2 * pair + e
                    user_sums[t, a] = multiply(
                        flat(sums[:, 2 * e : 2 * e + 2, :]),
                        w_i_codes[t],
                        w_i_scales[:, quarter(t)],
                        h_i_codes[a][:],
                        h_i_scales[a][:],
                        E5M2,
                    )

        du = {}

        def stage_users(t):
            tiles = (
                sbuf("du%d_0" % t, [P, HALF], F32, tag="du%d_0" % (t % 2)),
                placed("du%d_1" % t, [P, HALF], F32, 3 * KIB // 2 + t % 2 * KIB),
            )
            for a in range(2):
                some = user_sums[t, a].rearrange("p (s c) -> p c s", s=PACK)
                move(a, tiles[a][:].rearrange("p (c s) -> p c s", s=PACK), some)
                du[t, a] = tiles[a][:]

        def put_users(t):
            for a in range(2):
                scatter(a, du_window[t], user_list, du[t, a])
            nc.sync.dma_start(planes(out_1)[:, t, :], du_window[t][:])

        for t in range(2):
            stage_users(t)
        put_users(0)
        for t in range(1, PACK):
            if t + 1 < PACK:
                stage_users(t + 1)
            put_users(t)
